import numpy as np
import ml_dtypes


def mxq(x, axis, fmt="e4m3"):
    dtype, down = {"e4m3": (ml_dtypes.float8_e4m3fn, 7), "e5m2": (ml_dtypes.float8_e5m2, 14)}[fmt]
    v = np.moveaxis(np.asarray(x, np.float32).astype(ml_dtypes.bfloat16).astype(np.float64), axis, -1)
    blocks = v.reshape(v.shape[:-1] + (-1, 32))
    amax = np.abs(blocks).max(-1, keepdims=True)
    byte = np.maximum(np.where(amax > 0, np.frexp(amax)[1] - 1 + 127, 0) - down, 1)
    scale = np.exp2(byte - 127.0)
    codes = (blocks / scale).astype(np.float32).astype(dtype).astype(np.float64)
    return np.moveaxis((codes * scale).reshape(v.shape), -1, axis)


WIDE = False


def mx_kscale(k, group=512):
    if not WIDE:
        return np.ones(k)
    levels = np.array([10, -10, 5, -5, 0])
    if group != 512:
        return np.exp2(np.random.permutation(np.resize(levels, k // group))).repeat(group)
    if k % 512:
        return np.exp2(np.random.permutation(np.resize(levels, k // 32))).repeat(32)
    a = np.empty((k // 512, 16))
    for p in range(k // 512):
        a[p, :8] = np.random.permutation(np.resize(levels, 8))
        for g in range(8):
            far = levels[np.abs(levels - a[p, g]) >= 10]
            a[p, g + 8] = far[np.random.randint(len(far))]
    return np.exp2(a.ravel()).repeat(32)


def f64(x):
    return np.asarray(x).astype(np.float64)


def striped(idx):
    return np.tile(np.asarray(idx).reshape(-1, 16).T, (8, 1)).astype(np.uint16)


def unstriped(offs):
    return offs[:16].T.reshape(-1).astype(np.int64)


H, KV, D, NQ, N = 4, 1, 128, 512, 512
CAP = 2.0


def setup_inputs():
    n = np.random.standard_normal
    s = mx_kscale(D, 0)[:, None]
    u = mx_kscale(N)
    t = np.random.uniform(0.5, 2.0, N) * u
    v = n((KV, N, 128))
    v[:, :, 127] = 1.0
    return {
        "qT": (n((H, D, NQ)) * s * (0.70 / np.sqrt(D))).astype(np.float32),
        "kT": (n((KV, D, N)) / s).astype(np.float32),
        "t": t.reshape(N, 1).astype(np.float32),
        "v": (v / t[:, None]).astype(np.float32),
        "sink": (N * np.random.uniform(0.1, 1.0, (H, NQ, 1))).astype(np.float32),
    }


def reference(qT, kT, t, v, sink):
    a = np.repeat(mxq(f64(kT), 1, "e4m3"), H // KV, 0).transpose(0, 2, 1) @ mxq(f64(qT), 1, "e4m3")
    a = CAP * np.tanh(a / CAP)
    p = np.exp(a)
    w = p * f64(t)
    y = mxq(w, 1, "e4m3").transpose(0, 2, 1) @ np.repeat(mxq(f64(v), 1, "e4m3"), H // KV, 0)
    y = y / (y[:, :, 127:128] + f64(sink))
    return y

@@ -1,0 +1,305 @@
+from contextlib import ExitStack
+
+import concourse.mybir as mybir
+
+H, D, NQ, N = 4, 128, 512, 512
+CAP = 2.0
+FLOPS = 2 * 2 * H * NQ * N * D
+
+F32 = mybir.dt.float32
+BF16 = mybir.dt.bfloat16
+U32 = mybir.dt.uint32
+U8 = mybir.dt.uint8
+FP8X4 = mybir.dt.float8_e4m3fn_x4
+ACT = mybir.ActivationFunctionType
+ALU = mybir.AluOpType
+
+P = 128
+PACK = 4
+ROWS = D // PACK
+QT = 128
+UNITS = H * (NQ // QT)
+GROUPS = [(0, 4), (4, 8), (8, 12), (12, 14), (14, 15), (15, 16)]
+
+
+def tile_rows_sink_cap_gqa_kernel(tc, qT, kT, t, v, sink, out):
+    nc = tc.nc
+    with ExitStack() as ctx:
+        sb = ctx.enter_context(tc.tile_pool(name="sb", bufs=1))
+        ps = ctx.enter_context(tc.psum_pool(name="ps", bufs=1))
+        ctx.enter_context(tc.manual_schedule())
+
+        q_src = qT.rearrange("h (p j) q -> (h p) j q", j=PACK)
+        k_src = kT[0].rearrange("(p j) i -> p j i", j=PACK)
+        q_chunks = [(0, 128), (128, 256), (256, 512)]
+        q_raw = [sb.tile([P, PACK, b - a], F32, name="q_raw%d" % a) for a, b in q_chunks]
+        k_raw = [sb.tile([P, PACK, N // 2], F32, name="k_raw%d" % i) for i in range(2)]
+        v_raw = sb.tile([P, PACK, D], F32)
+        t_sb = sb.tile([P, PACK], F32)
+        sink_sb = sb.tile([P, UNITS], F32)
+        warm = sb.tile([P, 8], F32)
+        warm_out = sb.tile([P, 8], F32)
+
+        q_bf = sb.tile([P, NQ, PACK], BF16, align_bytes=64)
+        k_bf = sb.tile([P, PACK, P, PACK], BF16, align_bytes=64)
+        v_bf = sb.tile([P, D, PACK], BF16, align_bytes=64)
+        q_codes = sb.tile([P, NQ], U32, align_bytes=64)
+        q_scales = sb.tile([P, NQ], U8, align_bytes=64)
+        k_codes = sb.tile([P, N], U32, align_bytes=64)
+        k_scales = sb.tile([P, N], U8, align_bytes=64)
+        v_codes = sb.tile([P, D], U32, align_bytes=64)
+        v_scales = sb.tile([P, D], U8, align_bytes=64)
+        capped = sb.tile([P, UNITS, QT, PACK], F32)
+        probs = sb.tile([P, UNITS, QT, PACK], F32)
+        w_bf = sb.tile([P, UNITS, QT, PACK], BF16, align_bytes=64)
+        w_codes = sb.tile([P, UNITS * QT], U32, align_bytes=64)
+        w_scales = sb.tile([P, UNITS * QT], U8, align_bytes=64)
+        den = sb.tile([P, UNITS, 8], F32)
+        rec = sb.tile([P, UNITS, 8], F32)
+        res = sb.tile([P, UNITS, D], F32)
+        score_banks = [ps.tile([P, PACK, QT], F32, name="score%d" % g) for g in range(H)]
+        y_banks = [ps.tile([P, H, D], F32, name="y%d" % i) for i in range(4)]
+
+        def load_k(engine, g, half):
+            cols = slice(half * N // 2, (half + 1) * N // 2)
+            engine.dma_start(out=k_raw[half][ROWS * g : ROWS * (g + 1)], in_=k_src[:, :, cols])
+
+        def load_q(i):
+            a, b = q_chunks[i]
+            nc.sync.dma_start(out=q_raw[i][:], in_=q_src[:, :, a:b])
+
+        def round_q(i):
+            a, b = q_chunks[i]
+            nc.vector.tensor_copy(out=q_bf[:, a:b, :], in_=q_raw[i][:].rearrange("p j q -> p q j"))
+
+        def quantize_q(i):
+            a, b = q_chunks[i]
+            nc.vector.quantize_mx(
+                out=q_codes[:, a:b].bitcast(FP8X4),
+                scales=q_scales[:, a:b],
+                in_=q_bf[:, a:b, :].rearrange("p q j -> p (q j)"),
+            )
+
+        def k_views(half, r0, r1):
+            src = k_raw[half][:].rearrange("p j (s r) -> p r s j", r=PACK)[:, r0:r1]
+            return k_bf[:, r0:r1, half * P // 2 : (half + 1) * P // 2, :], src
+
+        def quantize_k(half, r):
+            s0, s1 = half * P // 2, (half + 1) * P // 2
+            cols = slice(r * P + s0, r * P + s1)
+            nc.vector.quantize_mx(
+                out=k_codes[:, cols].bitcast(FP8X4),
+                scales=k_scales[:, cols],
+                in_=k_bf[:, r, s0:s1, :].rearrange("p s j -> p (s j)"),
+            )
+
+        def score_pass(u, r):
+            c, g = divmod(u, H)
+            rows = slice(ROWS * g, ROWS * (g + 1))
+            kc = slice(r * P, (r + 1) * P)
+            qc = slice(c * QT, (c + 1) * QT)
+            nc.tensor.matmul_mx(
+                out=score_banks[g][:, r, :],
+                lhsT=k_codes[rows, kc].bitcast(FP8X4),
+                lhsT_scale=k_scales[rows, kc],
+                rhs=q_codes[rows, qc].bitcast(FP8X4),
+                rhs_scale=q_scales[rows, qc],
+                start=True,
+                stop=True,
+            )
+
+        def scores(u):
+            if u < UNITS:
+                for r in range(PACK):
+                    score_pass(u, r)
+
+        def cap(u, q0=0, q1=QT):
+            nc.scalar.activation(
+                out=capped[:, u, q0:q1, :],
+                in_=score_banks[u % H][:, :, q0:q1].rearrange("p r q -> p q r"),
+                func=ACT.Tanh,
+                scale=1.0 / CAP,
+            )
+
+        def weigh(u, q0=0, q1=QT):
+            nc.scalar.activation(out=probs[:, u, q0:q1, :], in_=capped[:, u, q0:q1, :], func=ACT.Exp, scale=CAP)
+
+        def scale_w(u, q0=0, q1=QT):
+            nc.vector.tensor_tensor(
+                out=w_bf[:, u, q0:q1, :],
+                in0=probs[:, u, q0:q1, :],
+                in1=t_sb[:].unsqueeze(1).to_broadcast([P, q1 - q0, PACK]),
+                op=ALU.mult,
+            )
+
+        def y_place(u):
+            i = [u0 <= u < u1 for u0, u1 in GROUPS].index(True)
+            return y_banks[i % 4], u - GROUPS[i][0]
+
+        def quantize_w(u, q0=0, q1=QT):
+            cols = slice(u * QT + q0, u * QT + q1)
+            nc.vector.quantize_mx(
+                out=w_codes[:, cols].bitcast(FP8X4),
+                scales=w_scales[:, cols],
+                in_=w_bf[:, u, q0:q1, :].rearrange("p q r -> p (q r)"),
+            )
+
+        def values(u):
+            bank, place = y_place(u)
+            cols = slice(u * QT, (u + 1) * QT)
+            nc.tensor.matmul_mx(
+                out=bank[:, place, :],
+                lhsT=w_codes[:, cols].bitcast(FP8X4),
+                lhsT_scale=w_scales[:, cols],
+                rhs=v_codes[:].bitcast(FP8X4),
+                rhs_scale=v_scales[:],
+                start=True,
+                stop=True,
+            )
+
+        def add_sink(u0, u1):
+            c, g = divmod(u0, H)
+            bank, place = y_place(u0)
+            n = u1 - u0
+            nc.vector.tensor_tensor(
+                out=den[:, u0, 0:n],
+                in0=bank[:, place : place + n, D - 1],
+                in1=sink_sb[:].rearrange("p (h c) -> p c h", h=H)[:, c, g : g + n],
+                op=ALU.add,
+            )
+
+        def invert(u0, u1):
+            nc.vector.reciprocal(out=rec[:, u0, 0 : u1 - u0], in_=den[:, u0, 0 : u1 - u0])
+
+        def store(u0, u1):
+            c, g = divmod(u0, H)
+            nc.sync.dma_start(
+                out=out[g : g + u1 - u0, c * QT : (c + 1) * QT, :].rearrange("h p e -> p h e"),
+                in_=res[:, u0:u1, :],
+            )
+
+        def divide_group(u0, u1):
+            bank, place = y_place(u0)
+            n = u1 - u0
+            nc.vector.tensor_tensor(
+                out=res[:, u0:u1, :],
+                in0=bank[:, place : place + n, :],
+                in1=rec[:, u0, 0:n].unsqueeze(2).to_broadcast([P, n, D]),
+                op=ALU.mult,
+            )
+            store(u0, u1)
+
+        def divide_on_vector(u):
+            bank, place = y_place(u)
+            nc.vector.tensor_scalar(
+                out=res[:, u, :], in0=bank[:, place, :], scalar1=rec[:, u, 0:1], scalar2=None, op0=ALU.mult
+            )
+            store(u, u + 1)
+
+        def divide_on_scalar(u0, u1):
+            for u in range(u0, u1):
+                bank, place = y_place(u)
+                nc.scalar.activation(
+                    out=res[:, u, :], in_=bank[:, place, :], func=ACT.Copy, scale=rec[:, u0, u - u0 : u - u0 + 1]
+                )
+            store(u0, u1)
+
+        load_q(0)
+        load_k(nc.sync, 0, 0)
+        load_k(nc.scalar, 2, 0)
+        load_k(nc.sync, 1, 0)
+        load_k(nc.scalar, 3, 0)
+        load_k(nc.sync, 0, 1)
+        load_k(nc.scalar, 2, 1)
+        load_k(nc.scalar, 3, 1)
+        load_k(nc.sync, 1, 1)
+        load_q(1)
+        nc.sync.dma_start(out=t_sb[:], in_=t.rearrange("(p j) o -> p (j o)", j=PACK))
+        nc.sync.dma_start(out=v_raw[:], in_=v[0].rearrange("(p j) e -> p j e", j=PACK))
+        load_q(2)
+        with nc.allow_non_contiguous_dma(reason="one sink value a partition"):
+            nc.sync.dma_start(out=sink_sb[:], in_=sink.rearrange("h (c p) o -> p (h c o)", p=QT))
+
+        nc.vector.memset(warm[:], 0.0)
+        nc.scalar.activation(out=warm_out[:], in_=warm[:], func=ACT.Exp)
+
+        def round_k(half, r0, r1, copy):
+            dst, src = k_views(half, r0, r1)
+            copy(out=dst, in_=src)
+
+        round_q(0)
+        round_k(0, 0, 3, nc.vector.tensor_copy)
+        round_k(0, 3, 4, nc.scalar.copy)
+        quantize_q(0)
+        for r in range(PACK):
+            quantize_k(0, r)
+        round_k(1, 0, 2, nc.vector.tensor_copy)
+        round_k(1, 3, 4, nc.scalar.copy)
+        round_k(1, 2, 3, nc.vector.tensor_copy)
+        for r in (0, 1, 3, 2):
+            quantize_k(1, r)
+        for g in range(H):
+            for r in (0, 1, 3, 2):
+                score_pass(g, r)
+
+        round_q(1)
+        nc.vector.tensor_copy(out=v_bf[:], in_=v_raw[:].rearrange("p j e -> p e j"))
+        quantize_q(1)
+        nc.vector.quantize_mx(
+            out=v_codes[:].bitcast(FP8X4), scales=v_scales[:], in_=v_bf[:].rearrange("p e j -> p (e j)")
+        )
+
+        last = UNITS - 1
+        half = QT // 2
+        den_at = {5: GROUPS[0], 9: GROUPS[1], 13: GROUPS[2]}
+        cap(0)
+        scores(H)
+        for u in range(last - 1):
+            cap(u + 1, 0, QT if u + 1 < last - 1 else half)
+            scores(u + 1 + H)
+            if u >= 2:
+                values(u - 2)
+            weigh(u)
+            if u - 1 in den_at:
+                invert(*den_at[u - 1])
+            scale_w(u)
+            if u == 0:
+                round_q(2)
+            else:
+                quantize_w(u - 1)
+            if u == 1:
+                quantize_q(2)
+            if u in den_at:
+                add_sink(*den_at[u])
+            if u - 1 in den_at:
+                divide_group(*den_at[u - 1])
+        values(last - 3)
+        cap(last - 1, half, QT)
+        weigh(last - 1, 0, half)
+        cap(last, 0, half)
+        weigh(last - 1, half, QT)
+        cap(last, half, QT)
+        weigh(last, 0, half)
+        weigh(last, half, QT)
+        scale_w(last - 1, 0, half)
+        quantize_w(last - 2)
+        values(last - 2)
+        invert(*GROUPS[2])
+        divide_on_scalar(*GROUPS[2])
+        scale_w(last - 1, half, QT)
+        scale_w(last, 0, half)
+        quantize_w(last - 1)
+        values(last - 1)
+        scale_w(last, half, QT)
+        quantize_w(last, 0, half)
+        add_sink(*GROUPS[3])
+        quantize_w(last, half, QT)
+        values(last)
+        invert(*GROUPS[3])
+        divide_on_scalar(*GROUPS[3])
+        add_sink(*GROUPS[4])
+        invert(*GROUPS[4])
+        add_sink(*GROUPS[5])
+        divide_on_scalar(*GROUPS[4])
+        invert(*GROUPS[5])
+        divide_on_vector(last)

@@ -36,7 +36,8 @@ def tile_rows_sink_cap_gqa_kernel(tc, qT, kT, t, v, sink, out):
         k_raw = [sb.tile([P, PACK, N // 2], F32, name="k_raw%d" % i) for i in range(2)]
         v_raw = sb.tile([P, PACK, D], F32)
         t_sb = sb.tile([P, PACK], F32)
-        sink_sb = sb.tile([P, UNITS], F32)
+        sink_rows = sb.tile([P, 32], F32, align_bytes=64)
+        sink_sb = sb.tile([P, 32], F32, align_bytes=64)
         warm = sb.tile([P, 8], F32)
         warm_out = sb.tile([P, 8], F32)
 
@@ -164,7 +165,7 @@ def tile_rows_sink_cap_gqa_kernel(tc, qT, kT, t, v, sink, out):
             nc.vector.tensor_tensor(
                 out=den[:, u0, 0:n],
                 in0=bank[:, place : place + n, D - 1],
-                in1=sink_sb[:].rearrange("p (h c) -> p c h", h=H)[:, c, g : g + n],
+                in1=sink_sb[:, 0:UNITS].rearrange("p (h c) -> p c h", h=H)[:, c, g : g + n],
                 op=ALU.add,
             )
 
@@ -217,10 +218,12 @@ def tile_rows_sink_cap_gqa_kernel(tc, qT, kT, t, v, sink, out):
         nc.sync.dma_start(out=t_sb[:], in_=t.rearrange("(p j) o -> p (j o)", j=PACK))
         nc.sync.dma_start(out=v_raw[:], in_=v[0].rearrange("(p j) e -> p j e", j=PACK))
         load_q(2)
-        with nc.allow_non_contiguous_dma(reason="one sink value a partition"):
-            nc.sync.dma_start(out=sink_sb[:], in_=sink.rearrange("h (c p) o -> p (h c o)", p=QT))
-
         nc.vector.memset(warm[:], 0.0)
+        nc.vector.memset(sink_rows[:], 0.0)
+        sink_src = sink.rearrange("h (c p) o -> (h c) (p o)", p=QT)
+        for b in range(4):
+            nc.sync.dma_start(out=sink_rows[32 * b : 32 * b + UNITS, :], in_=sink_src[:, 32 * b : 32 * (b + 1)])
+
         nc.scalar.activation(out=warm_out[:], in_=warm[:], func=ACT.Exp)
 
         def round_k(half, r0, r1, copy):
@@ -269,6 +272,8 @@ def tile_rows_sink_cap_gqa_kernel(tc, qT, kT, t, v, sink, out):
                 quantize_w(u - 1)
             if u == 1:
                 quantize_q(2)
+            if u == 2:
+                nc.vector.transpose(out=sink_sb[:], in_=sink_rows[:])
             if u in den_at:
                 add_sink(*den_at[u])
             if u - 1 in den_at:

@@ -109,10 +109,11 @@ def tile_rows_sink_cap_gqa_kernel(tc, qT, kT, t, v, sink, out):
                 stop=True,
             )
 
-        def scores(u):
+        def score_pair(u, order=range(PACK)):
             if u < UNITS:
-                for r in range(PACK):
+                for r in order:
                     score_pass(u, r)
+                    score_pass(u + 1, r)
 
         def cap(u, q0=0, q1=QT):
             nc.scalar.activation(
@@ -236,14 +237,15 @@ def tile_rows_sink_cap_gqa_kernel(tc, qT, kT, t, v, sink, out):
         quantize_q(0)
         for r in range(PACK):
             quantize_k(0, r)
-        round_k(1, 0, 2, nc.vector.tensor_copy)
+        round_k(1, 0, 1, nc.vector.tensor_copy)
         round_k(1, 3, 4, nc.scalar.copy)
+        round_k(1, 1, 2, nc.vector.tensor_copy)
+        quantize_k(1, 0)
         round_k(1, 2, 3, nc.vector.tensor_copy)
-        for r in (0, 1, 3, 2):
+        for r in (1, 3, 2):
             quantize_k(1, r)
-        for g in range(H):
-            for r in (0, 1, 3, 2):
-                score_pass(g, r)
+        score_pair(0, (0, 1, 3, 2))
+        score_pair(2)
 
         round_q(1)
         nc.vector.tensor_copy(out=v_bf[:], in_=v_raw[:].rearrange("p j e -> p e j"))
@@ -256,11 +258,12 @@ def tile_rows_sink_cap_gqa_kernel(tc, qT, kT, t, v, sink, out):
         half = QT // 2
         den_at = {5: GROUPS[0], 9: GROUPS[1], 13: GROUPS[2]}
         cap(0)
-        scores(H)
         for u in range(last - 1):
             cap(u + 1, 0, QT if u + 1 < last - 1 else half)
-            scores(u + 1 + H)
-            if u >= 2:
+            if u % 2 == 0:
+                score_pair(u + H)
+            elif u >= 3:
+                values(u - 3)
                 values(u - 2)
             weigh(u)
             if u - 1 in den_at:

@@ -8,7 +8,7 @@ FLOPS = 2 * 2 * H * NQ * N * D
 
 F32 = mybir.dt.float32
 BF16 = mybir.dt.bfloat16
-U32 = mybir.dt.uint32
+I32 = mybir.dt.int32
 U8 = mybir.dt.uint8
 FP8X4 = mybir.dt.float8_e4m3fn_x4
 ACT = mybir.ActivationFunctionType
@@ -18,8 +18,18 @@ P = 128
 PACK = 4
 ROWS = D // PACK
 QT = 128
-UNITS = H * (NQ // QT)
-GROUPS = [(0, 4), (4, 8), (8, 12), (12, 14), (14, 15), (15, 16)]
+CHUNKS = NQ // QT
+GROUPS = [
+    [(0, 0), (2, 0)],
+    [(0, 1), (2, 1)],
+    [(1, 0), (3, 0)],
+    [(0, 2), (2, 2)],
+    [(1, 1), (3, 1)],
+    [(0, 3), (2, 3)],
+    [(1, 2), (3, 2)],
+    [(1, 3)],
+    [(3, 3)],
+]
 
 
 def tile_rows_sink_cap_gqa_kernel(tc, qT, kT, t, v, sink, out):
@@ -30,284 +40,276 @@ def tile_rows_sink_cap_gqa_kernel(tc, qT, kT, t, v, sink, out):
         ctx.enter_context(tc.manual_schedule())
 
         q_src = qT.rearrange("h (p j) q -> (h p) j q", j=PACK)
-        k_src = kT[0].rearrange("(p j) i -> p j i", j=PACK)
-        q_chunks = [(0, 128), (128, 256), (256, 512)]
-        q_raw = [sb.tile([P, PACK, b - a], F32, name="q_raw%d" % a) for a, b in q_chunks]
-        k_raw = [sb.tile([P, PACK, N // 2], F32, name="k_raw%d" % i) for i in range(2)]
+        k_src = kT[0].rearrange("(p j) i -> p (j i)", j=PACK)
+        q_loads = [(0, 128), (128, 256), (256, 512)]
+        q_raw = [sb.tile([P, PACK, b - a], F32, name="q_raw%d" % a) for a, b in q_loads]
+        k_raw = sb.tile([P, PACK * N], F32)
         v_raw = sb.tile([P, PACK, D], F32)
         t_sb = sb.tile([P, PACK], F32)
-        sink_rows = sb.tile([P, 32], F32, align_bytes=64)
-        sink_sb = sb.tile([P, 32], F32, align_bytes=64)
-        warm = sb.tile([P, 8], F32)
-        warm_out = sb.tile([P, 8], F32)
+        t_abs = sb.tile([P, PACK], F32)
+        t_ln = sb.tile([P, PACK], F32)
+        t_half_sign = sb.tile([P, PACK], F32)
+        sink_sb = sb.tile([P, H, CHUNKS], F32)
 
-        q_bf = sb.tile([P, NQ, PACK], BF16, align_bytes=64)
-        k_bf = sb.tile([P, PACK, P, PACK], BF16, align_bytes=64)
+        q_bf = [sb.tile([P, QT, PACK], BF16, align_bytes=64, name="q_bf%d" % c) for c in range(CHUNKS)]
+        q_codes = [sb.tile([P, QT], I32, align_bytes=64, name="q_codes%d" % c) for c in range(CHUNKS)]
+        q_scales = [sb.tile([P, QT], U8, align_bytes=64, name="q_scales%d" % c) for c in range(CHUNKS)]
+        k_bf = [sb.tile([P, 2, P, PACK], BF16, align_bytes=64, name="k_bf%d" % i) for i in range(2)]
+        k_mx = [sb.tile([P, N + N // PACK], I32, align_bytes=64, name="k_mx%d" % i) for i in range(2)]
         v_bf = sb.tile([P, D, PACK], BF16, align_bytes=64)
-        q_codes = sb.tile([P, NQ], U32, align_bytes=64)
-        q_scales = sb.tile([P, NQ], U8, align_bytes=64)
-        k_codes = sb.tile([P, N], U32, align_bytes=64)
-        k_scales = sb.tile([P, N], U8, align_bytes=64)
-        v_codes = sb.tile([P, D], U32, align_bytes=64)
+        v_codes = sb.tile([P, D], I32, align_bytes=64)
         v_scales = sb.tile([P, D], U8, align_bytes=64)
-        capped = sb.tile([P, UNITS, QT, PACK], F32)
-        probs = sb.tile([P, UNITS, QT, PACK], F32)
-        w_bf = sb.tile([P, UNITS, QT, PACK], BF16, align_bytes=64)
-        w_codes = sb.tile([P, UNITS * QT], U32, align_bytes=64)
-        w_scales = sb.tile([P, UNITS * QT], U8, align_bytes=64)
-        den = sb.tile([P, UNITS, 8], F32)
-        rec = sb.tile([P, UNITS, 8], F32)
-        res = sb.tile([P, UNITS, D], F32)
+
+        def per_group(name, shape, dtype):
+            return [
+                sb.tile([P, len(g)] + shape, dtype, align_bytes=64, name="%s%d" % (name, i))
+                for i, g in enumerate(GROUPS)
+            ]
+
+        capped = per_group("capped", [PACK, QT], F32)
+        w_rows = per_group("w_rows", [PACK, QT], BF16)
+        w_bf = per_group("w_bf", [QT, PACK], BF16)
+        w_codes = per_group("w_codes", [QT], I32)
+        w_scales = per_group("w_scales", [QT], U8)
+        den = per_group("den", [], F32)
+        rec = per_group("rec", [], F32)
+        res = per_group("res", [D], F32)
         score_banks = [ps.tile([P, PACK, QT], F32, name="score%d" % g) for g in range(H)]
-        y_banks = [ps.tile([P, H, D], F32, name="y%d" % i) for i in range(4)]
+        y_banks = [ps.tile([P, PACK, D], F32, name="y%d" % i) for i in range(4)]
 
-        def load_k(engine, g, half):
-            cols = slice(half * N // 2, (half + 1) * N // 2)
-            engine.dma_start(out=k_raw[half][ROWS * g : ROWS * (g + 1)], in_=k_src[:, :, cols])
+        live = slice(0, 3 * ROWS)
 
-        def load_q(i):
-            a, b = q_chunks[i]
-            nc.sync.dma_start(out=q_raw[i][:], in_=q_src[:, :, a:b])
+        def k_codes(i):
+            return k_mx[i][:, 0:N]
 
-        def round_q(i):
-            a, b = q_chunks[i]
-            nc.vector.tensor_copy(out=q_bf[:, a:b, :], in_=q_raw[i][:].rearrange("p j q -> p q j"))
+        def k_scales(i):
+            return k_mx[i][:, N:].bitcast(U8)
 
-        def quantize_q(i):
-            a, b = q_chunks[i]
+        def round_q(c):
+            i = min(c, 2)
+            a = c * QT - q_loads[i][0]
+            nc.vector.tensor_copy(out=q_bf[c][:], in_=q_raw[i][:, :, a : a + QT].rearrange("p j q -> p q j"))
+
+        def quantize_q(c):
             nc.vector.quantize_mx(
-                out=q_codes[:, a:b].bitcast(FP8X4),
-                scales=q_scales[:, a:b],
-                in_=q_bf[:, a:b, :].rearrange("p q j -> p (q j)"),
+                out=q_codes[c][:].bitcast(FP8X4),
+                scales=q_scales[c][:],
+                in_=q_bf[c][:].rearrange("p q j -> p (q j)"),
             )
 
-        def k_views(half, r0, r1):
-            src = k_raw[half][:].rearrange("p j (s r) -> p r s j", r=PACK)[:, r0:r1]
-            return k_bf[:, r0:r1, half * P // 2 : (half + 1) * P // 2, :], src
+        def round_k(i):
+            src = k_raw[live, :].rearrange("p (j s r) -> p s j r", j=PACK, r=PACK)[:, :, :, 2 * i : 2 * i + 2]
+            nc.vector.tensor_copy(out=k_bf[i][live].rearrange("p r s j -> p s j r"), in_=src)
 
-        def quantize_k(half, r):
-            s0, s1 = half * P // 2, (half + 1) * P // 2
-            cols = slice(r * P + s0, r * P + s1)
+        def quantize_k(r):
+            cols = slice(r * P, (r + 1) * P)
             nc.vector.quantize_mx(
-                out=k_codes[:, cols].bitcast(FP8X4),
-                scales=k_scales[:, cols],
-                in_=k_bf[:, r, s0:s1, :].rearrange("p s j -> p (s j)"),
+                out=k_codes(0)[live, cols].bitcast(FP8X4),
+                scales=k_scales(0)[live, cols],
+                in_=k_bf[r // 2][live, r % 2].rearrange("p s j -> p (s j)"),
             )
 
-        def score_pass(u, r):
-            c, g = divmod(u, H)
-            rows = slice(ROWS * g, ROWS * (g + 1))
+        def score_pass(h, c, r):
+            rows = slice(ROWS * h, ROWS * (h + 1))
             kc = slice(r * P, (r + 1) * P)
-            qc = slice(c * QT, (c + 1) * QT)
             nc.tensor.matmul_mx(
-                out=score_banks[g][:, r, :],
-                lhsT=k_codes[rows, kc].bitcast(FP8X4),
-                lhsT_scale=k_scales[rows, kc],
-                rhs=q_codes[rows, qc].bitcast(FP8X4),
-                rhs_scale=q_scales[rows, qc],
+                out=score_banks[h][:, r, :],
+                lhsT=k_codes(h % 2)[rows, kc].bitcast(FP8X4),
+                lhsT_scale=k_scales(h % 2)[rows, kc],
+                rhs=q_codes[c][rows, :].bitcast(FP8X4),
+                rhs_scale=q_scales[c][rows, :],
                 start=True,
                 stop=True,
             )
 
-        def score_pair(u, order=range(PACK)):
-            if u < UNITS:
-                for r in order:
-                    score_pass(u, r)
-                    score_pass(u + 1, r)
+        def scores(i, n):
+            h, c = GROUPS[i][n]
+            for r in range(PACK):
+                score_pass(h, c, r)
 
-        def cap(u, q0=0, q1=QT):
+        def cap(i, n, r0=0, r1=PACK):
+            h = GROUPS[i][n][0]
             nc.scalar.activation(
-                out=capped[:, u, q0:q1, :],
-                in_=score_banks[u % H][:, :, q0:q1].rearrange("p r q -> p q r"),
-                func=ACT.Tanh,
-                scale=1.0 / CAP,
+                out=capped[i][:, n, r0:r1, :], in_=score_banks[h][:, r0:r1, :], func=ACT.Tanh, scale=1.0 / CAP
             )
 
-        def weigh(u, q0=0, q1=QT):
-            nc.scalar.activation(out=probs[:, u, q0:q1, :], in_=capped[:, u, q0:q1, :], func=ACT.Exp, scale=CAP)
-
-        def scale_w(u, q0=0, q1=QT):
-            nc.vector.tensor_tensor(
-                out=w_bf[:, u, q0:q1, :],
-                in0=probs[:, u, q0:q1, :],
-                in1=t_sb[:].unsqueeze(1).to_broadcast([P, q1 - q0, PACK]),
-                op=ALU.mult,
+        def weigh(i, r, n0=0, n1=2):
+            nc.scalar.activation(
+                out=w_rows[i][:, n0:n1, r, :],
+                in_=capped[i][:, n0:n1, r, :],
+                func=ACT.Exp,
+                scale=CAP,
+                bias=t_ln[:, r : r + 1],
             )
 
-        def y_place(u):
-            i = [u0 <= u < u1 for u0, u1 in GROUPS].index(True)
-            return y_banks[i % 4], u - GROUPS[i][0]
+        def interleave(i, n):
+            nc.vector.tensor_copy(out=w_bf[i][:, n], in_=w_rows[i][:, n].rearrange("p r q -> p q r"))
 
-        def quantize_w(u, q0=0, q1=QT):
-            cols = slice(u * QT + q0, u * QT + q1)
+        def quantize_w(i, n):
             nc.vector.quantize_mx(
-                out=w_codes[:, cols].bitcast(FP8X4),
-                scales=w_scales[:, cols],
-                in_=w_bf[:, u, q0:q1, :].rearrange("p q r -> p (q r)"),
+                out=w_codes[i][:, n, :].bitcast(FP8X4),
+                scales=w_scales[i][:, n, :],
+                in_=w_bf[i][:, n].rearrange("p q r -> p (q r)"),
             )
 
-        def values(u):
-            bank, place = y_place(u)
-            cols = slice(u * QT, (u + 1) * QT)
+        def values(i, n):
             nc.tensor.matmul_mx(
-                out=bank[:, place, :],
-                lhsT=w_codes[:, cols].bitcast(FP8X4),
-                lhsT_scale=w_scales[:, cols],
+                out=y_banks[i % 4][:, n, :],
+                lhsT=w_codes[i][:, n, :].bitcast(FP8X4),
+                lhsT_scale=w_scales[i][:, n, :],
                 rhs=v_codes[:].bitcast(FP8X4),
                 rhs_scale=v_scales[:],
                 start=True,
                 stop=True,
             )
 
-        def add_sink(u0, u1):
-            c, g = divmod(u0, H)
-            bank, place = y_place(u0)
-            n = u1 - u0
+        def heads(i):
+            h, c = GROUPS[i][0]
+            return slice(h, h + 2 * len(GROUPS[i]) - 1, 2), c
+
+        def add_sink(i):
+            hs, c = heads(i)
             nc.vector.tensor_tensor(
-                out=den[:, u0, 0:n],
-                in0=bank[:, place : place + n, D - 1],
-                in1=sink_sb[:, 0:UNITS].rearrange("p (h c) -> p c h", h=H)[:, c, g : g + n],
-                op=ALU.add,
+                out=den[i][:], in0=y_banks[i % 4][:, 0 : len(GROUPS[i]), D - 1], in1=sink_sb[:, hs, c], op=ALU.add
             )
 
-        def invert(u0, u1):
-            nc.vector.reciprocal(out=rec[:, u0, 0 : u1 - u0], in_=den[:, u0, 0 : u1 - u0])
+        def invert(i):
+            nc.vector.reciprocal(out=rec[i][:], in_=den[i][:])
 
-        def store(u0, u1):
-            c, g = divmod(u0, H)
+        def store(i):
+            hs, c = heads(i)
             nc.sync.dma_start(
-                out=out[g : g + u1 - u0, c * QT : (c + 1) * QT, :].rearrange("h p e -> p h e"),
-                in_=res[:, u0:u1, :],
+                out=out[hs, c * QT : (c + 1) * QT, :].rearrange("h p e -> p h e"), in_=res[i][:]
             )
 
-        def divide_group(u0, u1):
-            bank, place = y_place(u0)
-            n = u1 - u0
+        def divide(i):
+            n = len(GROUPS[i])
             nc.vector.tensor_tensor(
-                out=res[:, u0:u1, :],
-                in0=bank[:, place : place + n, :],
-                in1=rec[:, u0, 0:n].unsqueeze(2).to_broadcast([P, n, D]),
+                out=res[i][:],
+                in0=y_banks[i % 4][:, 0:n, :],
+                in1=rec[i][:].unsqueeze(2).to_broadcast([P, n, D]),
                 op=ALU.mult,
             )
-            store(u0, u1)
+            store(i)
 
-        def divide_on_vector(u):
-            bank, place = y_place(u)
-            nc.vector.tensor_scalar(
-                out=res[:, u, :], in0=bank[:, place, :], scalar1=rec[:, u, 0:1], scalar2=None, op0=ALU.mult
-            )
-            store(u, u + 1)
-
-        def divide_on_scalar(u0, u1):
-            for u in range(u0, u1):
-                bank, place = y_place(u)
+        def divide_on_scalar(i):
+            for n in range(len(GROUPS[i])):
                 nc.scalar.activation(
-                    out=res[:, u, :], in_=bank[:, place, :], func=ACT.Copy, scale=rec[:, u0, u - u0 : u - u0 + 1]
+                    out=res[i][:, n, :], in_=y_banks[i % 4][:, n, :], func=ACT.Copy, scale=rec[i][:, n : n + 1]
                 )
-            store(u0, u1)
+            store(i)
 
-        load_q(0)
-        load_k(nc.sync, 0, 0)
-        load_k(nc.scalar, 2, 0)
-        load_k(nc.sync, 1, 0)
-        load_k(nc.scalar, 3, 0)
-        load_k(nc.sync, 0, 1)
-        load_k(nc.scalar, 2, 1)
-        load_k(nc.scalar, 3, 1)
-        load_k(nc.sync, 1, 1)
-        load_q(1)
-        nc.sync.dma_start(out=t_sb[:], in_=t.rearrange("(p j) o -> p (j o)", j=PACK))
+        nc.scalar.dma_start(out=t_sb[:], in_=t.rearrange("(p j) o -> p (j o)", j=PACK))
+        nc.sync.dma_start(out=q_raw[0][:], in_=q_src[:, :, 0:128])
+        nc.scalar.dma_start(out=k_raw[2 * ROWS : 3 * ROWS, :], in_=k_src)
+        nc.sync.dma_start(out=k_raw[0:ROWS, :], in_=k_src)
+        nc.sync.dma_start(out=q_raw[1][:], in_=q_src[:, :, 128:256])
         nc.sync.dma_start(out=v_raw[:], in_=v[0].rearrange("(p j) e -> p j e", j=PACK))
-        load_q(2)
-        nc.vector.memset(warm[:], 0.0)
-        nc.vector.memset(sink_rows[:], 0.0)
-        sink_src = sink.rearrange("h (c p) o -> (h c) (p o)", p=QT)
-        for b in range(4):
-            nc.sync.dma_start(out=sink_rows[32 * b : 32 * b + UNITS, :], in_=sink_src[:, 32 * b : 32 * (b + 1)])
+        nc.sync.dma_start(out=q_raw[2][:], in_=q_src[:, :, 256:512])
+        with nc.allow_non_contiguous_dma(reason="one sink a query row"):
+            nc.sync.dma_start(out=sink_sb[:], in_=sink.rearrange("h (c p) o -> p h (c o)", p=QT))
 
-        nc.scalar.activation(out=warm_out[:], in_=warm[:], func=ACT.Exp)
-
-        def round_k(half, r0, r1, copy):
-            dst, src = k_views(half, r0, r1)
-            copy(out=dst, in_=src)
+        nc.vector.memset(k_mx[0][:, N:], 0)
+        nc.vector.memset(k_raw[ROWS : 2 * ROWS, :], 0.0)
+        nc.vector.scalar_tensor_tensor(
+            out=t_abs[:], in0=t_sb[:], scalar=-1.0, in1=t_sb[:], op0=ALU.mult, op1=ALU.max
+        )
+        nc.vector.tensor_scalar(
+            out=t_half_sign[:], in0=t_sb[:], scalar1=0.0, scalar2=0.5, op0=ALU.is_ge, op1=ALU.subtract
+        )
+        nc.scalar.activation(out=t_ln[:], in_=t_abs[:], func=ACT.Ln)
 
         round_q(0)
-        round_k(0, 0, 3, nc.vector.tensor_copy)
-        round_k(0, 3, 4, nc.scalar.copy)
         quantize_q(0)
-        for r in range(PACK):
-            quantize_k(0, r)
-        round_k(1, 0, 1, nc.vector.tensor_copy)
-        round_k(1, 3, 4, nc.scalar.copy)
-        round_k(1, 1, 2, nc.vector.tensor_copy)
-        quantize_k(1, 0)
-        round_k(1, 2, 3, nc.vector.tensor_copy)
-        for r in (1, 3, 2):
-            quantize_k(1, r)
-        score_pair(0, (0, 1, 3, 2))
-        score_pair(2)
-
+        round_k(0)
+        quantize_k(0)
+        quantize_k(1)
+        round_k(1)
         round_q(1)
-        nc.vector.tensor_copy(out=v_bf[:], in_=v_raw[:].rearrange("p j e -> p e j"))
+        quantize_k(2)
+        quantize_k(3)
         quantize_q(1)
+        for i in range(2):
+            nc.sync.dma_start(
+                out=k_mx[1][(2 * i + 1) * ROWS : (2 * i + 2) * ROWS, :], in_=k_mx[0][2 * i * ROWS : (2 * i + 1) * ROWS, :]
+            )
+        nc.vector.scalar_tensor_tensor(
+            out=v_bf[:],
+            in0=v_raw[:].rearrange("p j e -> p e j"),
+            scalar=2.0,
+            in1=t_half_sign[:].unsqueeze(1).to_broadcast([P, D, PACK]),
+            op0=ALU.mult,
+            op1=ALU.mult,
+        )
+        round_q(2)
         nc.vector.quantize_mx(
             out=v_codes[:].bitcast(FP8X4), scales=v_scales[:], in_=v_bf[:].rearrange("p e j -> p (e j)")
         )
+        quantize_q(2)
 
-        last = UNITS - 1
-        half = QT // 2
-        den_at = {5: GROUPS[0], 9: GROUPS[1], 13: GROUPS[2]}
-        cap(0)
-        for u in range(last - 1):
-            cap(u + 1, 0, QT if u + 1 < last - 1 else half)
-            if u % 2 == 0:
-                score_pair(u + H)
-            elif u >= 3:
-                values(u - 3)
-                values(u - 2)
-            weigh(u)
-            if u - 1 in den_at:
-                invert(*den_at[u - 1])
-            scale_w(u)
-            if u == 0:
-                round_q(2)
+        for half in range(2):
+            for r in (2 * half, 2 * half + 1):
+                for h, c in GROUPS[0]:
+                    score_pass(h, c, r)
+            for n in range(2):
+                cap(0, n, 2 * half, 2 * half + 2)
+            for n in range(2):
+                for r in (2 * half, 2 * half + 1):
+                    weigh(0, r, n, n + 1)
+        scores(1, 0)
+        scores(1, 1)
+        cap(1, 0)
+
+        def after_weights(i):
+            n = len(GROUPS[i])
+            interleave(i, 0)
+            if i > 0:
+                add_sink(i - 1)
+            interleave(i, 1)
+            if i > 0:
+                invert(i - 1)
+            quantize_w(i, 0)
+            if i > 0:
+                divide(i - 1)
+            if i == 0:
+                round_q(3)
+            quantize_w(i, 1)
+            if i == 0:
+                quantize_q(3)
+
+        last = len(GROUPS) - 1
+        after_weights(0)
+        for i in range(1, last - 1):
+            cap(i, 1)
+            scores(i + 1, 0)
+            cap(i + 1, 0)
+            if i + 1 < last - 1:
+                scores(i + 1, 1)
             else:
-                quantize_w(u - 1)
-            if u == 1:
-                quantize_q(2)
-            if u == 2:
-                nc.vector.transpose(out=sink_sb[:], in_=sink_rows[:])
-            if u in den_at:
-                add_sink(*den_at[u])
-            if u - 1 in den_at:
-                divide_group(*den_at[u - 1])
-        values(last - 3)
-        cap(last - 1, half, QT)
-        weigh(last - 1, 0, half)
-        cap(last, 0, half)
-        weigh(last - 1, half, QT)
-        cap(last, half, QT)
-        weigh(last, 0, half)
-        weigh(last, half, QT)
-        scale_w(last - 1, 0, half)
-        quantize_w(last - 2)
-        values(last - 2)
-        invert(*GROUPS[2])
-        divide_on_scalar(*GROUPS[2])
-        scale_w(last - 1, half, QT)
-        scale_w(last, 0, half)
-        quantize_w(last - 1)
-        values(last - 1)
-        scale_w(last, half, QT)
-        quantize_w(last, 0, half)
-        add_sink(*GROUPS[3])
-        quantize_w(last, half, QT)
-        values(last)
-        invert(*GROUPS[3])
-        divide_on_scalar(*GROUPS[3])
-        add_sink(*GROUPS[4])
-        invert(*GROUPS[4])
-        add_sink(*GROUPS[5])
-        divide_on_scalar(*GROUPS[4])
-        invert(*GROUPS[5])
-        divide_on_vector(last)
+                scores(last, 0)
+            values(i - 1, 0)
+            values(i - 1, 1)
+            for r in range(PACK):
+                weigh(i, r)
+            after_weights(i)
+        cap(last, 0)
+        values(last - 2, 0)
+        values(last - 2, 1)
+        for i in (last - 1, last):
+            for r in range(PACK):
+                weigh(i, r, 0, 1)
+        interleave(last - 1, 0)
+        interleave(last, 0)
+        quantize_w(last - 1, 0)
+        values(last - 1, 0)
+        add_sink(last - 2)
+        quantize_w(last, 0)
+        values(last, 0)
+        invert(last - 2)
+        divide_on_scalar(last - 2)
+        add_sink(last - 1)
+        invert(last - 1)
+        add_sink(last)
+        divide_on_scalar(last - 1)
+        invert(last)
+        divide(last)

@@ -20,14 +20,14 @@ ROWS = D // PACK
 QT = 128
 CHUNKS = NQ // QT
 GROUPS = [
-    [(0, 0), (2, 0)],
-    [(0, 1), (2, 1)],
-    [(1, 0), (3, 0)],
-    [(0, 2), (2, 2)],
-    [(1, 1), (3, 1)],
-    [(0, 3), (2, 3)],
-    [(1, 2), (3, 2)],
-    [(1, 3)],
+    [(1, 0), (2, 0)],
+    [(1, 1), (2, 1)],
+    [(0, 0), (3, 0)],
+    [(0, 1), (3, 1)],
+    [(1, 2), (2, 2)],
+    [(0, 2), (3, 2)],
+    [(1, 3), (2, 3)],
+    [(0, 3)],
     [(3, 3)],
 ]
 
@@ -51,9 +51,9 @@ def tile_rows_sink_cap_gqa_kernel(tc, qT, kT, t, v, sink, out):
         t_half_sign = sb.tile([P, PACK], F32)
         sink_sb = sb.tile([P, H, CHUNKS], F32)
 
-        q_bf = [sb.tile([P, QT, PACK], BF16, align_bytes=64, name="q_bf%d" % c) for c in range(CHUNKS)]
-        q_codes = [sb.tile([P, QT], I32, align_bytes=64, name="q_codes%d" % c) for c in range(CHUNKS)]
-        q_scales = [sb.tile([P, QT], U8, align_bytes=64, name="q_scales%d" % c) for c in range(CHUNKS)]
+        q_bf = [sb.tile([P, QT, PACK], BF16, align_bytes=64, name="q_bf%d" % c) for c in range(CHUNKS + 1)]
+        q_codes = [sb.tile([P, QT], I32, align_bytes=64, name="q_codes%d" % c) for c in range(CHUNKS + 1)]
+        q_scales = [sb.tile([P, QT], U8, align_bytes=64, name="q_scales%d" % c) for c in range(CHUNKS + 1)]
         k_bf = [sb.tile([P, 2, P, PACK], BF16, align_bytes=64, name="k_bf%d" % i) for i in range(2)]
         k_mx = [sb.tile([P, N + N // PACK], I32, align_bytes=64, name="k_mx%d" % i) for i in range(2)]
         v_bf = sb.tile([P, D, PACK], BF16, align_bytes=64)
@@ -71,6 +71,7 @@ def tile_rows_sink_cap_gqa_kernel(tc, qT, kT, t, v, sink, out):
         w_bf = per_group("w_bf", [QT, PACK], BF16)
         w_codes = per_group("w_codes", [QT], I32)
         w_scales = per_group("w_scales", [QT], U8)
+        logits = [sb.tile([P, QT, PACK], F32, name="logits%d" % i) for i in range(2)]
         den = per_group("den", [], F32)
         rec = per_group("rec", [], F32)
         res = per_group("res", [D], F32)
@@ -78,6 +79,7 @@ def tile_rows_sink_cap_gqa_kernel(tc, qT, kT, t, v, sink, out):
         y_banks = [ps.tile([P, PACK, D], F32, name="y%d" % i) for i in range(4)]
 
         live = slice(0, 3 * ROWS)
+        last = len(GROUPS) - 1
 
         def k_codes(i):
             return k_mx[i][:, 0:N]
@@ -97,6 +99,14 @@ def tile_rows_sink_cap_gqa_kernel(tc, qT, kT, t, v, sink, out):
                 in_=q_bf[c][:].rearrange("p q j -> p (q j)"),
             )
 
+        def first_q():
+            nc.vector.tensor_copy(out=q_bf[CHUNKS][live], in_=q_raw[0][live].rearrange("p j q -> p q j"))
+            nc.vector.quantize_mx(
+                out=q_codes[CHUNKS][live].bitcast(FP8X4),
+                scales=q_scales[CHUNKS][live],
+                in_=q_bf[CHUNKS][live].rearrange("p q j -> p (q j)"),
+            )
+
         def round_k(i):
             src = k_raw[live, :].rearrange("p (j s r) -> p s j r", j=PACK, r=PACK)[:, :, :, 2 * i : 2 * i + 2]
             nc.vector.tensor_copy(out=k_bf[i][live].rearrange("p r s j -> p s j r"), in_=src)
@@ -112,12 +122,14 @@ def tile_rows_sink_cap_gqa_kernel(tc, qT, kT, t, v, sink, out):
         def score_pass(h, c, r):
             rows = slice(ROWS * h, ROWS * (h + 1))
             kc = slice(r * P, (r + 1) * P)
+            copied = int(h in (0, 3))
+            qi = CHUNKS if (c == 0 and not copied) else c
             nc.tensor.matmul_mx(
                 out=score_banks[h][:, r, :],
-                lhsT=k_codes(h % 2)[rows, kc].bitcast(FP8X4),
-                lhsT_scale=k_scales(h % 2)[rows, kc],
-                rhs=q_codes[c][rows, :].bitcast(FP8X4),
-                rhs_scale=q_scales[c][rows, :],
+                lhsT=k_codes(copied)[rows, kc].bitcast(FP8X4),
+                lhsT_scale=k_scales(copied)[rows, kc],
+                rhs=q_codes[qi][rows, :].bitcast(FP8X4),
+                rhs_scale=q_scales[qi][rows, :],
                 start=True,
                 stop=True,
             )
@@ -142,14 +154,35 @@ def tile_rows_sink_cap_gqa_kernel(tc, qT, kT, t, v, sink, out):
                 bias=t_ln[:, r : r + 1],
             )
 
+        def cap_interleaved(i):
+            nc.scalar.activation(
+                out=capped[i][:, 0].rearrange("p r q -> p (r q)").rearrange("p (q r) -> p q r", r=PACK),
+                in_=score_banks[GROUPS[i][0][0]][:].rearrange("p r q -> p q r"),
+                func=ACT.Tanh,
+                scale=1.0 / CAP,
+            )
+
+        def add_ln(i):
+            nc.vector.scalar_tensor_tensor(
+                out=logits[i - last + 1][:],
+                in0=capped[i][:, 0].rearrange("p r q -> p (r q)").rearrange("p (q r) -> p q r", r=PACK),
+                scalar=CAP,
+                in1=t_ln[:].unsqueeze(1).to_broadcast([P, QT, PACK]),
+                op0=ALU.mult,
+                op1=ALU.add,
+            )
+
+        def weigh_interleaved(i, q0=0, q1=QT):
+            nc.scalar.activation(out=w_bf[i][:, 0, q0:q1, :], in_=logits[i - last + 1][:, q0:q1, :], func=ACT.Exp)
+
         def interleave(i, n):
             nc.vector.tensor_copy(out=w_bf[i][:, n], in_=w_rows[i][:, n].rearrange("p r q -> p q r"))
 
-        def quantize_w(i, n):
+        def quantize_w(i, n, q0=0, q1=QT):
             nc.vector.quantize_mx(
-                out=w_codes[i][:, n, :].bitcast(FP8X4),
-                scales=w_scales[i][:, n, :],
-                in_=w_bf[i][:, n].rearrange("p q r -> p (q r)"),
+                out=w_codes[i][:, n, q0:q1].bitcast(FP8X4),
+                scales=w_scales[i][:, n, q0:q1],
+                in_=w_bf[i][:, n, q0:q1, :].rearrange("p q r -> p (q r)"),
             )
 
         def values(i, n):
@@ -165,7 +198,8 @@ def tile_rows_sink_cap_gqa_kernel(tc, qT, kT, t, v, sink, out):
 
         def heads(i):
             h, c = GROUPS[i][0]
-            return slice(h, h + 2 * len(GROUPS[i]) - 1, 2), c
+            h1 = GROUPS[i][-1][0]
+            return slice(h, h1 + 1, max(h1 - h, 1)), c
 
         def add_sink(i):
             hs, c = heads(i)
@@ -199,18 +233,18 @@ def tile_rows_sink_cap_gqa_kernel(tc, qT, kT, t, v, sink, out):
                 )
             store(i)
 
-        nc.scalar.dma_start(out=t_sb[:], in_=t.rearrange("(p j) o -> p (j o)", j=PACK))
-        nc.sync.dma_start(out=q_raw[0][:], in_=q_src[:, :, 0:128])
+        nc.sync.dma_start(out=t_sb[:], in_=t.rearrange("(p j) o -> p (j o)", j=PACK))
         nc.scalar.dma_start(out=k_raw[2 * ROWS : 3 * ROWS, :], in_=k_src)
-        nc.sync.dma_start(out=k_raw[0:ROWS, :], in_=k_src)
+        nc.sync.dma_start(out=q_raw[0][ROWS : 3 * ROWS], in_=q_src[ROWS : 3 * ROWS, :, 0:128])
+        nc.sync.dma_start(out=k_raw[ROWS : 2 * ROWS, :], in_=k_src)
         nc.sync.dma_start(out=q_raw[1][:], in_=q_src[:, :, 128:256])
         nc.sync.dma_start(out=v_raw[:], in_=v[0].rearrange("(p j) e -> p j e", j=PACK))
+        nc.sync.dma_start(out=q_raw[0][3 * ROWS :], in_=q_src[3 * ROWS :, :, 0:128])
         nc.sync.dma_start(out=q_raw[2][:], in_=q_src[:, :, 256:512])
-        with nc.allow_non_contiguous_dma(reason="one sink a query row"):
-            nc.sync.dma_start(out=sink_sb[:], in_=sink.rearrange("h (c p) o -> p h (c o)", p=QT))
 
+        nc.vector.memset(q_raw[0][0:ROWS], 0.0)
+        nc.vector.memset(k_raw[0:ROWS, :], 0.0)
         nc.vector.memset(k_mx[0][:, N:], 0)
-        nc.vector.memset(k_raw[ROWS : 2 * ROWS, :], 0.0)
         nc.vector.scalar_tensor_tensor(
             out=t_abs[:], in0=t_sb[:], scalar=-1.0, in1=t_sb[:], op0=ALU.mult, op1=ALU.max
         )
@@ -219,8 +253,8 @@ def tile_rows_sink_cap_gqa_kernel(tc, qT, kT, t, v, sink, out):
         )
         nc.scalar.activation(out=t_ln[:], in_=t_abs[:], func=ACT.Ln)
 
-        round_q(0)
-        quantize_q(0)
+        first_q()
+        nc.sync.dma_start(out=q_raw[0][0:ROWS], in_=q_src[0:ROWS, :, 0:128])
         round_k(0)
         quantize_k(0)
         quantize_k(1)
@@ -229,10 +263,11 @@ def tile_rows_sink_cap_gqa_kernel(tc, qT, kT, t, v, sink, out):
         quantize_k(2)
         quantize_k(3)
         quantize_q(1)
-        for i in range(2):
-            nc.sync.dma_start(
-                out=k_mx[1][(2 * i + 1) * ROWS : (2 * i + 2) * ROWS, :], in_=k_mx[0][2 * i * ROWS : (2 * i + 1) * ROWS, :]
-            )
+        nc.sync.dma_start(out=k_mx[1][0:ROWS, :], in_=k_mx[0][ROWS : 2 * ROWS, :])
+        nc.sync.dma_start(out=k_mx[1][3 * ROWS :, :], in_=k_mx[0][2 * ROWS : 3 * ROWS, :])
+        with nc.allow_non_contiguous_dma(reason="one sink a query row"):
+            nc.sync.dma_start(out=sink_sb[:], in_=sink.rearrange("h (c p) o -> p h (c o)", p=QT))
+        round_q(0)
         nc.vector.scalar_tensor_tensor(
             out=v_bf[:],
             in0=v_raw[:].rearrange("p j e -> p e j"),
@@ -241,11 +276,10 @@ def tile_rows_sink_cap_gqa_kernel(tc, qT, kT, t, v, sink, out):
             op0=ALU.mult,
             op1=ALU.mult,
         )
-        round_q(2)
+        quantize_q(0)
         nc.vector.quantize_mx(
             out=v_codes[:].bitcast(FP8X4), scales=v_scales[:], in_=v_bf[:].rearrange("p e j -> p (e j)")
         )
-        quantize_q(2)
 
         for half in range(2):
             for r in (2 * half, 2 * half + 1):
@@ -261,55 +295,67 @@ def tile_rows_sink_cap_gqa_kernel(tc, qT, kT, t, v, sink, out):
         cap(1, 0)
 
         def after_weights(i):
-            n = len(GROUPS[i])
             interleave(i, 0)
             if i > 0:
-                add_sink(i - 1)
+                invert(i - 1)
             interleave(i, 1)
             if i > 0:
-                invert(i - 1)
-            quantize_w(i, 0)
-            if i > 0:
                 divide(i - 1)
-            if i == 0:
-                round_q(3)
+            quantize_w(i, 0)
+            if i < 2:
+                round_q(2 + i)
             quantize_w(i, 1)
-            if i == 0:
-                quantize_q(3)
+            if i < 2:
+                quantize_q(2 + i)
 
-        last = len(GROUPS) - 1
+        scores(2, 0)
         after_weights(0)
-        for i in range(1, last - 1):
+        pairs = last - 1
+        for i in range(1, pairs):
             cap(i, 1)
-            scores(i + 1, 0)
-            cap(i + 1, 0)
-            if i + 1 < last - 1:
+            if i + 1 < pairs:
                 scores(i + 1, 1)
+                cap(i + 1, 0)
+                scores(i + 2, 0)
             else:
                 scores(last, 0)
+                cap_interleaved(last - 1)
+                cap_interleaved(last)
             values(i - 1, 0)
             values(i - 1, 1)
+            if i + 1 < pairs:
+                add_sink(i - 1)
+            else:
+                add_ln(last - 1)
+                add_sink(i - 1)
+                add_ln(last)
+                invert(i - 1)
             for r in range(PACK):
                 weigh(i, r)
-            after_weights(i)
-        cap(last, 0)
-        values(last - 2, 0)
-        values(last - 2, 1)
-        for i in (last - 1, last):
-            for r in range(PACK):
-                weigh(i, r, 0, 1)
-        interleave(last - 1, 0)
-        interleave(last, 0)
+            if i + 1 < pairs:
+                after_weights(i)
+        half = QT // 2
+        weigh_interleaved(last - 1)
+        weigh_interleaved(last, 0, half)
+        weigh_interleaved(last, half, QT)
+        divide(last - 3)
+        interleave(last - 2, 0)
+        interleave(last - 2, 1)
+        quantize_w(last - 2, 0)
         quantize_w(last - 1, 0)
+        quantize_w(last - 2, 1)
+        quantize_w(last, 0, 0, half)
+        quantize_w(last, 0, half, QT)
+        values(last - 2, 0)
         values(last - 1, 0)
-        add_sink(last - 2)
-        quantize_w(last, 0)
+        values(last - 2, 1)
         values(last, 0)
-        invert(last - 2)
-        divide_on_scalar(last - 2)
         add_sink(last - 1)
+        add_sink(last - 2)
         invert(last - 1)
         add_sink(last)
-        divide_on_scalar(last - 1)
+        invert(last - 2)
         invert(last)
+        divide_on_scalar(last - 1)
+        divide_on_scalar(last - 2)
         divide(last)

@@ -26,9 +26,9 @@ GROUPS = [
     [(0, 1), (3, 1)],
     [(1, 2), (2, 2)],
     [(0, 2), (3, 2)],
-    [(1, 3), (2, 3)],
-    [(0, 3)],
-    [(3, 3)],
+    [(1, 3)],
+    [(0, 3), (3, 3)],
+    [(2, 3)],
 ]
 
 
@@ -75,11 +75,16 @@ def tile_rows_sink_cap_gqa_kernel(tc, qT, kT, t, v, sink, out):
         den = per_group("den", [], F32)
         rec = per_group("rec", [], F32)
         res = per_group("res", [D], F32)
-        score_banks = [ps.tile([P, PACK, QT], F32, name="score%d" % g) for g in range(H)]
-        y_banks = [ps.tile([P, PACK, D], F32, name="y%d" % i) for i in range(4)]
+        score_banks = [ps.tile([P, PACK, QT], F32, name="score%d" % g) for g in range(H + 1)]
+        y_banks = [ps.tile([P, PACK, D], F32, name="y%d" % i) for i in range(3)]
 
         live = slice(0, 3 * ROWS)
         last = len(GROUPS) - 1
+
+        def y_of(i):
+            if i == last:
+                return y_banks[(i - 2) % 3][:, 1:]
+            return y_banks[i % 3]
 
         def k_codes(i):
             return k_mx[i][:, 0:N]
@@ -119,13 +124,17 @@ def tile_rows_sink_cap_gqa_kernel(tc, qT, kT, t, v, sink, out):
                 in_=k_bf[r // 2][live, r % 2].rearrange("p s j -> p (s j)"),
             )
 
+        def bank_of(h, c, r):
+            second = h == 1 and (r == 1 if c == 0 else c % 2 == 1)
+            return score_banks[H if second else h]
+
         def score_pass(h, c, r):
             rows = slice(ROWS * h, ROWS * (h + 1))
             kc = slice(r * P, (r + 1) * P)
             copied = int(h in (0, 3))
             qi = CHUNKS if (c == 0 and not copied) else c
             nc.tensor.matmul_mx(
-                out=score_banks[h][:, r, :],
+                out=bank_of(h, c, r)[:, r, :],
                 lhsT=k_codes(copied)[rows, kc].bitcast(FP8X4),
                 lhsT_scale=k_scales(copied)[rows, kc],
                 rhs=q_codes[qi][rows, :].bitcast(FP8X4),
@@ -140,9 +149,9 @@ def tile_rows_sink_cap_gqa_kernel(tc, qT, kT, t, v, sink, out):
                 score_pass(h, c, r)
 
         def cap(i, n, r0=0, r1=PACK):
-            h = GROUPS[i][n][0]
+            h, c = GROUPS[i][n]
             nc.scalar.activation(
-                out=capped[i][:, n, r0:r1, :], in_=score_banks[h][:, r0:r1, :], func=ACT.Tanh, scale=1.0 / CAP
+                out=capped[i][:, n, r0:r1, :], in_=bank_of(h, c, r0)[:, r0:r1, :], func=ACT.Tanh, scale=1.0 / CAP
             )
 
         def weigh(i, r, n0=0, n1=2):
@@ -154,26 +163,30 @@ def tile_rows_sink_cap_gqa_kernel(tc, qT, kT, t, v, sink, out):
                 bias=t_ln[:, r : r + 1],
             )
 
-        def cap_interleaved(i):
+        def in_word_order(i, n):
+            return capped[i][:, n].rearrange("p r q -> p (r q)").rearrange("p (q r) -> p q r", r=PACK)
+
+        def cap_interleaved(i, n):
+            h, c = GROUPS[i][n]
             nc.scalar.activation(
-                out=capped[i][:, 0].rearrange("p r q -> p (r q)").rearrange("p (q r) -> p q r", r=PACK),
-                in_=score_banks[GROUPS[i][0][0]][:].rearrange("p r q -> p q r"),
+                out=in_word_order(i, n),
+                in_=bank_of(h, c, 0)[:].rearrange("p r q -> p q r"),
                 func=ACT.Tanh,
                 scale=1.0 / CAP,
             )
 
-        def add_ln(i):
+        def add_ln(i, n):
             nc.vector.scalar_tensor_tensor(
-                out=logits[i - last + 1][:],
-                in0=capped[i][:, 0].rearrange("p r q -> p (r q)").rearrange("p (q r) -> p q r", r=PACK),
+                out=logits[last - i][:],
+                in0=in_word_order(i, n),
                 scalar=CAP,
                 in1=t_ln[:].unsqueeze(1).to_broadcast([P, QT, PACK]),
                 op0=ALU.mult,
                 op1=ALU.add,
             )
 
-        def weigh_interleaved(i, q0=0, q1=QT):
-            nc.scalar.activation(out=w_bf[i][:, 0, q0:q1, :], in_=logits[i - last + 1][:, q0:q1, :], func=ACT.Exp)
+        def weigh_interleaved(i, n, q0=0, q1=QT):
+            nc.scalar.activation(out=w_bf[i][:, n, q0:q1, :], in_=logits[last - i][:, q0:q1, :], func=ACT.Exp)
 
         def interleave(i, n):
             nc.vector.tensor_copy(out=w_bf[i][:, n], in_=w_rows[i][:, n].rearrange("p r q -> p q r"))
@@ -187,7 +200,7 @@ def tile_rows_sink_cap_gqa_kernel(tc, qT, kT, t, v, sink, out):
 
         def values(i, n):
             nc.tensor.matmul_mx(
-                out=y_banks[i % 4][:, n, :],
+                out=y_of(i)[:, n, :],
                 lhsT=w_codes[i][:, n, :].bitcast(FP8X4),
                 lhsT_scale=w_scales[i][:, n, :],
                 rhs=v_codes[:].bitcast(FP8X4),
@@ -204,15 +217,15 @@ def tile_rows_sink_cap_gqa_kernel(tc, qT, kT, t, v, sink, out):
         def add_sink(i):
             hs, c = heads(i)
             nc.vector.tensor_tensor(
-                out=den[i][:], in0=y_banks[i % 4][:, 0 : len(GROUPS[i]), D - 1], in1=sink_sb[:, hs, c], op=ALU.add
+                out=den[i][:], in0=y_of(i)[:, 0 : len(GROUPS[i]), D - 1], in1=sink_sb[:, hs, c], op=ALU.add
             )
 
         def invert(i):
             nc.vector.reciprocal(out=rec[i][:], in_=den[i][:])
 
-        def store(i):
+        def store(i, queue=nc.sync):
             hs, c = heads(i)
-            nc.sync.dma_start(
+            queue.dma_start(
                 out=out[hs, c * QT : (c + 1) * QT, :].rearrange("h p e -> p h e"), in_=res[i][:]
             )
 
@@ -220,18 +233,18 @@ def tile_rows_sink_cap_gqa_kernel(tc, qT, kT, t, v, sink, out):
             n = len(GROUPS[i])
             nc.vector.tensor_tensor(
                 out=res[i][:],
-                in0=y_banks[i % 4][:, 0:n, :],
+                in0=y_of(i)[:, 0:n, :],
                 in1=rec[i][:].unsqueeze(2).to_broadcast([P, n, D]),
                 op=ALU.mult,
             )
             store(i)
 
-        def divide_on_scalar(i):
+        def divide_on_scalar(i, queue=nc.sync):
             for n in range(len(GROUPS[i])):
                 nc.scalar.activation(
-                    out=res[i][:, n, :], in_=y_banks[i % 4][:, n, :], func=ACT.Copy, scale=rec[i][:, n : n + 1]
+                    out=res[i][:, n, :], in_=y_of(i)[:, n, :], func=ACT.Copy, scale=rec[i][:, n : n + 1]
                 )
-            store(i)
+            store(i, queue)
 
         nc.sync.dma_start(out=t_sb[:], in_=t.rearrange("(p j) o -> p (j o)", j=PACK))
         nc.scalar.dma_start(out=k_raw[2 * ROWS : 3 * ROWS, :], in_=k_src)
@@ -281,12 +294,19 @@ def tile_rows_sink_cap_gqa_kernel(tc, qT, kT, t, v, sink, out):
             out=v_codes[:].bitcast(FP8X4), scales=v_scales[:], in_=v_bf[:].rearrange("p e j -> p (e j)")
         )
 
+        for r in range(2):
+            score_pass(1, 0, r)
+        for r in range(2):
+            score_pass(2, 0, r)
+        cap(0, 0, 0, 1)
+        cap(0, 0, 1, 2)
+        cap(0, 1, 0, 2)
         for half in range(2):
-            for r in (2 * half, 2 * half + 1):
-                for h, c in GROUPS[0]:
-                    score_pass(h, c, r)
-            for n in range(2):
-                cap(0, n, 2 * half, 2 * half + 2)
+            if half == 1:
+                for n, (h, c) in enumerate(GROUPS[0]):
+                    for r in (2, 3):
+                        score_pass(h, c, r)
+                    cap(0, n, 2, 4)
             for n in range(2):
                 for r in (2 * half, 2 * half + 1):
                     weigh(0, r, n, n + 1)
@@ -310,7 +330,7 @@ def tile_rows_sink_cap_gqa_kernel(tc, qT, kT, t, v, sink, out):
 
         scores(2, 0)
         after_weights(0)
-        pairs = last - 1
+        pairs = last - 2
         for i in range(1, pairs):
             cap(i, 1)
             if i + 1 < pairs:
@@ -318,44 +338,53 @@ def tile_rows_sink_cap_gqa_kernel(tc, qT, kT, t, v, sink, out):
                 cap(i + 1, 0)
                 scores(i + 2, 0)
             else:
+                scores(i + 2, 0)
+                cap(i + 1, 0)
                 scores(last, 0)
-                cap_interleaved(last - 1)
-                cap_interleaved(last)
             values(i - 1, 0)
             values(i - 1, 1)
-            if i + 1 < pairs:
-                add_sink(i - 1)
-            else:
-                add_ln(last - 1)
-                add_sink(i - 1)
-                add_ln(last)
-                invert(i - 1)
+            add_sink(i - 1)
             for r in range(PACK):
                 weigh(i, r)
-            if i + 1 < pairs:
-                after_weights(i)
+            after_weights(i)
+
         half = QT // 2
-        weigh_interleaved(last - 1)
-        weigh_interleaved(last, 0, half)
-        weigh_interleaved(last, half, QT)
-        divide(last - 3)
-        interleave(last - 2, 0)
-        interleave(last - 2, 1)
-        quantize_w(last - 2, 0)
-        quantize_w(last - 1, 0)
-        quantize_w(last - 2, 1)
-        quantize_w(last, 0, 0, half)
-        quantize_w(last, 0, half, QT)
-        values(last - 2, 0)
-        values(last - 1, 0)
-        values(last - 2, 1)
-        values(last, 0)
-        add_sink(last - 1)
-        add_sink(last - 2)
-        invert(last - 1)
-        add_sink(last)
-        invert(last - 2)
-        invert(last)
-        divide_on_scalar(last - 1)
-        divide_on_scalar(last - 2)
-        divide(last)
+        a, b, d = range(pairs, last + 1)
+        scores(b, 1)
+        cap(b, 0)
+        for r in range(PACK):
+            weigh(a, r, 0, 1)
+        cap_interleaved(b, 1)
+        cap_interleaved(d, 0)
+        for r in range(PACK):
+            weigh(b, r, 0, 1)
+        values(a - 1, 0)
+        values(a - 1, 1)
+        interleave(a, 0)
+        quantize_w(a, 0)
+        values(a, 0)
+        add_ln(b, 1)
+        add_ln(d, 0)
+        weigh_interleaved(b, 1)
+        weigh_interleaved(d, 0, 0, half)
+        weigh_interleaved(d, 0, half, QT)
+        add_sink(a - 1)
+        add_sink(a)
+        interleave(b, 0)
+        invert(a - 1)
+        divide_on_scalar(a - 1)
+        invert(a)
+        quantize_w(b, 1)
+        values(b, 1)
+        quantize_w(b, 0)
+        values(b, 0)
+        divide(a)
+        quantize_w(d, 0, 0, half)
+        quantize_w(d, 0, half, QT)
+        values(d, 0)
+        add_sink(b)
+        invert(b)
+        divide_on_scalar(b, nc.scalar)
+        add_sink(d)
+        invert(d)
+        divide(d)

@@ -20,15 +20,15 @@ ROWS = D // PACK
 QT = 128
 CHUNKS = NQ // QT
 GROUPS = [
+    [(0, 0), (0, 1)],
+    [(0, 2), (0, 3)],
     [(1, 0), (2, 0)],
-    [(1, 1), (2, 1)],
-    [(0, 0), (3, 0)],
-    [(0, 1), (3, 1)],
+    [(1, 1), (3, 0)],
+    [(2, 1), (3, 1)],
     [(1, 2), (2, 2)],
-    [(0, 2), (3, 2)],
-    [(1, 3)],
-    [(0, 3), (3, 3)],
-    [(2, 3)],
+    [(3, 2)],
+    [(1, 3), (2, 3)],
+    [(3, 3)],
 ]
 
 
@@ -41,21 +41,21 @@ def tile_rows_sink_cap_gqa_kernel(tc, qT, kT, t, v, sink, out):
 
         q_src = qT.rearrange("h (p j) q -> (h p) j q", j=PACK)
         k_src = kT[0].rearrange("(p j) i -> p (j i)", j=PACK)
-        q_loads = [(0, 128), (128, 256), (256, 512)]
+        q_loads = [(0, 256), (256, 512)]
         q_raw = [sb.tile([P, PACK, b - a], F32, name="q_raw%d" % a) for a, b in q_loads]
-        k_raw = sb.tile([P, PACK * N], F32)
+        k_raw = sb.tile([ROWS, PACK * N], F32)
         v_raw = sb.tile([P, PACK, D], F32)
         t_sb = sb.tile([P, PACK], F32)
         t_abs = sb.tile([P, PACK], F32)
         t_ln = sb.tile([P, PACK], F32)
         t_half_sign = sb.tile([P, PACK], F32)
-        sink_sb = sb.tile([P, H, CHUNKS], F32)
+        sink_sb = sb.tile([P, H * CHUNKS], F32)
 
-        q_bf = [sb.tile([P, QT, PACK], BF16, align_bytes=64, name="q_bf%d" % c) for c in range(CHUNKS + 1)]
-        q_codes = [sb.tile([P, QT], I32, align_bytes=64, name="q_codes%d" % c) for c in range(CHUNKS + 1)]
-        q_scales = [sb.tile([P, QT], U8, align_bytes=64, name="q_scales%d" % c) for c in range(CHUNKS + 1)]
-        k_bf = [sb.tile([P, 2, P, PACK], BF16, align_bytes=64, name="k_bf%d" % i) for i in range(2)]
-        k_mx = [sb.tile([P, N + N // PACK], I32, align_bytes=64, name="k_mx%d" % i) for i in range(2)]
+        q_bf = [sb.tile([P, QT, PACK], BF16, align_bytes=64, name="q_bf%d" % c) for c in range(CHUNKS + 2)]
+        q_codes = [sb.tile([P, QT], I32, align_bytes=64, name="q_codes%d" % c) for c in range(CHUNKS + 2)]
+        q_scales = [sb.tile([P, QT], U8, align_bytes=64, name="q_scales%d" % c) for c in range(CHUNKS + 2)]
+        k_bf = [sb.tile([ROWS, 2, P, PACK], BF16, align_bytes=64, name="k_bf%d" % i) for i in range(2)]
+        k_mx = sb.tile([P, N + N // PACK], I32, align_bytes=64)
         v_bf = sb.tile([P, D, PACK], BF16, align_bytes=64)
         v_codes = sb.tile([P, D], I32, align_bytes=64)
         v_scales = sb.tile([P, D], U8, align_bytes=64)
@@ -78,7 +78,7 @@ def tile_rows_sink_cap_gqa_kernel(tc, qT, kT, t, v, sink, out):
         score_banks = [ps.tile([P, PACK, QT], F32, name="score%d" % g) for g in range(H + 1)]
         y_banks = [ps.tile([P, PACK, D], F32, name="y%d" % i) for i in range(3)]
 
-        live = slice(0, 3 * ROWS)
+        live = slice(0, ROWS)
         last = len(GROUPS) - 1
 
         def y_of(i):
@@ -86,30 +86,21 @@ def tile_rows_sink_cap_gqa_kernel(tc, qT, kT, t, v, sink, out):
                 return y_banks[(i - 2) % 3][:, 1:]
             return y_banks[i % 3]
 
-        def k_codes(i):
-            return k_mx[i][:, 0:N]
+        k_codes = k_mx[:, 0:N]
+        k_scales = k_mx[:, N:].bitcast(U8)
 
-        def k_scales(i):
-            return k_mx[i][:, N:].bitcast(U8)
+        def round_q(c, first=False):
+            rows = live if first else slice(0, P)
+            src = q_raw[c // 2][rows, :, (c % 2) * QT : (c % 2 + 1) * QT]
+            nc.vector.tensor_copy(out=q_bf[c + CHUNKS * first][rows], in_=src.rearrange("p j q -> p q j"))
 
-        def round_q(c):
-            i = min(c, 2)
-            a = c * QT - q_loads[i][0]
-            nc.vector.tensor_copy(out=q_bf[c][:], in_=q_raw[i][:, :, a : a + QT].rearrange("p j q -> p q j"))
-
-        def quantize_q(c):
+        def quantize_q(c, first=False):
+            rows = live if first else slice(0, P)
+            i = c + CHUNKS * first
             nc.vector.quantize_mx(
-                out=q_codes[c][:].bitcast(FP8X4),
-                scales=q_scales[c][:],
-                in_=q_bf[c][:].rearrange("p q j -> p (q j)"),
-            )
-
-        def first_q():
-            nc.vector.tensor_copy(out=q_bf[CHUNKS][live], in_=q_raw[0][live].rearrange("p j q -> p q j"))
-            nc.vector.quantize_mx(
-                out=q_codes[CHUNKS][live].bitcast(FP8X4),
-                scales=q_scales[CHUNKS][live],
-                in_=q_bf[CHUNKS][live].rearrange("p q j -> p (q j)"),
+                out=q_codes[i][rows].bitcast(FP8X4),
+                scales=q_scales[i][rows],
+                in_=q_bf[i][rows].rearrange("p q j -> p (q j)"),
             )
 
         def round_k(i):
@@ -119,28 +110,33 @@ def tile_rows_sink_cap_gqa_kernel(tc, qT, kT, t, v, sink, out):
         def quantize_k(r):
             cols = slice(r * P, (r + 1) * P)
             nc.vector.quantize_mx(
-                out=k_codes(0)[live, cols].bitcast(FP8X4),
-                scales=k_scales(0)[live, cols],
+                out=k_codes[live, cols].bitcast(FP8X4),
+                scales=k_scales[live, cols],
                 in_=k_bf[r // 2][live, r % 2].rearrange("p s j -> p (s j)"),
             )
 
         def bank_of(h, c, r):
-            second = h == 1 and (r == 1 if c == 0 else c % 2 == 1)
+            second = h == 0 and (r if c < 2 else c) % 2 == 1
             return score_banks[H if second else h]
 
         def score_pass(h, c, r):
             rows = slice(ROWS * h, ROWS * (h + 1))
             kc = slice(r * P, (r + 1) * P)
-            copied = int(h in (0, 3))
-            qi = CHUNKS if (c == 0 and not copied) else c
+            first = h == 0 and c < 2
+            qi = c + CHUNKS * first
             nc.tensor.matmul_mx(
-                out=bank_of(h, c, r)[:, r, :],
-                lhsT=k_codes(copied)[rows, kc].bitcast(FP8X4),
-                lhsT_scale=k_scales(copied)[rows, kc],
+                out=bank_of(h, c, r)[:, c if first else r, :],
+                lhsT=k_codes[rows, kc].bitcast(FP8X4),
+                lhsT_scale=k_scales[rows, kc],
                 rhs=q_codes[qi][rows, :].bitcast(FP8X4),
                 rhs_scale=q_scales[qi][rows, :],
                 start=True,
                 stop=True,
+            )
+
+        def cap_first(r):
+            nc.scalar.activation(
+                out=capped[0][:, :, r, :], in_=bank_of(0, 0, r)[:, 0:2, :], func=ACT.Tanh, scale=1.0 / CAP
             )
 
         def scores(i, n):
@@ -209,25 +205,20 @@ def tile_rows_sink_cap_gqa_kernel(tc, qT, kT, t, v, sink, out):
                 stop=True,
             )
 
-        def heads(i):
-            h, c = GROUPS[i][0]
-            h1 = GROUPS[i][-1][0]
-            return slice(h, h1 + 1, max(h1 - h, 1)), c
+        def places(i):
+            first, final = [CHUNKS * h + c for h, c in (GROUPS[i][0], GROUPS[i][-1])]
+            return slice(first, final + 1, max(final - first, 1))
 
         def add_sink(i):
-            hs, c = heads(i)
             nc.vector.tensor_tensor(
-                out=den[i][:], in0=y_of(i)[:, 0 : len(GROUPS[i]), D - 1], in1=sink_sb[:, hs, c], op=ALU.add
+                out=den[i][:], in0=y_of(i)[:, 0 : len(GROUPS[i]), D - 1], in1=sink_sb[:, places(i)], op=ALU.add
             )
 
         def invert(i):
             nc.vector.reciprocal(out=rec[i][:], in_=den[i][:])
 
         def store(i, queue=nc.sync):
-            hs, c = heads(i)
-            queue.dma_start(
-                out=out[hs, c * QT : (c + 1) * QT, :].rearrange("h p e -> p h e"), in_=res[i][:]
-            )
+            queue.dma_start(out=out.rearrange("h (c p) e -> p (h c) e", p=QT)[:, places(i), :], in_=res[i][:])
 
         def divide(i):
             n = len(GROUPS[i])
@@ -247,17 +238,14 @@ def tile_rows_sink_cap_gqa_kernel(tc, qT, kT, t, v, sink, out):
             store(i, queue)
 
         nc.sync.dma_start(out=t_sb[:], in_=t.rearrange("(p j) o -> p (j o)", j=PACK))
-        nc.scalar.dma_start(out=k_raw[2 * ROWS : 3 * ROWS, :], in_=k_src)
-        nc.sync.dma_start(out=q_raw[0][ROWS : 3 * ROWS], in_=q_src[ROWS : 3 * ROWS, :, 0:128])
-        nc.sync.dma_start(out=k_raw[ROWS : 2 * ROWS, :], in_=k_src)
-        nc.sync.dma_start(out=q_raw[1][:], in_=q_src[:, :, 128:256])
+        nc.scalar.dma_start(out=q_raw[0][live], in_=q_src[live, :, 0:256])
+        nc.sync.dma_start(out=k_raw[:], in_=k_src)
+        nc.sync.dma_start(out=q_raw[1][:], in_=q_src[:, :, 256:512])
+        for rows in (slice(ROWS, 2 * ROWS), slice(2 * ROWS, P)):
+            nc.sync.dma_start(out=q_raw[0][rows], in_=q_src[rows, :, 0:256])
         nc.sync.dma_start(out=v_raw[:], in_=v[0].rearrange("(p j) e -> p j e", j=PACK))
-        nc.sync.dma_start(out=q_raw[0][3 * ROWS :], in_=q_src[3 * ROWS :, :, 0:128])
-        nc.sync.dma_start(out=q_raw[2][:], in_=q_src[:, :, 256:512])
 
-        nc.vector.memset(q_raw[0][0:ROWS], 0.0)
-        nc.vector.memset(k_raw[0:ROWS, :], 0.0)
-        nc.vector.memset(k_mx[0][:, N:], 0)
+        nc.vector.memset(k_mx[live, N:], 0)
         nc.vector.scalar_tensor_tensor(
             out=t_abs[:], in0=t_sb[:], scalar=-1.0, in1=t_sb[:], op0=ALU.mult, op1=ALU.max
         )
@@ -266,21 +254,26 @@ def tile_rows_sink_cap_gqa_kernel(tc, qT, kT, t, v, sink, out):
         )
         nc.scalar.activation(out=t_ln[:], in_=t_abs[:], func=ACT.Ln)
 
-        first_q()
-        nc.sync.dma_start(out=q_raw[0][0:ROWS], in_=q_src[0:ROWS, :, 0:128])
+        for c in range(2):
+            round_q(c, True)
+        for c in range(2):
+            quantize_q(c, True)
         round_k(0)
         quantize_k(0)
         quantize_k(1)
         round_k(1)
-        round_q(1)
+        round_q(2)
         quantize_k(2)
         quantize_k(3)
-        quantize_q(1)
-        nc.sync.dma_start(out=k_mx[1][0:ROWS, :], in_=k_mx[0][ROWS : 2 * ROWS, :])
-        nc.sync.dma_start(out=k_mx[1][3 * ROWS :, :], in_=k_mx[0][2 * ROWS : 3 * ROWS, :])
+        for g in range(1, H):
+            nc.sync.dma_start(out=k_mx[g * ROWS : (g + 1) * ROWS, :], in_=k_mx[live, :])
         with nc.allow_non_contiguous_dma(reason="one sink a query row"):
-            nc.sync.dma_start(out=sink_sb[:], in_=sink.rearrange("h (c p) o -> p h (c o)", p=QT))
+            nc.sync.dma_start(out=sink_sb[:], in_=sink.rearrange("h (c p) o -> p (h c o)", p=QT))
+        quantize_q(2)
+        round_q(3)
         round_q(0)
+        quantize_q(3)
+        quantize_q(0)
         nc.vector.scalar_tensor_tensor(
             out=v_bf[:],
             in0=v_raw[:].rearrange("p j e -> p e j"),
@@ -289,27 +282,19 @@ def tile_rows_sink_cap_gqa_kernel(tc, qT, kT, t, v, sink, out):
             op0=ALU.mult,
             op1=ALU.mult,
         )
-        quantize_q(0)
+        round_q(1)
         nc.vector.quantize_mx(
             out=v_codes[:].bitcast(FP8X4), scales=v_scales[:], in_=v_bf[:].rearrange("p e j -> p (e j)")
         )
+        quantize_q(1)
 
-        for r in range(2):
-            score_pass(1, 0, r)
-        for r in range(2):
-            score_pass(2, 0, r)
-        cap(0, 0, 0, 1)
-        cap(0, 0, 1, 2)
-        cap(0, 1, 0, 2)
         for half in range(2):
-            if half == 1:
-                for n, (h, c) in enumerate(GROUPS[0]):
-                    for r in (2, 3):
-                        score_pass(h, c, r)
-                    cap(0, n, 2, 4)
-            for n in range(2):
-                for r in (2 * half, 2 * half + 1):
-                    weigh(0, r, n, n + 1)
+            for r in (2 * half, 2 * half + 1):
+                for c in range(2):
+                    score_pass(0, c, r)
+                cap_first(r)
+            for r in (2 * half, 2 * half + 1):
+                weigh(0, r)
         scores(1, 0)
         scores(1, 1)
         cap(1, 0)
@@ -322,11 +307,7 @@ def tile_rows_sink_cap_gqa_kernel(tc, qT, kT, t, v, sink, out):
             if i > 0:
                 divide(i - 1)
             quantize_w(i, 0)
-            if i < 2:
-                round_q(2 + i)
             quantize_w(i, 1)
-            if i < 2:
-                quantize_q(2 + i)
 
         scores(2, 0)
         after_weights(0)

@@ -23,7 +23,7 @@ GROUPS = [
     [(0, 0), (0, 1)],
     [(0, 2), (0, 3)],
     [(1, 0), (2, 0)],
-    [(1, 1), (3, 0)],
+    [(3, 0), (1, 1)],
     [(2, 1), (3, 1)],
     [(1, 2), (2, 2)],
     [(3, 2)],
@@ -40,10 +40,10 @@ def tile_rows_sink_cap_gqa_kernel(tc, qT, kT, t, v, sink, out):
         ctx.enter_context(tc.manual_schedule())
 
         q_src = qT.rearrange("h (p j) q -> (h p) j q", j=PACK)
-        k_src = kT[0].rearrange("(p j) i -> p (j i)", j=PACK)
+        k_src = kT[0].rearrange("(p j) i -> p j i", j=PACK)
         q_loads = [(0, 256), (256, 512)]
         q_raw = [sb.tile([P, PACK, b - a], F32, name="q_raw%d" % a) for a, b in q_loads]
-        k_raw = sb.tile([ROWS, PACK * N], F32)
+        k_raw = [sb.tile([ROWS, PACK, N // 2], F32, name="k_raw%d" % i) for i in range(2)]
         v_raw = sb.tile([P, PACK, D], F32)
         t_sb = sb.tile([P, PACK], F32)
         t_abs = sb.tile([P, PACK], F32)
@@ -103,9 +103,10 @@ def tile_rows_sink_cap_gqa_kernel(tc, qT, kT, t, v, sink, out):
                 in_=q_bf[i][rows].rearrange("p q j -> p (q j)"),
             )
 
-        def round_k(i):
-            src = k_raw[live, :].rearrange("p (j s r) -> p s j r", j=PACK, r=PACK)[:, :, :, 2 * i : 2 * i + 2]
-            nc.vector.tensor_copy(out=k_bf[i][live].rearrange("p r s j -> p s j r"), in_=src)
+        def round_k(i, half):
+            src = k_raw[half][:].rearrange("p j (s r) -> p s j r", r=PACK)[:, :, :, 2 * i : 2 * i + 2]
+            dst = k_bf[i][:, :, half * P // 2 : (half + 1) * P // 2, :]
+            nc.vector.tensor_copy(out=dst.rearrange("p r s j -> p s j r"), in_=src)
 
         def quantize_k(r):
             cols = slice(r * P, (r + 1) * P)
@@ -116,7 +117,7 @@ def tile_rows_sink_cap_gqa_kernel(tc, qT, kT, t, v, sink, out):
             )
 
         def bank_of(h, c, r):
-            second = h == 0 and (r if c < 2 else c) % 2 == 1
+            second = h == 0 and r % 2 == 1
             return score_banks[H if second else h]
 
         def score_pass(h, c, r):
@@ -125,7 +126,7 @@ def tile_rows_sink_cap_gqa_kernel(tc, qT, kT, t, v, sink, out):
             first = h == 0 and c < 2
             qi = c + CHUNKS * first
             nc.tensor.matmul_mx(
-                out=bank_of(h, c, r)[:, c if first else r, :],
+                out=bank_of(h, c, r)[:, c % 2 if h == 0 else r, :],
                 lhsT=k_codes[rows, kc].bitcast(FP8X4),
                 lhsT_scale=k_scales[rows, kc],
                 rhs=q_codes[qi][rows, :].bitcast(FP8X4),
@@ -134,9 +135,9 @@ def tile_rows_sink_cap_gqa_kernel(tc, qT, kT, t, v, sink, out):
                 stop=True,
             )
 
-        def cap_first(r):
+        def cap_first(i, r):
             nc.scalar.activation(
-                out=capped[0][:, :, r, :], in_=bank_of(0, 0, r)[:, 0:2, :], func=ACT.Tanh, scale=1.0 / CAP
+                out=capped[i][:, :, r, :], in_=bank_of(0, 0, r)[:, 0:2, :], func=ACT.Tanh, scale=1.0 / CAP
             )
 
         def scores(i, n):
@@ -196,7 +197,7 @@ def tile_rows_sink_cap_gqa_kernel(tc, qT, kT, t, v, sink, out):
 
         def values(i, n):
             nc.tensor.matmul_mx(
-                out=y_of(i)[:, n, :],
+                out=y_of(i)[:, sorted(GROUPS[i]).index(GROUPS[i][n]), :],
                 lhsT=w_codes[i][:, n, :].bitcast(FP8X4),
                 lhsT_scale=w_scales[i][:, n, :],
                 rhs=v_codes[:].bitcast(FP8X4),
@@ -206,7 +207,7 @@ def tile_rows_sink_cap_gqa_kernel(tc, qT, kT, t, v, sink, out):
             )
 
         def places(i):
-            first, final = [CHUNKS * h + c for h, c in (GROUPS[i][0], GROUPS[i][-1])]
+            first, final = [CHUNKS * h + c for h, c in (min(GROUPS[i]), max(GROUPS[i]))]
             return slice(first, final + 1, max(final - first, 1))
 
         def add_sink(i):
@@ -237,11 +238,12 @@ def tile_rows_sink_cap_gqa_kernel(tc, qT, kT, t, v, sink, out):
                 )
             store(i, queue)
 
-        nc.sync.dma_start(out=t_sb[:], in_=t.rearrange("(p j) o -> p (j o)", j=PACK))
-        nc.scalar.dma_start(out=q_raw[0][live], in_=q_src[live, :, 0:256])
-        nc.sync.dma_start(out=k_raw[:], in_=k_src)
+        nc.scalar.dma_start(out=t_sb[:], in_=t.rearrange("(p j) o -> p (j o)", j=PACK))
+        nc.sync.dma_start(out=q_raw[0][live], in_=q_src[live, :, 0:256])
+        for half in range(2):
+            nc.sync.dma_start(out=k_raw[half][:], in_=k_src[:, :, half * N // 2 : (half + 1) * N // 2])
         nc.sync.dma_start(out=q_raw[1][:], in_=q_src[:, :, 256:512])
-        for rows in (slice(ROWS, 2 * ROWS), slice(2 * ROWS, P)):
+        for rows in (slice(ROWS, 3 * ROWS), slice(3 * ROWS, P)):
             nc.sync.dma_start(out=q_raw[0][rows], in_=q_src[rows, :, 0:256])
         nc.sync.dma_start(out=v_raw[:], in_=v[0].rearrange("(p j) e -> p j e", j=PACK))
 
@@ -258,22 +260,26 @@ def tile_rows_sink_cap_gqa_kernel(tc, qT, kT, t, v, sink, out):
             round_q(c, True)
         for c in range(2):
             quantize_q(c, True)
-        round_k(0)
+        round_k(0, 0)
+        round_k(0, 1)
+        round_k(1, 0)
         quantize_k(0)
         quantize_k(1)
-        round_k(1)
-        round_q(2)
+        round_k(1, 1)
         quantize_k(2)
         quantize_k(3)
         for g in range(1, H):
             nc.sync.dma_start(out=k_mx[g * ROWS : (g + 1) * ROWS, :], in_=k_mx[live, :])
         with nc.allow_non_contiguous_dma(reason="one sink a query row"):
             nc.sync.dma_start(out=sink_sb[:], in_=sink.rearrange("h (c p) o -> p (h c o)", p=QT))
-        quantize_q(2)
+        round_q(2)
         round_q(3)
-        round_q(0)
+        quantize_q(2)
         quantize_q(3)
+        round_q(0)
+        round_q(1)
         quantize_q(0)
+        quantize_q(1)
         nc.vector.scalar_tensor_tensor(
             out=v_bf[:],
             in0=v_raw[:].rearrange("p j e -> p e j"),
@@ -282,22 +288,15 @@ def tile_rows_sink_cap_gqa_kernel(tc, qT, kT, t, v, sink, out):
             op0=ALU.mult,
             op1=ALU.mult,
         )
-        round_q(1)
-        nc.vector.quantize_mx(
-            out=v_codes[:].bitcast(FP8X4), scales=v_scales[:], in_=v_bf[:].rearrange("p e j -> p (e j)")
-        )
-        quantize_q(1)
 
-        for half in range(2):
-            for r in (2 * half, 2 * half + 1):
-                for c in range(2):
-                    score_pass(0, c, r)
-                cap_first(r)
-            for r in (2 * half, 2 * half + 1):
-                weigh(0, r)
-        scores(1, 0)
-        scores(1, 1)
-        cap(1, 0)
+        for i in range(2):
+            for half in range(2):
+                for r in (2 * half, 2 * half + 1):
+                    for h, c in GROUPS[i]:
+                        score_pass(h, c, r)
+                    cap_first(i, r)
+                for r in (2 * half, 2 * half + 1):
+                    weigh(i, r)
 
         def after_weights(i):
             interleave(i, 0)
@@ -306,17 +305,28 @@ def tile_rows_sink_cap_gqa_kernel(tc, qT, kT, t, v, sink, out):
             interleave(i, 1)
             if i > 0:
                 divide(i - 1)
+            if i == 0:
+                nc.vector.quantize_mx(
+                    out=v_codes[:].bitcast(FP8X4), scales=v_scales[:], in_=v_bf[:].rearrange("p e j -> p (e j)")
+                )
             quantize_w(i, 0)
             quantize_w(i, 1)
 
-        scores(2, 0)
         after_weights(0)
+        scores(2, 0)
+        values(0, 0)
+        values(0, 1)
+        add_sink(0)
+        after_weights(1)
+        scores(2, 1)
+        cap(2, 0)
+        scores(3, 0)
         pairs = last - 2
-        for i in range(1, pairs):
+        for i in range(2, pairs):
             cap(i, 1)
             if i + 1 < pairs:
-                scores(i + 1, 1)
                 cap(i + 1, 0)
+                scores(i + 1, 1)
                 scores(i + 2, 0)
             else:
                 scores(i + 2, 0)

@@ -314,13 +314,13 @@ def tile_rows_sink_cap_gqa_kernel(tc, qT, kT, t, v, sink, out):
 
         after_weights(0)
         scores(2, 0)
+        scores(2, 1)
+        scores(3, 0)
         values(0, 0)
         values(0, 1)
         add_sink(0)
         after_weights(1)
-        scores(2, 1)
         cap(2, 0)
-        scores(3, 0)
         pairs = last - 2
         for i in range(2, pairs):
             cap(i, 1)

@@ -245,7 +245,6 @@ def tile_rows_sink_cap_gqa_kernel(tc, qT, kT, t, v, sink, out):
         nc.sync.dma_start(out=q_raw[1][:], in_=q_src[:, :, 256:512])
         for rows in (slice(ROWS, 3 * ROWS), slice(3 * ROWS, P)):
             nc.sync.dma_start(out=q_raw[0][rows], in_=q_src[rows, :, 0:256])
-        nc.sync.dma_start(out=v_raw[:], in_=v[0].rearrange("(p j) e -> p j e", j=PACK))
 
         nc.vector.memset(k_mx[live, N:], 0)
         nc.vector.scalar_tensor_tensor(
@@ -270,6 +269,7 @@ def tile_rows_sink_cap_gqa_kernel(tc, qT, kT, t, v, sink, out):
         quantize_k(3)
         for g in range(1, H):
             nc.sync.dma_start(out=k_mx[g * ROWS : (g + 1) * ROWS, :], in_=k_mx[live, :])
+        nc.sync.dma_start(out=v_raw[:], in_=v[0].rearrange("(p j) e -> p j e", j=PACK))
         with nc.allow_non_contiguous_dma(reason="one sink a query row"):
             nc.sync.dma_start(out=sink_sb[:], in_=sink.rearrange("h (c p) o -> p (h c o)", p=QT))
         round_q(2)
@@ -280,14 +280,6 @@ def tile_rows_sink_cap_gqa_kernel(tc, qT, kT, t, v, sink, out):
         round_q(1)
         quantize_q(0)
         quantize_q(1)
-        nc.vector.scalar_tensor_tensor(
-            out=v_bf[:],
-            in0=v_raw[:].rearrange("p j e -> p e j"),
-            scalar=2.0,
-            in1=t_half_sign[:].unsqueeze(1).to_broadcast([P, D, PACK]),
-            op0=ALU.mult,
-            op1=ALU.mult,
-        )
 
         for i in range(2):
             for half in range(2):
@@ -305,14 +297,21 @@ def tile_rows_sink_cap_gqa_kernel(tc, qT, kT, t, v, sink, out):
             interleave(i, 1)
             if i > 0:
                 divide(i - 1)
-            if i == 0:
-                nc.vector.quantize_mx(
-                    out=v_codes[:].bitcast(FP8X4), scales=v_scales[:], in_=v_bf[:].rearrange("p e j -> p (e j)")
-                )
             quantize_w(i, 0)
             quantize_w(i, 1)
 
         after_weights(0)
+        nc.vector.scalar_tensor_tensor(
+            out=v_bf[:],
+            in0=v_raw[:].rearrange("p j e -> p e j"),
+            scalar=2.0,
+            in1=t_half_sign[:].unsqueeze(1).to_broadcast([P, D, PACK]),
+            op0=ALU.mult,
+            op1=ALU.mult,
+        )
+        nc.vector.quantize_mx(
+            out=v_codes[:].bitcast(FP8X4), scales=v_scales[:], in_=v_bf[:].rearrange("p e j -> p (e j)")
+        )
         scores(2, 0)
         scores(2, 1)
         scores(3, 0)

@@ -89,10 +89,10 @@ def tile_rows_sink_cap_gqa_kernel(tc, qT, kT, t, v, sink, out):
         k_codes = k_mx[:, 0:N]
         k_scales = k_mx[:, N:].bitcast(U8)
 
-        def round_q(c, first=False):
+        def round_q(c, first=False, copy=nc.vector.tensor_copy):
             rows = live if first else slice(0, P)
             src = q_raw[c // 2][rows, :, (c % 2) * QT : (c % 2 + 1) * QT]
-            nc.vector.tensor_copy(out=q_bf[c + CHUNKS * first][rows], in_=src.rearrange("p j q -> p q j"))
+            copy(out=q_bf[c + CHUNKS * first][rows], in_=src.rearrange("p j q -> p q j"))
 
         def quantize_q(c, first=False):
             rows = live if first else slice(0, P)
@@ -255,13 +255,13 @@ def tile_rows_sink_cap_gqa_kernel(tc, qT, kT, t, v, sink, out):
         )
         nc.scalar.activation(out=t_ln[:], in_=t_abs[:], func=ACT.Ln)
 
-        for c in range(2):
-            round_q(c, True)
-        for c in range(2):
-            quantize_q(c, True)
+        round_q(0, True)
+        round_q(1, True, nc.scalar.copy)
+        quantize_q(0, True)
         round_k(0, 0)
-        round_k(0, 1)
         round_k(1, 0)
+        round_k(0, 1)
+        quantize_q(1, True)
         quantize_k(0)
         quantize_k(1)
         round_k(1, 1)
@@ -351,9 +351,9 @@ def tile_rows_sink_cap_gqa_kernel(tc, qT, kT, t, v, sink, out):
         values(a - 1, 0)
         values(a - 1, 1)
         interleave(a, 0)
+        add_ln(b, 1)
         quantize_w(a, 0)
         values(a, 0)
-        add_ln(b, 1)
         add_ln(d, 0)
         weigh_interleaved(b, 1)
         weigh_interleaved(d, 0, 0, half)

@@ -82,8 +82,6 @@ def tile_rows_sink_cap_gqa_kernel(tc, qT, kT, t, v, sink, out):
         last = len(GROUPS) - 1
 
         def y_of(i):
-            if i == last:
-                return y_banks[(i - 2) % 3][:, 1:]
             return y_banks[i % 3]
 
         k_codes = k_mx[:, 0:N]
@@ -355,23 +353,23 @@ def tile_rows_sink_cap_gqa_kernel(tc, qT, kT, t, v, sink, out):
         quantize_w(a, 0)
         values(a, 0)
         add_ln(d, 0)
+        add_sink(a - 1)
         weigh_interleaved(b, 1)
         weigh_interleaved(d, 0, 0, half)
         weigh_interleaved(d, 0, half, QT)
-        add_sink(a - 1)
-        add_sink(a)
         interleave(b, 0)
         invert(a - 1)
         divide_on_scalar(a - 1)
-        invert(a)
+        add_sink(a)
         quantize_w(b, 1)
         values(b, 1)
         quantize_w(b, 0)
         values(b, 0)
-        divide(a)
         quantize_w(d, 0, 0, half)
+        invert(a)
         quantize_w(d, 0, half, QT)
         values(d, 0)
+        divide_on_scalar(a)
         add_sink(b)
         invert(b)
         divide_on_scalar(b, nc.scalar)

@@ -328,7 +328,6 @@ def tile_rows_sink_cap_gqa_kernel(tc, qT, kT, t, v, sink, out):
             else:
                 scores(i + 2, 0)
                 cap(i + 1, 0)
-                scores(last, 0)
             values(i - 1, 0)
             values(i - 1, 1)
             add_sink(i - 1)
@@ -339,6 +338,7 @@ def tile_rows_sink_cap_gqa_kernel(tc, qT, kT, t, v, sink, out):
         half = QT // 2
         a, b, d = range(pairs, last + 1)
         scores(b, 1)
+        scores(d, 0)
         cap(b, 0)
         for r in range(PACK):
             weigh(a, r, 0, 1)
@@ -372,7 +372,7 @@ def tile_rows_sink_cap_gqa_kernel(tc, qT, kT, t, v, sink, out):
         divide_on_scalar(a)
         add_sink(b)
         invert(b)
-        divide_on_scalar(b, nc.scalar)
+        divide_on_scalar(b)
         add_sink(d)
         invert(d)
         divide(d)

@@ -90,7 +90,10 @@ def tile_rows_sink_cap_gqa_kernel(tc, qT, kT, t, v, sink, out):
         def round_q(c, first=False, copy=nc.vector.tensor_copy):
             rows = live if first else slice(0, P)
             src = q_raw[c // 2][rows, :, (c % 2) * QT : (c % 2 + 1) * QT]
-            copy(out=q_bf[c + CHUNKS * first][rows], in_=src.rearrange("p j q -> p q j"))
+            copy(
+                out=q_bf[c + CHUNKS * first][rows].rearrange("p (c i) j -> p c j i", i=4),
+                in_=src.rearrange("p j (c i) -> p c j i", i=4),
+            )
 
         def quantize_q(c, first=False):
             rows = live if first else slice(0, P)
@@ -184,7 +187,10 @@ def tile_rows_sink_cap_gqa_kernel(tc, qT, kT, t, v, sink, out):
             nc.scalar.activation(out=w_bf[i][:, n, q0:q1, :], in_=logits[last - i][:, q0:q1, :], func=ACT.Exp)
 
         def interleave(i, n):
-            nc.vector.tensor_copy(out=w_bf[i][:, n], in_=w_rows[i][:, n].rearrange("p r q -> p q r"))
+            nc.vector.tensor_copy(
+                out=w_bf[i][:, n].rearrange("p (c i) r -> p c r i", i=4),
+                in_=w_rows[i][:, n].rearrange("p r (c i) -> p c r i", i=4),
+            )
 
         def quantize_w(i, n, q0=0, q1=QT):
             nc.vector.quantize_mx(

@@ -24,10 +24,10 @@ GROUPS = [
     [(0, 2), (0, 3)],
     [(1, 0), (2, 0)],
     [(3, 0), (1, 1)],
-    [(2, 1), (3, 1)],
-    [(1, 2), (2, 2)],
-    [(3, 2)],
-    [(1, 3), (2, 3)],
+    [(2, 1), (1, 2)],
+    [(2, 2), (1, 3)],
+    [(3, 1), (3, 2)],
+    [(2, 3)],
     [(3, 3)],
 ]
 
@@ -71,7 +71,7 @@ def tile_rows_sink_cap_gqa_kernel(tc, qT, kT, t, v, sink, out):
         w_bf = per_group("w_bf", [QT, PACK], BF16)
         w_codes = per_group("w_codes", [QT], I32)
         w_scales = per_group("w_scales", [QT], U8)
-        logits = [sb.tile([P, QT, PACK], F32, name="logits%d" % i) for i in range(2)]
+        logits = [sb.tile([P, len(g), QT, PACK], F32, name="logits%d" % i) for i, g in enumerate(GROUPS[-3:])]
         den = per_group("den", [], F32)
         rec = per_group("rec", [], F32)
         res = per_group("res", [D], F32)
@@ -175,7 +175,7 @@ def tile_rows_sink_cap_gqa_kernel(tc, qT, kT, t, v, sink, out):
 
         def add_ln(i, n):
             nc.vector.scalar_tensor_tensor(
-                out=logits[last - i][:],
+                out=logits[i - last - 1][:, n],
                 in0=in_word_order(i, n),
                 scalar=CAP,
                 in1=t_ln[:].unsqueeze(1).to_broadcast([P, QT, PACK]),
@@ -184,7 +184,7 @@ def tile_rows_sink_cap_gqa_kernel(tc, qT, kT, t, v, sink, out):
             )
 
         def weigh_interleaved(i, n, q0=0, q1=QT):
-            nc.scalar.activation(out=w_bf[i][:, n, q0:q1, :], in_=logits[last - i][:, q0:q1, :], func=ACT.Exp)
+            nc.scalar.activation(out=w_bf[i][:, n, q0:q1, :], in_=logits[i - last - 1][:, n, q0:q1, :], func=ACT.Exp)
 
         def interleave(i, n):
             nc.vector.tensor_copy(
@@ -324,57 +324,65 @@ def tile_rows_sink_cap_gqa_kernel(tc, qT, kT, t, v, sink, out):
         add_sink(0)
         after_weights(1)
         cap(2, 0)
-        pairs = last - 2
-        for i in range(2, pairs):
+        half = QT // 2
+        a, b, d = range(last - 2, last + 1)
+        late = {3: (a, 0), 4: (a, 1), 5: (b, 0)}
+        for i in range(2, a):
             cap(i, 1)
-            if i + 1 < pairs:
+            if i + 1 < a:
                 cap(i + 1, 0)
-                scores(i + 1, 1)
-                scores(i + 2, 0)
-            else:
-                scores(i + 2, 0)
-                cap(i + 1, 0)
+            if i in late:
+                cap_interleaved(*late[i])
+            ahead = [(i + 1, 1), (i + 2, 0), late.get(i + 1, (d, 0))]
+            ahead = [unit for unit in ahead[:2] if unit[0] < a] + ahead[2:]
+            for unit in ahead[:2]:
+                scores(*unit)
             values(i - 1, 0)
             values(i - 1, 1)
+            for unit in ahead[2:]:
+                scores(*unit)
+            if i in late:
+                add_ln(*late[i])
             add_sink(i - 1)
             for r in range(PACK):
                 weigh(i, r)
-            after_weights(i)
+            if i + 2 < a:
+                after_weights(i)
+            elif i + 2 == a:
+                for n in range(2):
+                    interleave(i, n)
+                quantize_w(i, 0)
+                invert(i - 1)
+                quantize_w(i, 1)
+                divide(i - 1)
 
-        half = QT // 2
-        a, b, d = range(pairs, last + 1)
-        scores(b, 1)
-        scores(d, 0)
-        cap(b, 0)
-        for r in range(PACK):
-            weigh(a, r, 0, 1)
-        cap_interleaved(b, 1)
         cap_interleaved(d, 0)
-        for r in range(PACK):
-            weigh(b, r, 0, 1)
-        values(a - 1, 0)
-        values(a - 1, 1)
-        interleave(a, 0)
-        add_ln(b, 1)
-        quantize_w(a, 0)
-        values(a, 0)
+        invert(a - 2)
+        for n in range(2):
+            interleave(a - 1, n)
+        for n in range(2):
+            quantize_w(a - 1, n)
+            values(a - 1, n)
         add_ln(d, 0)
-        add_sink(a - 1)
-        weigh_interleaved(b, 1)
+        weigh_interleaved(a, 0)
+        weigh_interleaved(a, 1)
+        weigh_interleaved(b, 0)
         weigh_interleaved(d, 0, 0, half)
         weigh_interleaved(d, 0, half, QT)
-        interleave(b, 0)
+        for n in range(2):
+            quantize_w(a, n)
+            values(a, n)
+        add_sink(a - 1)
+        divide(a - 2)
         invert(a - 1)
         divide_on_scalar(a - 1)
-        add_sink(a)
-        quantize_w(b, 1)
-        values(b, 1)
         quantize_w(b, 0)
         values(b, 0)
         quantize_w(d, 0, 0, half)
-        invert(a)
+        add_sink(a)
         quantize_w(d, 0, half, QT)
         values(d, 0)
+        invert(a)
         divide_on_scalar(a)
         add_sink(b)
         invert(b)

@@ -210,6 +210,18 @@ def tile_rows_sink_cap_gqa_kernel(tc, qT, kT, t, v, sink, out):
                 stop=True,
             )
 
+        def keep_busy(i, passes):
+            for rep in range(passes):
+                nc.tensor.matmul_mx(
+                    out=y_of(i + 2)[:, PACK - 1, :],
+                    lhsT=w_codes[i][:, 0, :].bitcast(FP8X4),
+                    lhsT_scale=w_scales[i][:, 0, :],
+                    rhs=v_codes[:].bitcast(FP8X4),
+                    rhs_scale=v_scales[:],
+                    start=True,
+                    stop=True,
+                )
+
         def places(i):
             first, final = [CHUNKS * h + c for h, c in (min(GROUPS[i]), max(GROUPS[i]))]
             return slice(first, final + 1, max(final - first, 1))
@@ -341,6 +353,8 @@ def tile_rows_sink_cap_gqa_kernel(tc, qT, kT, t, v, sink, out):
             values(i - 1, 1)
             for unit in ahead[2:]:
                 scores(*unit)
+            if i + 1 == a:
+                keep_busy(i - 1, 10)
             if i in late:
                 add_ln(*late[i])
             add_sink(i - 1)
@@ -363,6 +377,7 @@ def tile_rows_sink_cap_gqa_kernel(tc, qT, kT, t, v, sink, out):
         for n in range(2):
             quantize_w(a - 1, n)
             values(a - 1, n)
+        keep_busy(a - 2, 4)
         add_ln(d, 0)
         weigh_interleaved(a, 0)
         weigh_interleaved(a, 1)

@@ -56,6 +56,9 @@ def tile_rows_sink_cap_gqa_kernel(tc, qT, kT, t, v, sink, out):
         q_scales = [sb.tile([P, QT], U8, align_bytes=64, name="q_scales%d" % c) for c in range(CHUNKS + 2)]
         k_bf = [sb.tile([ROWS, 2, P, PACK], BF16, align_bytes=64, name="k_bf%d" % i) for i in range(2)]
         k_mx = sb.tile([P, N + N // PACK], I32, align_bytes=64)
+        warm_bf = sb.tile([P, QT * PACK], BF16, align_bytes=64)
+        warm_codes = sb.tile([P, QT], I32, align_bytes=64)
+        warm_scales = sb.tile([P, QT], U8, align_bytes=64)
         v_bf = sb.tile([P, D, PACK], BF16, align_bytes=64)
         v_codes = sb.tile([P, D], I32, align_bytes=64)
         v_scales = sb.tile([P, D], U8, align_bytes=64)
@@ -222,6 +225,18 @@ def tile_rows_sink_cap_gqa_kernel(tc, qT, kT, t, v, sink, out):
                     stop=True,
                 )
 
+        def warm(passes):
+            for rep in range(passes):
+                nc.tensor.matmul_mx(
+                    out=y_banks[2][:, PACK - 1, :],
+                    lhsT=warm_codes[:].bitcast(FP8X4),
+                    lhsT_scale=warm_scales[:],
+                    rhs=warm_codes[:].bitcast(FP8X4),
+                    rhs_scale=warm_scales[:],
+                    start=True,
+                    stop=True,
+                )
+
         def places(i):
             first, final = [CHUNKS * h + c for h, c in (min(GROUPS[i]), max(GROUPS[i]))]
             return slice(first, final + 1, max(final - first, 1))
@@ -262,7 +277,10 @@ def tile_rows_sink_cap_gqa_kernel(tc, qT, kT, t, v, sink, out):
         for rows in (slice(ROWS, 3 * ROWS), slice(3 * ROWS, P)):
             nc.sync.dma_start(out=q_raw[0][rows], in_=q_src[rows, :, 0:256])
 
+        nc.vector.memset(warm_bf[:].bitcast(I32), 0)
         nc.vector.memset(k_mx[live, N:], 0)
+        nc.vector.quantize_mx(out=warm_codes[:].bitcast(FP8X4), scales=warm_scales[:], in_=warm_bf[:])
+        warm(22)
         nc.vector.scalar_tensor_tensor(
             out=t_abs[:], in0=t_sb[:], scalar=-1.0, in1=t_sb[:], op0=ALU.mult, op1=ALU.max
         )
@@ -303,6 +321,8 @@ def tile_rows_sink_cap_gqa_kernel(tc, qT, kT, t, v, sink, out):
                     for h, c in GROUPS[i]:
                         score_pass(h, c, r)
                     cap_first(i, r)
+                if 2 * i + half < 3:
+                    warm(4)
                 for r in (2 * half, 2 * half + 1):
                     weigh(i, r)
 

@@ -48,6 +48,7 @@ def tile_rows_sink_cap_gqa_kernel(tc, qT, kT, t, v, sink, out):
         t_sb = sb.tile([P, PACK], F32)
         t_abs = sb.tile([P, PACK], F32)
         t_ln = sb.tile([P, PACK], F32)
+        t_warm = sb.tile([P, PACK], F32)
         t_half_sign = sb.tile([P, PACK], F32)
         sink_sb = sb.tile([P, H * CHUNKS], F32)
 
@@ -107,10 +108,10 @@ def tile_rows_sink_cap_gqa_kernel(tc, qT, kT, t, v, sink, out):
                 in_=q_bf[i][rows].rearrange("p q j -> p (q j)"),
             )
 
-        def round_k(i, half):
+        def round_k(i, half, copy=nc.vector.tensor_copy):
             src = k_raw[half][:].rearrange("p j (s r) -> p s j r", r=PACK)[:, :, :, 2 * i : 2 * i + 2]
             dst = k_bf[i][:, :, half * P // 2 : (half + 1) * P // 2, :]
-            nc.vector.tensor_copy(out=dst.rearrange("p r s j -> p s j r"), in_=src)
+            copy(out=dst.rearrange("p r s j -> p s j r"), in_=src)
 
         def quantize_k(r):
             cols = slice(r * P, (r + 1) * P)
@@ -280,7 +281,7 @@ def tile_rows_sink_cap_gqa_kernel(tc, qT, kT, t, v, sink, out):
         nc.vector.memset(warm_bf[:].bitcast(I32), 0)
         nc.vector.memset(k_mx[live, N:], 0)
         nc.vector.quantize_mx(out=warm_codes[:].bitcast(FP8X4), scales=warm_scales[:], in_=warm_bf[:])
-        warm(22)
+        warm(20)
         nc.vector.scalar_tensor_tensor(
             out=t_abs[:], in0=t_sb[:], scalar=-1.0, in1=t_sb[:], op0=ALU.mult, op1=ALU.max
         )
@@ -289,13 +290,15 @@ def tile_rows_sink_cap_gqa_kernel(tc, qT, kT, t, v, sink, out):
         )
         nc.scalar.activation(out=t_ln[:], in_=t_abs[:], func=ACT.Ln)
 
+        nc.scalar.activation(out=t_warm[:], in_=t_abs[:], func=ACT.Tanh)
+
         round_q(0, True)
-        round_q(1, True, nc.scalar.copy)
+        round_q(1, True)
         quantize_q(0, True)
         round_k(0, 0)
-        round_k(1, 0)
-        round_k(0, 1)
+        round_k(1, 0, nc.scalar.copy)
         quantize_q(1, True)
+        round_k(0, 1)
         quantize_k(0)
         quantize_k(1)
         round_k(1, 1)
@@ -321,8 +324,6 @@ def tile_rows_sink_cap_gqa_kernel(tc, qT, kT, t, v, sink, out):
                     for h, c in GROUPS[i]:
                         score_pass(h, c, r)
                     cap_first(i, r)
-                if 2 * i + half < 3:
-                    warm(4)
                 for r in (2 * half, 2 * half + 1):
                     weigh(i, r)
 

@@ -22,13 +22,13 @@ CHUNKS = NQ // QT
 GROUPS = [
     [(0, 0), (0, 1)],
     [(0, 2), (0, 3)],
-    [(1, 0), (2, 0)],
-    [(3, 0), (1, 1)],
-    [(2, 1), (1, 2)],
-    [(2, 2), (1, 3)],
-    [(3, 1), (3, 2)],
-    [(2, 3)],
-    [(3, 3)],
+    [(2, 2), (3, 2)],
+    [(1, 2), (2, 3)],
+    [(3, 3), (2, 0)],
+    [(3, 0), (2, 1)],
+    [(1, 3), (1, 0)],
+    [(3, 1)],
+    [(1, 1)],
 ]
 
 
@@ -275,8 +275,7 @@ def tile_rows_sink_cap_gqa_kernel(tc, qT, kT, t, v, sink, out):
         for half in range(2):
             nc.sync.dma_start(out=k_raw[half][:], in_=k_src[:, :, half * N // 2 : (half + 1) * N // 2])
         nc.sync.dma_start(out=q_raw[1][:], in_=q_src[:, :, 256:512])
-        for rows in (slice(ROWS, 3 * ROWS), slice(3 * ROWS, P)):
-            nc.sync.dma_start(out=q_raw[0][rows], in_=q_src[rows, :, 0:256])
+        nc.sync.dma_start(out=v_raw[:], in_=v[0].rearrange("(p j) e -> p j e", j=PACK))
 
         nc.vector.memset(warm_bf[:].bitcast(I32), 0)
         nc.vector.memset(k_mx[live, N:], 0)
@@ -299,24 +298,32 @@ def tile_rows_sink_cap_gqa_kernel(tc, qT, kT, t, v, sink, out):
         round_k(1, 0, nc.scalar.copy)
         quantize_q(1, True)
         round_k(0, 1)
+        round_k(1, 1)
         quantize_k(0)
         quantize_k(1)
-        round_k(1, 1)
         quantize_k(2)
         quantize_k(3)
-        for g in range(1, H):
+        for g in (2, 3, 1):
             nc.sync.dma_start(out=k_mx[g * ROWS : (g + 1) * ROWS, :], in_=k_mx[live, :])
-        nc.sync.dma_start(out=v_raw[:], in_=v[0].rearrange("(p j) e -> p j e", j=PACK))
         with nc.allow_non_contiguous_dma(reason="one sink a query row"):
             nc.sync.dma_start(out=sink_sb[:], in_=sink.rearrange("h (c p) o -> p (h c o)", p=QT))
+        for rows in (slice(ROWS, 3 * ROWS), slice(3 * ROWS, P)):
+            nc.sync.dma_start(out=q_raw[0][rows], in_=q_src[rows, :, 0:256])
         round_q(2)
         round_q(3)
         quantize_q(2)
         quantize_q(3)
-        round_q(0)
-        round_q(1)
-        quantize_q(0)
-        quantize_q(1)
+        nc.vector.scalar_tensor_tensor(
+            out=v_bf[:],
+            in0=v_raw[:].rearrange("p j e -> p e j"),
+            scalar=2.0,
+            in1=t_half_sign[:].unsqueeze(1).to_broadcast([P, D, PACK]),
+            op0=ALU.mult,
+            op1=ALU.mult,
+        )
+        nc.vector.quantize_mx(
+            out=v_codes[:].bitcast(FP8X4), scales=v_scales[:], in_=v_bf[:].rearrange("p e j -> p (e j)")
+        )
 
         for i in range(2):
             for half in range(2):
@@ -338,17 +345,6 @@ def tile_rows_sink_cap_gqa_kernel(tc, qT, kT, t, v, sink, out):
             quantize_w(i, 1)
 
         after_weights(0)
-        nc.vector.scalar_tensor_tensor(
-            out=v_bf[:],
-            in0=v_raw[:].rearrange("p j e -> p e j"),
-            scalar=2.0,
-            in1=t_half_sign[:].unsqueeze(1).to_broadcast([P, D, PACK]),
-            op0=ALU.mult,
-            op1=ALU.mult,
-        )
-        nc.vector.quantize_mx(
-            out=v_codes[:].bitcast(FP8X4), scales=v_scales[:], in_=v_bf[:].rearrange("p e j -> p (e j)")
-        )
         scores(2, 0)
         scores(2, 1)
         scores(3, 0)
@@ -356,6 +352,10 @@ def tile_rows_sink_cap_gqa_kernel(tc, qT, kT, t, v, sink, out):
         values(0, 1)
         add_sink(0)
         after_weights(1)
+        round_q(0)
+        round_q(1)
+        quantize_q(0)
+        quantize_q(1)
         cap(2, 0)
         half = QT // 2
         a, b, d = range(last - 2, last + 1)

@@ -19,16 +19,9 @@ PACK = 4
 ROWS = D // PACK
 QT = 128
 CHUNKS = NQ // QT
-GROUPS = [
-    [(0, 0), (0, 1)],
-    [(0, 2), (0, 3)],
-    [(2, 2), (3, 2)],
-    [(1, 2), (2, 3)],
-    [(3, 3), (2, 0)],
-    [(3, 0), (2, 1)],
-    [(1, 3), (1, 0)],
-    [(3, 1)],
-    [(1, 1)],
+LATER = [(h, c) for c in (2, 3, 0, 1) for h in (2, 3, 1)]
+GROUPS = [[(0, 0), (0, 1)], [(0, 2), (0, 3)]] + [
+    [LATER[u] for u in units] for units in ((0, 1), (3, 4), (6, 7), (5, 8), (2, 9), (10,), (11,))
 ]
 
 
@@ -75,7 +68,7 @@ def tile_rows_sink_cap_gqa_kernel(tc, qT, kT, t, v, sink, out):
         w_bf = per_group("w_bf", [QT, PACK], BF16)
         w_codes = per_group("w_codes", [QT], I32)
         w_scales = per_group("w_scales", [QT], U8)
-        logits = [sb.tile([P, len(g), QT, PACK], F32, name="logits%d" % i) for i, g in enumerate(GROUPS[-3:])]
+        logits = [sb.tile([P, len(g), QT, PACK], F32, name="logits%d" % i) for i, g in enumerate(GROUPS)]
         den = per_group("den", [], F32)
         rec = per_group("rec", [], F32)
         res = per_group("res", [D], F32)
@@ -179,7 +172,7 @@ def tile_rows_sink_cap_gqa_kernel(tc, qT, kT, t, v, sink, out):
 
         def add_ln(i, n):
             nc.vector.scalar_tensor_tensor(
-                out=logits[i - last - 1][:, n],
+                out=logits[i][:, n],
                 in0=in_word_order(i, n),
                 scalar=CAP,
                 in1=t_ln[:].unsqueeze(1).to_broadcast([P, QT, PACK]),
@@ -188,7 +181,10 @@ def tile_rows_sink_cap_gqa_kernel(tc, qT, kT, t, v, sink, out):
             )
 
         def weigh_interleaved(i, n, q0=0, q1=QT):
-            nc.scalar.activation(out=w_bf[i][:, n, q0:q1, :], in_=logits[i - last - 1][:, n, q0:q1, :], func=ACT.Exp)
+            nc.scalar.activation(out=w_bf[i][:, n, q0:q1, :], in_=logits[i][:, n, q0:q1, :], func=ACT.Exp)
+
+        def weigh_group(i):
+            nc.scalar.activation(out=w_bf[i][:], in_=logits[i][:], func=ACT.Exp)
 
         def interleave(i, n):
             nc.vector.tensor_copy(
@@ -214,10 +210,10 @@ def tile_rows_sink_cap_gqa_kernel(tc, qT, kT, t, v, sink, out):
                 stop=True,
             )
 
-        def keep_busy(i, passes):
+        def keep_busy(i, bank, passes):
             for rep in range(passes):
                 nc.tensor.matmul_mx(
-                    out=y_of(i + 2)[:, PACK - 1, :],
+                    out=y_banks[bank][:, PACK - 1, :],
                     lhsT=w_codes[i][:, 0, :].bitcast(FP8X4),
                     lhsT_scale=w_scales[i][:, 0, :],
                     rhs=v_codes[:].bitcast(FP8X4),
@@ -344,76 +340,79 @@ def tile_rows_sink_cap_gqa_kernel(tc, qT, kT, t, v, sink, out):
             quantize_w(i, 0)
             quantize_w(i, 1)
 
+        where = {unit: (i, n) for i, g in enumerate(GROUPS) for n, unit in enumerate(g)}
+        later = [where[unit] for unit in LATER]
+        half = QT // 2
+        e, a, b, d = range(last - 3, last + 1)
+
+        def cap_and_refill(u):
+            (cap if later[u][0] < e else cap_interleaved)(*later[u])
+            if u + 3 < len(later):
+                scores(*later[u + 3])
+
         after_weights(0)
-        scores(2, 0)
-        scores(2, 1)
-        scores(3, 0)
+        scores(*later[0])
+        scores(*later[1])
         values(0, 0)
         values(0, 1)
+        scores(*later[2])
         add_sink(0)
         after_weights(1)
         round_q(0)
         round_q(1)
-        quantize_q(0)
-        quantize_q(1)
-        cap(2, 0)
-        half = QT // 2
-        a, b, d = range(last - 2, last + 1)
-        late = {3: (a, 0), 4: (a, 1), 5: (b, 0)}
-        for i in range(2, a):
-            cap(i, 1)
-            if i + 1 < a:
-                cap(i + 1, 0)
-            if i in late:
-                cap_interleaved(*late[i])
-            ahead = [(i + 1, 1), (i + 2, 0), late.get(i + 1, (d, 0))]
-            ahead = [unit for unit in ahead[:2] if unit[0] < a] + ahead[2:]
-            for unit in ahead[:2]:
-                scores(*unit)
+        for i in range(2, e):
+            u = 3 * (i - 2)
+            cap_and_refill(u)
+            cap_and_refill(u + 1)
             values(i - 1, 0)
             values(i - 1, 1)
-            for unit in ahead[2:]:
-                scores(*unit)
-            if i + 1 == a:
-                keep_busy(i - 1, 10)
-            if i in late:
-                add_ln(*late[i])
+            if i == 2:
+                quantize_q(0)
+                quantize_q(1)
+            cap_and_refill(u + 2)
+            add_ln(*later[u + 2])
             add_sink(i - 1)
-            for r in range(PACK):
-                weigh(i, r)
-            if i + 2 < a:
-                after_weights(i)
-            elif i + 2 == a:
-                for n in range(2):
-                    interleave(i, n)
-                quantize_w(i, 0)
-                invert(i - 1)
-                quantize_w(i, 1)
-                divide(i - 1)
+            weigh(i, 0)
+            weigh(i, 1)
+            if i + 1 == e:
+                cap_and_refill(u + 3)
+                add_ln(*later[u + 3])
+            weigh(i, 2)
+            weigh(i, 3)
+            after_weights(i)
 
+        cap_interleaved(b, 0)
+        weigh_group(e)
         cap_interleaved(d, 0)
-        invert(a - 2)
-        for n in range(2):
-            interleave(a - 1, n)
-        for n in range(2):
-            quantize_w(a - 1, n)
-            values(a - 1, n)
-        keep_busy(a - 2, 4)
+        values(e - 1, 0)
+        values(e - 1, 1)
+        keep_busy(e - 1, 0, 5)
+        add_ln(b, 0)
+        quantize_w(e, 0)
+        values(e, 0)
+        quantize_w(e, 1)
+        values(e, 1)
+        keep_busy(e, 0, 4)
+        add_sink(e - 1)
         add_ln(d, 0)
         weigh_interleaved(a, 0)
         weigh_interleaved(a, 1)
         weigh_interleaved(b, 0)
         weigh_interleaved(d, 0, 0, half)
         weigh_interleaved(d, 0, half, QT)
-        for n in range(2):
-            quantize_w(a, n)
-            values(a, n)
-        add_sink(a - 1)
-        divide(a - 2)
-        invert(a - 1)
-        divide_on_scalar(a - 1)
+        invert(e - 1)
+        quantize_w(a, 0)
+        values(a, 0)
+        keep_busy(e, 0, 1)
+        add_sink(e)
+        quantize_w(a, 1)
+        values(a, 1)
+        divide(e - 1)
+        keep_busy(e, 1, 4)
+        invert(e)
         quantize_w(b, 0)
         values(b, 0)
+        divide_on_scalar(e)
         quantize_w(d, 0, 0, half)
         add_sink(a)
         quantize_w(d, 0, half, QT)

@@ -353,12 +353,17 @@ def tile_rows_sink_cap_gqa_kernel(tc, qT, kT, t, v, sink, out):
         after_weights(0)
         scores(*later[0])
         scores(*later[1])
+        scores(*later[2])
         values(0, 0)
         values(0, 1)
-        scores(*later[2])
+        interleave(1, 0)
+        interleave(1, 1)
         add_sink(0)
-        after_weights(1)
+        quantize_w(1, 0)
+        invert(0)
+        quantize_w(1, 1)
         round_q(0)
+        divide(0)
         round_q(1)
         for i in range(2, e):
             u = 3 * (i - 2)

@@ -41,8 +41,7 @@ def tile_rows_sink_cap_gqa_kernel(tc, qT, kT, t, v, sink, out):
         t_sb = sb.tile([P, PACK], F32)
         t_abs = sb.tile([P, PACK], F32)
         t_ln = sb.tile([P, PACK], F32)
-        t_warm = sb.tile([P, PACK], F32)
-        t_half_sign = sb.tile([P, PACK], F32)
+        t_sign = sb.tile([P, PACK], F32)
         sink_sb = sb.tile([P, H * CHUNKS], F32)
 
         q_bf = [sb.tile([P, QT, PACK], BF16, align_bytes=64, name="q_bf%d" % c) for c in range(CHUNKS + 2)]
@@ -276,16 +275,13 @@ def tile_rows_sink_cap_gqa_kernel(tc, qT, kT, t, v, sink, out):
         nc.vector.memset(warm_bf[:].bitcast(I32), 0)
         nc.vector.memset(k_mx[live, N:], 0)
         nc.vector.quantize_mx(out=warm_codes[:].bitcast(FP8X4), scales=warm_scales[:], in_=warm_bf[:])
-        warm(20)
+        warm(26)
         nc.vector.scalar_tensor_tensor(
             out=t_abs[:], in0=t_sb[:], scalar=-1.0, in1=t_sb[:], op0=ALU.mult, op1=ALU.max
         )
-        nc.vector.tensor_scalar(
-            out=t_half_sign[:], in0=t_sb[:], scalar1=0.0, scalar2=0.5, op0=ALU.is_ge, op1=ALU.subtract
-        )
         nc.scalar.activation(out=t_ln[:], in_=t_abs[:], func=ACT.Ln)
 
-        nc.scalar.activation(out=t_warm[:], in_=t_abs[:], func=ACT.Tanh)
+        nc.scalar.activation(out=t_sign[:], in_=t_sb[:], func=ACT.Tanh, scale=2.0**69)
 
         round_q(0, True)
         round_q(1, True)
@@ -309,13 +305,11 @@ def tile_rows_sink_cap_gqa_kernel(tc, qT, kT, t, v, sink, out):
         round_q(3)
         quantize_q(2)
         quantize_q(3)
-        nc.vector.scalar_tensor_tensor(
+        nc.vector.tensor_tensor(
             out=v_bf[:],
             in0=v_raw[:].rearrange("p j e -> p e j"),
-            scalar=2.0,
-            in1=t_half_sign[:].unsqueeze(1).to_broadcast([P, D, PACK]),
-            op0=ALU.mult,
-            op1=ALU.mult,
+            in1=t_sign[:].unsqueeze(1).to_broadcast([P, D, PACK]),
+            op=ALU.mult,
         )
         nc.vector.quantize_mx(
             out=v_codes[:].bitcast(FP8X4), scales=v_scales[:], in_=v_bf[:].rearrange("p e j -> p (e j)")
@@ -391,13 +385,13 @@ def tile_rows_sink_cap_gqa_kernel(tc, qT, kT, t, v, sink, out):
         cap_interleaved(d, 0)
         values(e - 1, 0)
         values(e - 1, 1)
-        keep_busy(e - 1, 0, 5)
+        keep_busy(e - 1, 0, 4)
         add_ln(b, 0)
         quantize_w(e, 0)
         values(e, 0)
         quantize_w(e, 1)
         values(e, 1)
-        keep_busy(e, 0, 4)
+        keep_busy(e, 0, 2)
         add_sink(e - 1)
         add_ln(d, 0)
         weigh_interleaved(a, 0)
@@ -408,12 +402,11 @@ def tile_rows_sink_cap_gqa_kernel(tc, qT, kT, t, v, sink, out):
         invert(e - 1)
         quantize_w(a, 0)
         values(a, 0)
-        keep_busy(e, 0, 1)
         add_sink(e)
         quantize_w(a, 1)
         values(a, 1)
         divide(e - 1)
-        keep_busy(e, 1, 4)
+        keep_busy(e, 1, 2)
         invert(e)
         quantize_w(b, 0)
         values(b, 0)

@@ -19,10 +19,22 @@ PACK = 4
 ROWS = D // PACK
 QT = 128
 CHUNKS = NQ // QT
-LATER = [(h, c) for c in (2, 3, 0, 1) for h in (2, 3, 1)]
-GROUPS = [[(0, 0), (0, 1)], [(0, 2), (0, 3)]] + [
-    [LATER[u] for u in units] for units in ((0, 1), (3, 4), (6, 7), (5, 8), (2, 9), (10,), (11,))
-]
+WALK = 4
+
+SATURATE = 2.0**69
+
+OTHER_HEADS = (2, 3, 1)
+TURNS = [(h, c) for c in (2, 3, 0, 1) for h in OTHER_HEADS]
+HEAD0_GROUPS = [[(0, 0), (0, 1)], [(0, 2), (0, 3)]]
+BY_PLACE = [TURNS[u : u + 2] for u in (0, 3, 6)]
+SUMMED = [[TURNS[5], TURNS[8]], [TURNS[2], TURNS[9]], [TURNS[10]], [TURNS[11]]]
+GROUPS = HEAD0_GROUPS + BY_PLACE + SUMMED
+FIRST_SUMMED = len(GROUPS) - len(SUMMED)
+Y_BANKS = 3
+
+WARM_START = 28
+WARM_LONG_GAP = 4
+WARM_SHORT_GAP = 2
 
 
 def tile_rows_sink_cap_gqa_kernel(tc, qT, kT, t, v, sink, out):
@@ -34,8 +46,7 @@ def tile_rows_sink_cap_gqa_kernel(tc, qT, kT, t, v, sink, out):
 
         q_src = qT.rearrange("h (p j) q -> (h p) j q", j=PACK)
         k_src = kT[0].rearrange("(p j) i -> p j i", j=PACK)
-        q_loads = [(0, 256), (256, 512)]
-        q_raw = [sb.tile([P, PACK, b - a], F32, name="q_raw%d" % a) for a, b in q_loads]
+        q_raw = [sb.tile([P, PACK, NQ // 2], F32, name="q_raw%d" % i) for i in range(2)]
         k_raw = [sb.tile([ROWS, PACK, N // 2], F32, name="k_raw%d" % i) for i in range(2)]
         v_raw = sb.tile([P, PACK, D], F32)
         t_sb = sb.tile([P, PACK], F32)
@@ -44,11 +55,14 @@ def tile_rows_sink_cap_gqa_kernel(tc, qT, kT, t, v, sink, out):
         t_sign = sb.tile([P, PACK], F32)
         sink_sb = sb.tile([P, H * CHUNKS], F32)
 
-        q_bf = [sb.tile([P, QT, PACK], BF16, align_bytes=64, name="q_bf%d" % c) for c in range(CHUNKS + 2)]
-        q_codes = [sb.tile([P, QT], I32, align_bytes=64, name="q_codes%d" % c) for c in range(CHUNKS + 2)]
-        q_scales = [sb.tile([P, QT], U8, align_bytes=64, name="q_scales%d" % c) for c in range(CHUNKS + 2)]
+        q_slots = range(CHUNKS + 2)
+        q_bf = [sb.tile([P, QT, PACK], BF16, align_bytes=64, name="q_bf%d" % c) for c in q_slots]
+        q_codes = [sb.tile([P, QT], I32, align_bytes=64, name="q_codes%d" % c) for c in q_slots]
+        q_scales = [sb.tile([P, QT], U8, align_bytes=64, name="q_scales%d" % c) for c in q_slots]
         k_bf = [sb.tile([ROWS, 2, P, PACK], BF16, align_bytes=64, name="k_bf%d" % i) for i in range(2)]
         k_mx = sb.tile([P, N + N // PACK], I32, align_bytes=64)
+        k_codes = k_mx[:, 0:N]
+        k_scales = k_mx[:, N:].bitcast(U8)
         warm_bf = sb.tile([P, QT * PACK], BF16, align_bytes=64)
         warm_codes = sb.tile([P, QT], I32, align_bytes=64)
         warm_scales = sb.tile([P, QT], U8, align_bytes=64)
@@ -56,140 +70,128 @@ def tile_rows_sink_cap_gqa_kernel(tc, qT, kT, t, v, sink, out):
         v_codes = sb.tile([P, D], I32, align_bytes=64)
         v_scales = sb.tile([P, D], U8, align_bytes=64)
 
-        def per_group(name, shape, dtype):
-            return [
-                sb.tile([P, len(g)] + shape, dtype, align_bytes=64, name="%s%d" % (name, i))
-                for i, g in enumerate(GROUPS)
-            ]
+        def per_group(name, shape, dtype, first=0, end=len(GROUPS)):
+            return {
+                i: sb.tile([P, len(GROUPS[i])] + shape, dtype, align_bytes=64, name="%s%d" % (name, i))
+                for i in range(first, end)
+            }
 
-        capped = per_group("capped", [PACK, QT], F32)
-        w_rows = per_group("w_rows", [PACK, QT], BF16)
+        capped_rows = per_group("capped_rows", [PACK, QT], F32, end=FIRST_SUMMED)
+        w_rows = per_group("w_rows", [PACK, QT], BF16, end=FIRST_SUMMED)
+        capped_words = per_group("capped_words", [QT, PACK], F32, first=FIRST_SUMMED)
+        logits = per_group("logits", [QT, PACK], F32, first=FIRST_SUMMED)
         w_bf = per_group("w_bf", [QT, PACK], BF16)
         w_codes = per_group("w_codes", [QT], I32)
         w_scales = per_group("w_scales", [QT], U8)
-        logits = [sb.tile([P, len(g), QT, PACK], F32, name="logits%d" % i) for i, g in enumerate(GROUPS)]
         den = per_group("den", [], F32)
         rec = per_group("rec", [], F32)
         res = per_group("res", [D], F32)
         score_banks = [ps.tile([P, PACK, QT], F32, name="score%d" % g) for g in range(H + 1)]
-        y_banks = [ps.tile([P, PACK, D], F32, name="y%d" % i) for i in range(3)]
+        y_banks = [ps.tile([P, PACK, D], F32, name="y%d" % i) for i in range(Y_BANKS)]
 
-        live = slice(0, ROWS)
-        last = len(GROUPS) - 1
+        tile0 = slice(0, ROWS)
 
-        def y_of(i):
-            return y_banks[i % 3]
-
-        k_codes = k_mx[:, 0:N]
-        k_scales = k_mx[:, N:].bitcast(U8)
-
-        def round_q(c, first=False, copy=nc.vector.tensor_copy):
-            rows = live if first else slice(0, P)
+        def round_q(c, early=False):
+            rows = tile0 if early else slice(0, P)
             src = q_raw[c // 2][rows, :, (c % 2) * QT : (c % 2 + 1) * QT]
-            copy(
-                out=q_bf[c + CHUNKS * first][rows].rearrange("p (c i) j -> p c j i", i=4),
-                in_=src.rearrange("p j (c i) -> p c j i", i=4),
+            nc.vector.tensor_copy(
+                out=q_bf[c + CHUNKS * early][rows].rearrange("p (c i) j -> p c j i", i=WALK),
+                in_=src.rearrange("p j (c i) -> p c j i", i=WALK),
             )
 
-        def quantize_q(c, first=False):
-            rows = live if first else slice(0, P)
-            i = c + CHUNKS * first
+        def quantize_q(c, early=False):
+            rows = tile0 if early else slice(0, P)
+            slot = c + CHUNKS * early
             nc.vector.quantize_mx(
-                out=q_codes[i][rows].bitcast(FP8X4),
-                scales=q_scales[i][rows],
-                in_=q_bf[i][rows].rearrange("p q j -> p (q j)"),
+                out=q_codes[slot][rows].bitcast(FP8X4),
+                scales=q_scales[slot][rows],
+                in_=q_bf[slot][rows].rearrange("p q j -> p (q j)"),
             )
 
-        def round_k(i, half, copy=nc.vector.tensor_copy):
-            src = k_raw[half][:].rearrange("p j (s r) -> p s j r", r=PACK)[:, :, :, 2 * i : 2 * i + 2]
-            dst = k_bf[i][:, :, half * P // 2 : (half + 1) * P // 2, :]
+        def round_k(pair, half, copy=nc.vector.tensor_copy):
+            src = k_raw[half][:].rearrange("p j (s r) -> p s j r", r=PACK)[:, :, :, 2 * pair : 2 * pair + 2]
+            dst = k_bf[pair][:, :, half * P // 2 : (half + 1) * P // 2, :]
             copy(out=dst.rearrange("p r s j -> p s j r"), in_=src)
 
         def quantize_k(r):
             cols = slice(r * P, (r + 1) * P)
             nc.vector.quantize_mx(
-                out=k_codes[live, cols].bitcast(FP8X4),
-                scales=k_scales[live, cols],
-                in_=k_bf[r // 2][live, r % 2].rearrange("p s j -> p (s j)"),
+                out=k_codes[tile0, cols].bitcast(FP8X4),
+                scales=k_scales[tile0, cols],
+                in_=k_bf[r // 2][tile0, r % 2].rearrange("p s j -> p (s j)"),
             )
 
-        def bank_of(h, c, r):
-            second = h == 0 and r % 2 == 1
-            return score_banks[H if second else h]
-
-        def score_pass(h, c, r):
+        def score_pass(dst, h, c, r):
             rows = slice(ROWS * h, ROWS * (h + 1))
-            kc = slice(r * P, (r + 1) * P)
-            first = h == 0 and c < 2
-            qi = c + CHUNKS * first
+            cols = slice(r * P, (r + 1) * P)
+            slot = c + CHUNKS * (h == 0 and c < 2)
             nc.tensor.matmul_mx(
-                out=bank_of(h, c, r)[:, c % 2 if h == 0 else r, :],
-                lhsT=k_codes[rows, kc].bitcast(FP8X4),
-                lhsT_scale=k_scales[rows, kc],
-                rhs=q_codes[qi][rows, :].bitcast(FP8X4),
-                rhs_scale=q_scales[qi][rows, :],
+                out=dst,
+                lhsT=k_codes[rows, cols].bitcast(FP8X4),
+                lhsT_scale=k_scales[rows, cols],
+                rhs=q_codes[slot][rows, :].bitcast(FP8X4),
+                rhs_scale=q_scales[slot][rows, :],
                 start=True,
                 stop=True,
             )
 
-        def cap_first(i, r):
-            nc.scalar.activation(
-                out=capped[i][:, :, r, :], in_=bank_of(0, 0, r)[:, 0:2, :], func=ACT.Tanh, scale=1.0 / CAP
+        def whole_pass(dst, lhs_codes, lhs_scales, rhs_codes, rhs_scales):
+            nc.tensor.matmul_mx(
+                out=dst,
+                lhsT=lhs_codes.bitcast(FP8X4),
+                lhsT_scale=lhs_scales,
+                rhs=rhs_codes.bitcast(FP8X4),
+                rhs_scale=rhs_scales,
+                start=True,
+                stop=True,
             )
+
+        def cap_head0_place(i, r):
+            bank = score_banks[H if r % 2 else 0]
+            for n, (h, c) in enumerate(GROUPS[i]):
+                score_pass(bank[:, n, :], h, c, r)
+            nc.scalar.activation(out=capped_rows[i][:, :, r, :], in_=bank[:, 0:2, :], func=ACT.Tanh, scale=1.0 / CAP)
 
         def scores(i, n):
             h, c = GROUPS[i][n]
             for r in range(PACK):
-                score_pass(h, c, r)
+                score_pass(score_banks[h][:, r, :], h, c, r)
 
-        def cap(i, n, r0=0, r1=PACK):
-            h, c = GROUPS[i][n]
-            nc.scalar.activation(
-                out=capped[i][:, n, r0:r1, :], in_=bank_of(h, c, r0)[:, r0:r1, :], func=ACT.Tanh, scale=1.0 / CAP
-            )
+        def cap(i, n):
+            bank = score_banks[GROUPS[i][n][0]]
+            if i < FIRST_SUMMED:
+                dst, src = capped_rows[i][:, n], bank[:]
+            else:
+                dst, src = capped_words[i][:, n], bank[:].rearrange("p r q -> p q r")
+            nc.scalar.activation(out=dst, in_=src, func=ACT.Tanh, scale=1.0 / CAP)
 
-        def weigh(i, r, n0=0, n1=2):
+        def weigh_place(i, r):
             nc.scalar.activation(
-                out=w_rows[i][:, n0:n1, r, :],
-                in_=capped[i][:, n0:n1, r, :],
+                out=w_rows[i][:, :, r, :],
+                in_=capped_rows[i][:, :, r, :],
                 func=ACT.Exp,
                 scale=CAP,
                 bias=t_ln[:, r : r + 1],
             )
 
-        def in_word_order(i, n):
-            return capped[i][:, n].rearrange("p r q -> p (r q)").rearrange("p (q r) -> p q r", r=PACK)
-
-        def cap_interleaved(i, n):
-            h, c = GROUPS[i][n]
-            nc.scalar.activation(
-                out=in_word_order(i, n),
-                in_=bank_of(h, c, 0)[:].rearrange("p r q -> p q r"),
-                func=ACT.Tanh,
-                scale=1.0 / CAP,
+        def interleave(i, n):
+            nc.vector.tensor_copy(
+                out=w_bf[i][:, n].rearrange("p (c i) r -> p c r i", i=WALK),
+                in_=w_rows[i][:, n].rearrange("p r (c i) -> p c r i", i=WALK),
             )
 
         def add_ln(i, n):
             nc.vector.scalar_tensor_tensor(
                 out=logits[i][:, n],
-                in0=in_word_order(i, n),
+                in0=capped_words[i][:, n],
                 scalar=CAP,
                 in1=t_ln[:].unsqueeze(1).to_broadcast([P, QT, PACK]),
                 op0=ALU.mult,
                 op1=ALU.add,
             )
 
-        def weigh_interleaved(i, n, q0=0, q1=QT):
+        def weigh_summed(i, n, q0=0, q1=QT):
             nc.scalar.activation(out=w_bf[i][:, n, q0:q1, :], in_=logits[i][:, n, q0:q1, :], func=ACT.Exp)
-
-        def weigh_group(i):
-            nc.scalar.activation(out=w_bf[i][:], in_=logits[i][:], func=ACT.Exp)
-
-        def interleave(i, n):
-            nc.vector.tensor_copy(
-                out=w_bf[i][:, n].rearrange("p (c i) r -> p c r i", i=4),
-                in_=w_rows[i][:, n].rearrange("p r (c i) -> p c r i", i=4),
-            )
 
         def quantize_w(i, n, q0=0, q1=QT):
             nc.vector.quantize_mx(
@@ -199,108 +201,85 @@ def tile_rows_sink_cap_gqa_kernel(tc, qT, kT, t, v, sink, out):
             )
 
         def values(i, n):
-            nc.tensor.matmul_mx(
-                out=y_of(i)[:, sorted(GROUPS[i]).index(GROUPS[i][n]), :],
-                lhsT=w_codes[i][:, n, :].bitcast(FP8X4),
-                lhsT_scale=w_scales[i][:, n, :],
-                rhs=v_codes[:].bitcast(FP8X4),
-                rhs_scale=v_scales[:],
-                start=True,
-                stop=True,
-            )
+            dst = y_banks[i % Y_BANKS][:, sorted(GROUPS[i]).index(GROUPS[i][n]), :]
+            whole_pass(dst, w_codes[i][:, n, :], w_scales[i][:, n, :], v_codes[:], v_scales[:])
 
-        def keep_busy(i, bank, passes):
+        def keep_warm(i, bank_of, passes):
+            dst = y_banks[bank_of % Y_BANKS][:, PACK - 1, :]
             for rep in range(passes):
-                nc.tensor.matmul_mx(
-                    out=y_banks[bank][:, PACK - 1, :],
-                    lhsT=w_codes[i][:, 0, :].bitcast(FP8X4),
-                    lhsT_scale=w_scales[i][:, 0, :],
-                    rhs=v_codes[:].bitcast(FP8X4),
-                    rhs_scale=v_scales[:],
-                    start=True,
-                    stop=True,
-                )
+                whole_pass(dst, w_codes[i][:, 0, :], w_scales[i][:, 0, :], v_codes[:], v_scales[:])
 
-        def warm(passes):
-            for rep in range(passes):
-                nc.tensor.matmul_mx(
-                    out=y_banks[2][:, PACK - 1, :],
-                    lhsT=warm_codes[:].bitcast(FP8X4),
-                    lhsT_scale=warm_scales[:],
-                    rhs=warm_codes[:].bitcast(FP8X4),
-                    rhs_scale=warm_scales[:],
-                    start=True,
-                    stop=True,
-                )
-
-        def places(i):
+        def units_in_out(i):
             first, final = [CHUNKS * h + c for h, c in (min(GROUPS[i]), max(GROUPS[i]))]
             return slice(first, final + 1, max(final - first, 1))
 
         def add_sink(i):
+            y = y_banks[i % Y_BANKS]
             nc.vector.tensor_tensor(
-                out=den[i][:], in0=y_of(i)[:, 0 : len(GROUPS[i]), D - 1], in1=sink_sb[:, places(i)], op=ALU.add
+                out=den[i][:], in0=y[:, 0 : len(GROUPS[i]), D - 1], in1=sink_sb[:, units_in_out(i)], op=ALU.add
             )
 
         def invert(i):
             nc.vector.reciprocal(out=rec[i][:], in_=den[i][:])
 
-        def store(i, queue=nc.sync):
-            queue.dma_start(out=out.rearrange("h (c p) e -> p (h c) e", p=QT)[:, places(i), :], in_=res[i][:])
+        def store(i):
+            dst = out.rearrange("h (c p) e -> p (h c) e", p=QT)[:, units_in_out(i), :]
+            nc.sync.dma_start(out=dst, in_=res[i][:])
 
         def divide(i):
             n = len(GROUPS[i])
             nc.vector.tensor_tensor(
                 out=res[i][:],
-                in0=y_of(i)[:, 0:n, :],
+                in0=y_banks[i % Y_BANKS][:, 0:n, :],
                 in1=rec[i][:].unsqueeze(2).to_broadcast([P, n, D]),
                 op=ALU.mult,
             )
             store(i)
 
-        def divide_on_scalar(i, queue=nc.sync):
+        def divide_on_scalar(i):
             for n in range(len(GROUPS[i])):
                 nc.scalar.activation(
-                    out=res[i][:, n, :], in_=y_of(i)[:, n, :], func=ACT.Copy, scale=rec[i][:, n : n + 1]
+                    out=res[i][:, n, :], in_=y_banks[i % Y_BANKS][:, n, :], func=ACT.Copy, scale=rec[i][:, n : n + 1]
                 )
-            store(i, queue)
+            store(i)
 
         nc.scalar.dma_start(out=t_sb[:], in_=t.rearrange("(p j) o -> p (j o)", j=PACK))
-        nc.sync.dma_start(out=q_raw[0][live], in_=q_src[live, :, 0:256])
+        nc.sync.dma_start(out=q_raw[0][tile0], in_=q_src[tile0, :, 0 : NQ // 2])
         for half in range(2):
             nc.sync.dma_start(out=k_raw[half][:], in_=k_src[:, :, half * N // 2 : (half + 1) * N // 2])
-        nc.sync.dma_start(out=q_raw[1][:], in_=q_src[:, :, 256:512])
+        nc.sync.dma_start(out=q_raw[1][:], in_=q_src[:, :, NQ // 2 : NQ])
         nc.sync.dma_start(out=v_raw[:], in_=v[0].rearrange("(p j) e -> p j e", j=PACK))
 
         nc.vector.memset(warm_bf[:].bitcast(I32), 0)
-        nc.vector.memset(k_mx[live, N:], 0)
+        nc.vector.memset(k_mx[tile0, N:], 0)
         nc.vector.quantize_mx(out=warm_codes[:].bitcast(FP8X4), scales=warm_scales[:], in_=warm_bf[:])
-        warm(26)
+        for rep in range(WARM_START):
+            whole_pass(
+                y_banks[Y_BANKS - 1][:, PACK - 1, :], warm_codes[:], warm_scales[:], warm_codes[:], warm_scales[:]
+            )
+
         nc.vector.scalar_tensor_tensor(
             out=t_abs[:], in0=t_sb[:], scalar=-1.0, in1=t_sb[:], op0=ALU.mult, op1=ALU.max
         )
         nc.scalar.activation(out=t_ln[:], in_=t_abs[:], func=ACT.Ln)
+        nc.scalar.activation(out=t_sign[:], in_=t_sb[:], func=ACT.Tanh, scale=SATURATE)
 
-        nc.scalar.activation(out=t_sign[:], in_=t_sb[:], func=ACT.Tanh, scale=2.0**69)
-
-        round_q(0, True)
-        round_q(1, True)
-        quantize_q(0, True)
+        round_q(0, early=True)
+        round_q(1, early=True)
+        quantize_q(0, early=True)
         round_k(0, 0)
         round_k(1, 0, nc.scalar.copy)
-        quantize_q(1, True)
+        quantize_q(1, early=True)
         round_k(0, 1)
         round_k(1, 1)
-        quantize_k(0)
-        quantize_k(1)
-        quantize_k(2)
-        quantize_k(3)
-        for g in (2, 3, 1):
-            nc.sync.dma_start(out=k_mx[g * ROWS : (g + 1) * ROWS, :], in_=k_mx[live, :])
+        for r in range(PACK):
+            quantize_k(r)
+        for g in OTHER_HEADS:
+            nc.sync.dma_start(out=k_mx[g * ROWS : (g + 1) * ROWS, :], in_=k_mx[tile0, :])
         with nc.allow_non_contiguous_dma(reason="one sink a query row"):
             nc.sync.dma_start(out=sink_sb[:], in_=sink.rearrange("h (c p) o -> p (h c o)", p=QT))
         for rows in (slice(ROWS, 3 * ROWS), slice(3 * ROWS, P)):
-            nc.sync.dma_start(out=q_raw[0][rows], in_=q_src[rows, :, 0:256])
+            nc.sync.dma_start(out=q_raw[0][rows], in_=q_src[rows, :, 0 : NQ // 2])
         round_q(2)
         round_q(3)
         quantize_q(2)
@@ -315,39 +294,36 @@ def tile_rows_sink_cap_gqa_kernel(tc, qT, kT, t, v, sink, out):
             out=v_codes[:].bitcast(FP8X4), scales=v_scales[:], in_=v_bf[:].rearrange("p e j -> p (e j)")
         )
 
-        for i in range(2):
-            for half in range(2):
-                for r in (2 * half, 2 * half + 1):
-                    for h, c in GROUPS[i]:
-                        score_pass(h, c, r)
-                    cap_first(i, r)
-                for r in (2 * half, 2 * half + 1):
-                    weigh(i, r)
+        for i in range(len(HEAD0_GROUPS)):
+            for pair in ((0, 1), (2, 3)):
+                for r in pair:
+                    cap_head0_place(i, r)
+                for r in pair:
+                    weigh_place(i, r)
 
-        def after_weights(i):
+        member = {unit: (i, n) for i, g in enumerate(GROUPS) for n, unit in enumerate(g)}
+        turn = [member[unit] for unit in TURNS]
+        ahead = len(OTHER_HEADS)
+
+        def cap_and_refill(u):
+            cap(*turn[u])
+            if u + ahead < len(turn):
+                scores(*turn[u + ahead])
+
+        def finish_by_place(i):
             interleave(i, 0)
-            if i > 0:
-                invert(i - 1)
+            invert(i - 1)
             interleave(i, 1)
-            if i > 0:
-                divide(i - 1)
+            divide(i - 1)
             quantize_w(i, 0)
             quantize_w(i, 1)
 
-        where = {unit: (i, n) for i, g in enumerate(GROUPS) for n, unit in enumerate(g)}
-        later = [where[unit] for unit in LATER]
-        half = QT // 2
-        e, a, b, d = range(last - 3, last + 1)
-
-        def cap_and_refill(u):
-            (cap if later[u][0] < e else cap_interleaved)(*later[u])
-            if u + 3 < len(later):
-                scores(*later[u + 3])
-
-        after_weights(0)
-        scores(*later[0])
-        scores(*later[1])
-        scores(*later[2])
+        interleave(0, 0)
+        interleave(0, 1)
+        quantize_w(0, 0)
+        quantize_w(0, 1)
+        for u in range(ahead):
+            scores(*turn[u])
         values(0, 0)
         values(0, 1)
         interleave(1, 0)
@@ -359,67 +335,69 @@ def tile_rows_sink_cap_gqa_kernel(tc, qT, kT, t, v, sink, out):
         round_q(0)
         divide(0)
         round_q(1)
-        for i in range(2, e):
-            u = 3 * (i - 2)
+        quantize_q(0)
+        quantize_q(1)
+
+        for i in range(len(HEAD0_GROUPS), FIRST_SUMMED):
+            u = ahead * (i - len(HEAD0_GROUPS))
             cap_and_refill(u)
             cap_and_refill(u + 1)
             values(i - 1, 0)
             values(i - 1, 1)
-            if i == 2:
-                quantize_q(0)
-                quantize_q(1)
             cap_and_refill(u + 2)
-            add_ln(*later[u + 2])
+            add_ln(*turn[u + 2])
             add_sink(i - 1)
-            weigh(i, 0)
-            weigh(i, 1)
-            if i + 1 == e:
+            weigh_place(i, 0)
+            weigh_place(i, 1)
+            if i + 1 == FIRST_SUMMED:
                 cap_and_refill(u + 3)
-                add_ln(*later[u + 3])
-            weigh(i, 2)
-            weigh(i, 3)
-            after_weights(i)
+                add_ln(*turn[u + 3])
+            weigh_place(i, 2)
+            weigh_place(i, 3)
+            finish_by_place(i)
 
-        cap_interleaved(b, 0)
-        weigh_group(e)
-        cap_interleaved(d, 0)
-        values(e - 1, 0)
-        values(e - 1, 1)
-        keep_busy(e - 1, 0, 4)
-        add_ln(b, 0)
-        quantize_w(e, 0)
-        values(e, 0)
-        quantize_w(e, 1)
-        values(e, 1)
-        keep_busy(e, 0, 2)
-        add_sink(e - 1)
-        add_ln(d, 0)
-        weigh_interleaved(a, 0)
-        weigh_interleaved(a, 1)
-        weigh_interleaved(b, 0)
-        weigh_interleaved(d, 0, 0, half)
-        weigh_interleaved(d, 0, half, QT)
-        invert(e - 1)
-        quantize_w(a, 0)
-        values(a, 0)
-        add_sink(e)
-        quantize_w(a, 1)
-        values(a, 1)
-        divide(e - 1)
-        keep_busy(e, 1, 2)
-        invert(e)
-        quantize_w(b, 0)
-        values(b, 0)
-        divide_on_scalar(e)
-        quantize_w(d, 0, 0, half)
-        add_sink(a)
-        quantize_w(d, 0, half, QT)
-        values(d, 0)
-        invert(a)
-        divide_on_scalar(a)
-        add_sink(b)
-        invert(b)
-        divide_on_scalar(b)
-        add_sink(d)
-        invert(d)
-        divide(d)
+        placed = FIRST_SUMMED - 1
+        pair1, pair2, single1, single2 = range(FIRST_SUMMED, len(GROUPS))
+        half_q = QT // 2
+        cap(single1, 0)
+        nc.scalar.activation(out=w_bf[pair1][:], in_=logits[pair1][:], func=ACT.Exp)
+        cap(single2, 0)
+        values(placed, 0)
+        values(placed, 1)
+        keep_warm(placed, pair2, WARM_LONG_GAP)
+        add_ln(single1, 0)
+        for n in range(2):
+            quantize_w(pair1, n)
+            values(pair1, n)
+        keep_warm(pair1, pair2, WARM_SHORT_GAP)
+        add_sink(placed)
+        add_ln(single2, 0)
+        weigh_summed(pair2, 0)
+        weigh_summed(pair2, 1)
+        weigh_summed(single1, 0)
+        weigh_summed(single2, 0, 0, half_q)
+        weigh_summed(single2, 0, half_q, QT)
+        invert(placed)
+        quantize_w(pair2, 0)
+        values(pair2, 0)
+        add_sink(pair1)
+        quantize_w(pair2, 1)
+        values(pair2, 1)
+        divide(placed)
+        keep_warm(pair1, single1, WARM_SHORT_GAP)
+        invert(pair1)
+        quantize_w(single1, 0)
+        values(single1, 0)
+        divide_on_scalar(pair1)
+        quantize_w(single2, 0, 0, half_q)
+        add_sink(pair2)
+        quantize_w(single2, 0, half_q, QT)
+        values(single2, 0)
+        invert(pair2)
+        divide_on_scalar(pair2)
+        add_sink(single1)
+        invert(single1)
+        divide_on_scalar(single1)
+        add_sink(single2)
+        invert(single2)
+        divide(single2)

@@ -1,3 +1,4 @@
+import math
 from contextlib import ExitStack
 
 import concourse.mybir as mybir
@@ -10,6 +11,7 @@ F32 = mybir.dt.float32
 BF16 = mybir.dt.bfloat16
 I32 = mybir.dt.int32
 U8 = mybir.dt.uint8
+U32 = mybir.dt.uint32
 FP8X4 = mybir.dt.float8_e4m3fn_x4
 ACT = mybir.ActivationFunctionType
 ALU = mybir.AluOpType
@@ -21,7 +23,9 @@ QT = 128
 CHUNKS = NQ // QT
 WALK = 4
 
-SATURATE = 2.0**69
+BITS_TO_LN = math.log(2.0) / 2.0**23
+BITS_OFFSET = -127.0 * math.log(2.0) + 0.0298
+LN_DEGREE = 5
 
 OTHER_HEADS = (2, 3, 1)
 TURNS = [(h, c) for c in (2, 3, 0, 1) for h in OTHER_HEADS]
@@ -53,6 +57,10 @@ def tile_rows_sink_cap_gqa_kernel(tc, qT, kT, t, v, sink, out):
         t_abs = sb.tile([P, PACK], F32)
         t_ln = sb.tile([P, PACK], F32)
         t_sign = sb.tile([P, PACK], F32)
+        t_guess = sb.tile([P, PACK], F32)
+        t_inv = sb.tile([P, PACK], F32)
+        t_rest = sb.tile([P, PACK], F32)
+        t_horner = [sb.tile([P, PACK], F32, name="t_horner%d" % i) for i in range(LN_DEGREE - 1)]
         sink_sb = sb.tile([P, H * CHUNKS], F32)
 
         q_slots = range(CHUNKS + 2)
@@ -77,7 +85,8 @@ def tile_rows_sink_cap_gqa_kernel(tc, qT, kT, t, v, sink, out):
             }
 
         capped_rows = per_group("capped_rows", [PACK, QT], F32, end=FIRST_SUMMED)
-        w_rows = per_group("w_rows", [PACK, QT], BF16, end=FIRST_SUMMED)
+        w_rows = per_group("w_rows", [PACK, QT], BF16, first=1, end=FIRST_SUMMED)
+        p_rows = sb.tile([P, 2, PACK, QT], F32, align_bytes=64)
         capped_words = per_group("capped_words", [QT, PACK], F32, first=FIRST_SUMMED)
         logits = per_group("logits", [QT, PACK], F32, first=FIRST_SUMMED)
         w_bf = per_group("w_bf", [QT, PACK], BF16)
@@ -91,10 +100,10 @@ def tile_rows_sink_cap_gqa_kernel(tc, qT, kT, t, v, sink, out):
 
         tile0 = slice(0, ROWS)
 
-        def round_q(c, early=False):
+        def round_q(c, early=False, copy=nc.vector.tensor_copy):
             rows = tile0 if early else slice(0, P)
             src = q_raw[c // 2][rows, :, (c % 2) * QT : (c % 2 + 1) * QT]
-            nc.vector.tensor_copy(
+            copy(
                 out=q_bf[c + CHUNKS * early][rows].rearrange("p (c i) j -> p c j i", i=WALK),
                 in_=src.rearrange("p j (c i) -> p c j i", i=WALK),
             )
@@ -166,6 +175,9 @@ def tile_rows_sink_cap_gqa_kernel(tc, qT, kT, t, v, sink, out):
             nc.scalar.activation(out=dst, in_=src, func=ACT.Tanh, scale=1.0 / CAP)
 
         def weigh_place(i, r):
+            if i == 0:
+                nc.scalar.activation(out=p_rows[:, :, r, :], in_=capped_rows[i][:, :, r, :], func=ACT.Exp, scale=CAP)
+                return
             nc.scalar.activation(
                 out=w_rows[i][:, :, r, :],
                 in_=capped_rows[i][:, :, r, :],
@@ -175,9 +187,34 @@ def tile_rows_sink_cap_gqa_kernel(tc, qT, kT, t, v, sink, out):
             )
 
         def interleave(i, n):
+            if i == 0:
+                nc.vector.tensor_tensor(
+                    out=w_bf[i][:, n].rearrange("p (c i) r -> p c r i", i=WALK),
+                    in0=p_rows[:, n].rearrange("p r (c i) -> p c r i", i=WALK),
+                    in1=t_abs[:].unsqueeze(1).unsqueeze(3).to_broadcast([P, QT // WALK, PACK, WALK]),
+                    op=ALU.mult,
+                )
+                return
             nc.vector.tensor_copy(
                 out=w_bf[i][:, n].rearrange("p (c i) r -> p c r i", i=WALK),
                 in_=w_rows[i][:, n].rearrange("p r (c i) -> p c r i", i=WALK),
+            )
+
+        def ln_step(k):
+            lead = (-1.0) ** (LN_DEGREE + 1) / LN_DEGREE
+            if k == LN_DEGREE - 1:
+                nc.vector.scalar_tensor_tensor(
+                    out=t_ln[:], in0=t_horner[k - 1][:], scalar=lead, in1=t_guess[:], op0=ALU.mult, op1=ALU.add
+                )
+                return
+            power = LN_DEGREE - 1 - k
+            nc.vector.scalar_tensor_tensor(
+                out=t_horner[k][:],
+                in0=t_horner[k - 1][:] if k else t_rest[:],
+                scalar=(-1.0) ** (power + 1) / power / lead,
+                in1=t_rest[:],
+                op0=ALU.add,
+                op1=ALU.mult,
             )
 
         def add_ln(i, n):
@@ -258,17 +295,21 @@ def tile_rows_sink_cap_gqa_kernel(tc, qT, kT, t, v, sink, out):
                 y_banks[Y_BANKS - 1][:, PACK - 1, :], warm_codes[:], warm_scales[:], warm_codes[:], warm_scales[:]
             )
 
-        nc.vector.scalar_tensor_tensor(
-            out=t_abs[:], in0=t_sb[:], scalar=-1.0, in1=t_sb[:], op0=ALU.mult, op1=ALU.max
-        )
-        nc.scalar.activation(out=t_ln[:], in_=t_abs[:], func=ACT.Ln)
-        nc.scalar.activation(out=t_sign[:], in_=t_sb[:], func=ACT.Tanh, scale=SATURATE)
-
         round_q(0, early=True)
-        round_q(1, early=True)
+        round_q(1, early=True, copy=nc.scalar.copy)
+        round_k(1, 0, nc.scalar.copy)
+        nc.scalar.activation(out=t_abs[:], in_=t_sb[:], func=ACT.Abs)
+        nc.scalar.activation(out=t_sign[:], in_=t_sb[:], func=ACT.Sign)
+        nc.scalar.activation(
+            out=t_guess[:], in_=t_abs[:].bitcast(U32), func=ACT.Copy, scale=BITS_TO_LN, bias=BITS_OFFSET
+        )
+        nc.scalar.activation(out=t_inv[:], in_=t_guess[:], func=ACT.Exp, scale=-1.0)
+        for r in range(PACK):
+            nc.scalar.activation(
+                out=t_rest[:, r : r + 1], in_=t_inv[:, r : r + 1], func=ACT.Copy, scale=t_abs[:, r : r + 1], bias=-1.0
+            )
         quantize_q(0, early=True)
         round_k(0, 0)
-        round_k(1, 0, nc.scalar.copy)
         quantize_q(1, early=True)
         round_k(0, 1)
         round_k(1, 1)
@@ -281,15 +322,20 @@ def tile_rows_sink_cap_gqa_kernel(tc, qT, kT, t, v, sink, out):
         for rows in (slice(ROWS, 3 * ROWS), slice(3 * ROWS, P)):
             nc.sync.dma_start(out=q_raw[0][rows], in_=q_src[rows, :, 0 : NQ // 2])
         round_q(2)
+        ln_step(0)
         round_q(3)
+        ln_step(1)
         quantize_q(2)
+        ln_step(2)
         quantize_q(3)
+        ln_step(3)
         nc.vector.tensor_tensor(
             out=v_bf[:],
             in0=v_raw[:].rearrange("p j e -> p e j"),
             in1=t_sign[:].unsqueeze(1).to_broadcast([P, D, PACK]),
             op=ALU.mult,
         )
+        ln_step(4)
         nc.vector.quantize_mx(
             out=v_codes[:].bitcast(FP8X4), scales=v_scales[:], in_=v_bf[:].rearrange("p e j -> p (e j)")
         )

@@ -296,8 +296,7 @@ def tile_rows_sink_cap_gqa_kernel(tc, qT, kT, t, v, sink, out):
             )
 
         round_q(0, early=True)
-        round_q(1, early=True, copy=nc.scalar.copy)
-        round_k(1, 0, nc.scalar.copy)
+        round_q(1, early=True)
         nc.scalar.activation(out=t_abs[:], in_=t_sb[:], func=ACT.Abs)
         nc.scalar.activation(out=t_sign[:], in_=t_sb[:], func=ACT.Sign)
         nc.scalar.activation(
@@ -310,18 +309,21 @@ def tile_rows_sink_cap_gqa_kernel(tc, qT, kT, t, v, sink, out):
             )
         quantize_q(0, early=True)
         round_k(0, 0)
-        quantize_q(1, early=True)
+        round_k(1, 0)
         round_k(0, 1)
+        quantize_q(1, early=True)
+        quantize_k(0)
+        quantize_k(1)
         round_k(1, 1)
-        for r in range(PACK):
-            quantize_k(r)
+        round_q(2)
+        quantize_k(2)
+        quantize_k(3)
         for g in OTHER_HEADS:
             nc.sync.dma_start(out=k_mx[g * ROWS : (g + 1) * ROWS, :], in_=k_mx[tile0, :])
         with nc.allow_non_contiguous_dma(reason="one sink a query row"):
             nc.sync.dma_start(out=sink_sb[:], in_=sink.rearrange("h (c p) o -> p (h c o)", p=QT))
         for rows in (slice(ROWS, 3 * ROWS), slice(3 * ROWS, P)):
             nc.sync.dma_start(out=q_raw[0][rows], in_=q_src[rows, :, 0 : NQ // 2])
-        round_q(2)
         ln_step(0)
         round_q(3)
         ln_step(1)

@@ -21,6 +21,7 @@ PACK = 4
 ROWS = D // PACK
 QT = 128
 CHUNKS = NQ // QT
+K_PIECES = ((0, 256), (256, 384), (384, 512))
 WALK = 4
 
 BITS_TO_LN = math.log(2.0) / 2.0**23
@@ -36,7 +37,7 @@ GROUPS = HEAD0_GROUPS + BY_PLACE + SUMMED
 FIRST_SUMMED = len(GROUPS) - len(SUMMED)
 Y_BANKS = 3
 
-WARM_START = 28
+WARM_START = 22
 WARM_LONG_GAP = 4
 WARM_SHORT_GAP = 2
 
@@ -51,7 +52,7 @@ def tile_rows_sink_cap_gqa_kernel(tc, qT, kT, t, v, sink, out):
         q_src = qT.rearrange("h (p j) q -> (h p) j q", j=PACK)
         k_src = kT[0].rearrange("(p j) i -> p j i", j=PACK)
         q_raw = [sb.tile([P, PACK, NQ // 2], F32, name="q_raw%d" % i) for i in range(2)]
-        k_raw = [sb.tile([ROWS, PACK, N // 2], F32, name="k_raw%d" % i) for i in range(2)]
+        k_raw = [sb.tile([ROWS, PACK, b - a], F32, name="k_raw%d" % a) for a, b in K_PIECES]
         v_raw = sb.tile([P, PACK, D], F32)
         t_sb = sb.tile([P, PACK], F32)
         t_abs = sb.tile([P, PACK], F32)
@@ -59,6 +60,7 @@ def tile_rows_sink_cap_gqa_kernel(tc, qT, kT, t, v, sink, out):
         t_sign = sb.tile([P, PACK], F32)
         t_guess = sb.tile([P, PACK], F32)
         t_inv = sb.tile([P, PACK], F32)
+        t_near1 = sb.tile([P, PACK], F32)
         t_rest = sb.tile([P, PACK], F32)
         t_horner = [sb.tile([P, PACK], F32, name="t_horner%d" % i) for i in range(LN_DEGREE - 1)]
         sink_sb = sb.tile([P, H * CHUNKS], F32)
@@ -119,7 +121,7 @@ def tile_rows_sink_cap_gqa_kernel(tc, qT, kT, t, v, sink, out):
 
         def round_k(pair, half, copy=nc.vector.tensor_copy):
             src = k_raw[half][:].rearrange("p j (s r) -> p s j r", r=PACK)[:, :, :, 2 * pair : 2 * pair + 2]
-            dst = k_bf[pair][:, :, half * P // 2 : (half + 1) * P // 2, :]
+            dst = k_bf[pair][:, :, K_PIECES[half][0] // PACK : K_PIECES[half][1] // PACK, :]
             copy(out=dst.rearrange("p r s j -> p s j r"), in_=src)
 
         def quantize_k(r):
@@ -175,9 +177,6 @@ def tile_rows_sink_cap_gqa_kernel(tc, qT, kT, t, v, sink, out):
             nc.scalar.activation(out=dst, in_=src, func=ACT.Tanh, scale=1.0 / CAP)
 
         def weigh_place(i, r):
-            if i == 0:
-                nc.scalar.activation(out=p_rows[:, :, r, :], in_=capped_rows[i][:, :, r, :], func=ACT.Exp, scale=CAP)
-                return
             nc.scalar.activation(
                 out=w_rows[i][:, :, r, :],
                 in_=capped_rows[i][:, :, r, :],
@@ -281,9 +280,10 @@ def tile_rows_sink_cap_gqa_kernel(tc, qT, kT, t, v, sink, out):
             store(i)
 
         nc.scalar.dma_start(out=t_sb[:], in_=t.rearrange("(p j) o -> p (j o)", j=PACK))
-        nc.sync.dma_start(out=q_raw[0][tile0], in_=q_src[tile0, :, 0 : NQ // 2])
-        for half in range(2):
-            nc.sync.dma_start(out=k_raw[half][:], in_=k_src[:, :, half * N // 2 : (half + 1) * N // 2])
+        nc.sync.dma_start(out=q_raw[0][tile0, :, 0:QT], in_=q_src[tile0, :, 0:QT])
+        for i, (a, b) in enumerate(K_PIECES):
+            nc.sync.dma_start(out=k_raw[i][:], in_=k_src[:, :, a:b])
+        nc.sync.dma_start(out=q_raw[0][tile0, :, QT : 2 * QT], in_=q_src[tile0, :, QT : 2 * QT])
         nc.sync.dma_start(out=q_raw[1][:], in_=q_src[:, :, NQ // 2 : NQ])
         nc.sync.dma_start(out=v_raw[:], in_=v[0].rearrange("(p j) e -> p j e", j=PACK))
 
@@ -296,34 +296,32 @@ def tile_rows_sink_cap_gqa_kernel(tc, qT, kT, t, v, sink, out):
             )
 
         round_q(0, early=True)
-        round_q(1, early=True)
+        round_k(1, 0, nc.scalar.copy)
         nc.scalar.activation(out=t_abs[:], in_=t_sb[:], func=ACT.Abs)
         nc.scalar.activation(out=t_sign[:], in_=t_sb[:], func=ACT.Sign)
+        round_k(1, 2, nc.scalar.copy)
         nc.scalar.activation(
             out=t_guess[:], in_=t_abs[:].bitcast(U32), func=ACT.Copy, scale=BITS_TO_LN, bias=BITS_OFFSET
         )
+        round_q(1, early=True, copy=nc.scalar.copy)
         nc.scalar.activation(out=t_inv[:], in_=t_guess[:], func=ACT.Exp, scale=-1.0)
-        for r in range(PACK):
-            nc.scalar.activation(
-                out=t_rest[:, r : r + 1], in_=t_inv[:, r : r + 1], func=ACT.Copy, scale=t_abs[:, r : r + 1], bias=-1.0
-            )
         quantize_q(0, early=True)
         round_k(0, 0)
-        round_k(1, 0)
         round_k(0, 1)
-        quantize_q(1, early=True)
-        quantize_k(0)
-        quantize_k(1)
+        round_k(0, 2)
         round_k(1, 1)
-        round_q(2)
-        quantize_k(2)
-        quantize_k(3)
+        for r in range(PACK):
+            quantize_k(r)
+        quantize_q(1, early=True)
+        nc.vector.tensor_tensor(out=t_near1[:], in0=t_inv[:], in1=t_abs[:], op=ALU.mult)
         for g in OTHER_HEADS:
             nc.sync.dma_start(out=k_mx[g * ROWS : (g + 1) * ROWS, :], in_=k_mx[tile0, :])
         with nc.allow_non_contiguous_dma(reason="one sink a query row"):
             nc.sync.dma_start(out=sink_sb[:], in_=sink.rearrange("h (c p) o -> p (h c o)", p=QT))
         for rows in (slice(ROWS, 3 * ROWS), slice(3 * ROWS, P)):
             nc.sync.dma_start(out=q_raw[0][rows], in_=q_src[rows, :, 0 : NQ // 2])
+        nc.vector.tensor_scalar(out=t_rest[:], in0=t_near1[:], scalar1=-1.0, scalar2=None, op0=ALU.add)
+        round_q(2)
         ln_step(0)
         round_q(3)
         ln_step(1)
@@ -342,12 +340,23 @@ def tile_rows_sink_cap_gqa_kernel(tc, qT, kT, t, v, sink, out):
             out=v_codes[:].bitcast(FP8X4), scales=v_scales[:], in_=v_bf[:].rearrange("p e j -> p (e j)")
         )
 
-        for i in range(len(HEAD0_GROUPS)):
-            for pair in ((0, 1), (2, 3)):
-                for r in pair:
-                    cap_head0_place(i, r)
-                for r in pair:
-                    weigh_place(i, r)
+        for c in range(2):
+            for pair, bank in enumerate((score_banks[0], score_banks[H])):
+                for n in range(2):
+                    score_pass(bank[:, n, :], 0, c, 2 * pair + n)
+                nc.scalar.activation(
+                    out=capped_rows[0][:, c, 2 * pair : 2 * pair + 2, :], in_=bank[:, 0:2, :], func=ACT.Tanh, scale=1.0 / CAP
+                )
+            for pair in range(2):
+                places = slice(2 * pair, 2 * pair + 2)
+                nc.scalar.activation(
+                    out=p_rows[:, c, places, :], in_=capped_rows[0][:, c, places, :], func=ACT.Exp, scale=CAP
+                )
+        for pair in ((0, 1), (2, 3)):
+            for r in pair:
+                cap_head0_place(1, r)
+            for r in pair:
+                weigh_place(1, r)
 
         member = {unit: (i, n) for i, g in enumerate(GROUPS) for n, unit in enumerate(g)}
         turn = [member[unit] for unit in TURNS]

@@ -87,8 +87,8 @@ def tile_rows_sink_cap_gqa_kernel(tc, qT, kT, t, v, sink, out):
             }
 
         capped_rows = per_group("capped_rows", [PACK, QT], F32, end=FIRST_SUMMED)
-        w_rows = per_group("w_rows", [PACK, QT], BF16, first=1, end=FIRST_SUMMED)
-        p_rows = sb.tile([P, 2, PACK, QT], F32, align_bytes=64)
+        w_rows = per_group("w_rows", [PACK, QT], BF16, first=2, end=FIRST_SUMMED)
+        p_rows = per_group("p_rows", [PACK, QT], F32, end=2)
         capped_words = per_group("capped_words", [QT, PACK], F32, first=FIRST_SUMMED)
         logits = per_group("logits", [QT, PACK], F32, first=FIRST_SUMMED)
         w_bf = per_group("w_bf", [QT, PACK], BF16)
@@ -186,10 +186,10 @@ def tile_rows_sink_cap_gqa_kernel(tc, qT, kT, t, v, sink, out):
             )
 
         def interleave(i, n):
-            if i == 0:
+            if i < 2:
                 nc.vector.tensor_tensor(
                     out=w_bf[i][:, n].rearrange("p (c i) r -> p c r i", i=WALK),
-                    in0=p_rows[:, n].rearrange("p r (c i) -> p c r i", i=WALK),
+                    in0=p_rows[i][:, n].rearrange("p r (c i) -> p c r i", i=WALK),
                     in1=t_abs[:].unsqueeze(1).unsqueeze(3).to_broadcast([P, QT // WALK, PACK, WALK]),
                     op=ALU.mult,
                 )
@@ -279,11 +279,11 @@ def tile_rows_sink_cap_gqa_kernel(tc, qT, kT, t, v, sink, out):
                 )
             store(i)
 
-        nc.scalar.dma_start(out=t_sb[:], in_=t.rearrange("(p j) o -> p (j o)", j=PACK))
         nc.sync.dma_start(out=q_raw[0][tile0, :, 0:QT], in_=q_src[tile0, :, 0:QT])
         for i, (a, b) in enumerate(K_PIECES):
             nc.sync.dma_start(out=k_raw[i][:], in_=k_src[:, :, a:b])
         nc.sync.dma_start(out=q_raw[0][tile0, :, QT : 2 * QT], in_=q_src[tile0, :, QT : 2 * QT])
+        nc.sync.dma_start(out=t_sb[:], in_=t.rearrange("(p j) o -> p (j o)", j=PACK))
         nc.sync.dma_start(out=q_raw[1][:], in_=q_src[:, :, NQ // 2 : NQ])
         nc.sync.dma_start(out=v_raw[:], in_=v[0].rearrange("(p j) e -> p j e", j=PACK))
 
@@ -297,14 +297,8 @@ def tile_rows_sink_cap_gqa_kernel(tc, qT, kT, t, v, sink, out):
 
         round_q(0, early=True)
         round_k(1, 0, nc.scalar.copy)
-        nc.scalar.activation(out=t_abs[:], in_=t_sb[:], func=ACT.Abs)
-        nc.scalar.activation(out=t_sign[:], in_=t_sb[:], func=ACT.Sign)
         round_k(1, 2, nc.scalar.copy)
-        nc.scalar.activation(
-            out=t_guess[:], in_=t_abs[:].bitcast(U32), func=ACT.Copy, scale=BITS_TO_LN, bias=BITS_OFFSET
-        )
         round_q(1, early=True, copy=nc.scalar.copy)
-        nc.scalar.activation(out=t_inv[:], in_=t_guess[:], func=ACT.Exp, scale=-1.0)
         quantize_q(0, early=True)
         round_k(0, 0)
         round_k(0, 1)
@@ -312,51 +306,69 @@ def tile_rows_sink_cap_gqa_kernel(tc, qT, kT, t, v, sink, out):
         round_k(1, 1)
         for r in range(PACK):
             quantize_k(r)
+        nc.vector.scalar_tensor_tensor(
+            out=t_abs[:], in0=t_sb[:], scalar=-1.0, in1=t_sb[:], op0=ALU.mult, op1=ALU.max
+        )
         quantize_q(1, early=True)
-        nc.vector.tensor_tensor(out=t_near1[:], in0=t_inv[:], in1=t_abs[:], op=ALU.mult)
+        nc.vector.tensor_scalar(
+            out=t_guess[:], in0=t_abs[:].bitcast(I32), scalar1=BITS_TO_LN, scalar2=BITS_OFFSET, op0=ALU.mult, op1=ALU.add
+        )
+
+        def first_cap(c):
+            for pair, bank in enumerate((score_banks[0], score_banks[H])):
+                for n in range(2):
+                    score_pass(bank[:, n, :], 0, c, 2 * pair + n)
+                nc.scalar.activation(
+                    out=capped_rows[c // 2][:, c % 2, 2 * pair : 2 * pair + 2, :], in_=bank[:, 0:2, :], func=ACT.Tanh, scale=1.0 / CAP
+                )
+
+        def first_exp(c):
+            for pair in range(2):
+                places = slice(2 * pair, 2 * pair + 2)
+                nc.scalar.activation(
+                    out=p_rows[c // 2][:, c % 2, places, :], in_=capped_rows[c // 2][:, c % 2, places, :], func=ACT.Exp, scale=CAP
+                )
+
+        first_cap(0)
+        nc.scalar.activation(out=t_inv[:], in_=t_guess[:], func=ACT.Exp, scale=-1.0)
+        nc.scalar.activation(out=t_sign[:], in_=t_sb[:], func=ACT.Sign)
+        first_exp(0)
+        first_cap(1)
+        first_exp(1)
         for g in OTHER_HEADS:
             nc.sync.dma_start(out=k_mx[g * ROWS : (g + 1) * ROWS, :], in_=k_mx[tile0, :])
         with nc.allow_non_contiguous_dma(reason="one sink a query row"):
             nc.sync.dma_start(out=sink_sb[:], in_=sink.rearrange("h (c p) o -> p (h c o)", p=QT))
         for rows in (slice(ROWS, 3 * ROWS), slice(3 * ROWS, P)):
             nc.sync.dma_start(out=q_raw[0][rows], in_=q_src[rows, :, 0 : NQ // 2])
-        nc.vector.tensor_scalar(out=t_rest[:], in0=t_near1[:], scalar1=-1.0, scalar2=None, op0=ALU.add)
         round_q(2)
-        ln_step(0)
         round_q(3)
-        ln_step(1)
         quantize_q(2)
-        ln_step(2)
+        nc.vector.tensor_tensor(out=t_near1[:], in0=t_inv[:], in1=t_abs[:], op=ALU.mult)
         quantize_q(3)
-        ln_step(3)
+        nc.vector.tensor_scalar(out=t_rest[:], in0=t_near1[:], scalar1=-1.0, scalar2=None, op0=ALU.add)
         nc.vector.tensor_tensor(
             out=v_bf[:],
             in0=v_raw[:].rearrange("p j e -> p e j"),
             in1=t_sign[:].unsqueeze(1).to_broadcast([P, D, PACK]),
             op=ALU.mult,
         )
-        ln_step(4)
+        ln_step(0)
+        interleave(0, 0)
         nc.vector.quantize_mx(
             out=v_codes[:].bitcast(FP8X4), scales=v_scales[:], in_=v_bf[:].rearrange("p e j -> p (e j)")
         )
+        ln_step(1)
+        interleave(0, 1)
+        ln_step(2)
+        quantize_w(0, 0)
+        ln_step(3)
+        quantize_w(0, 1)
+        ln_step(4)
 
-        for c in range(2):
-            for pair, bank in enumerate((score_banks[0], score_banks[H])):
-                for n in range(2):
-                    score_pass(bank[:, n, :], 0, c, 2 * pair + n)
-                nc.scalar.activation(
-                    out=capped_rows[0][:, c, 2 * pair : 2 * pair + 2, :], in_=bank[:, 0:2, :], func=ACT.Tanh, scale=1.0 / CAP
-                )
-            for pair in range(2):
-                places = slice(2 * pair, 2 * pair + 2)
-                nc.scalar.activation(
-                    out=p_rows[:, c, places, :], in_=capped_rows[0][:, c, places, :], func=ACT.Exp, scale=CAP
-                )
-        for pair in ((0, 1), (2, 3)):
-            for r in pair:
-                cap_head0_place(1, r)
-            for r in pair:
-                weigh_place(1, r)
+        for c in (2, 3):
+            first_cap(c)
+            first_exp(c)
 
         member = {unit: (i, n) for i, g in enumerate(GROUPS) for n, unit in enumerate(g)}
         turn = [member[unit] for unit in TURNS]
@@ -375,10 +387,6 @@ def tile_rows_sink_cap_gqa_kernel(tc, qT, kT, t, v, sink, out):
             quantize_w(i, 0)
             quantize_w(i, 1)
 
-        interleave(0, 0)
-        interleave(0, 1)
-        quantize_w(0, 0)
-        quantize_w(0, 1)
         for u in range(ahead):
             scores(*turn[u])
         values(0, 0)

@@ -86,9 +86,12 @@ def tile_rows_sink_cap_gqa_kernel(tc, qT, kT, t, v, sink, out):
                 for i in range(first, end)
             }
 
-        capped_rows = per_group("capped_rows", [PACK, QT], F32, end=FIRST_SUMMED)
+        capped_rows = per_group("capped_rows", [PACK, QT], F32, first=2, end=FIRST_SUMMED)
         w_rows = per_group("w_rows", [PACK, QT], BF16, first=2, end=FIRST_SUMMED)
-        p_rows = per_group("p_rows", [PACK, QT], F32, end=2)
+        p_rows = sb.tile([P, PACK, QT], F32, align_bytes=64)
+        capped0 = sb.tile([P, PACK, QT], F32, align_bytes=64)
+        head0_capped = {c: sb.tile([P, QT, PACK], F32, align_bytes=64, name="head0_capped%d" % c) for c in (1, 2, 3)}
+        head0_p = {c: sb.tile([P, QT, PACK], F32, align_bytes=64, name="head0_p%d" % c) for c in (1, 2, 3)}
         capped_words = per_group("capped_words", [QT, PACK], F32, first=FIRST_SUMMED)
         logits = per_group("logits", [QT, PACK], F32, first=FIRST_SUMMED)
         w_bf = per_group("w_bf", [QT, PACK], BF16)
@@ -186,10 +189,18 @@ def tile_rows_sink_cap_gqa_kernel(tc, qT, kT, t, v, sink, out):
             )
 
         def interleave(i, n):
+            if i < 2 and (i, n) != (0, 0):
+                nc.vector.tensor_tensor(
+                    out=w_bf[i][:, n],
+                    in0=head0_p[2 * i + n][:],
+                    in1=t_abs[:].unsqueeze(1).to_broadcast([P, QT, PACK]),
+                    op=ALU.mult,
+                )
+                return
             if i < 2:
                 nc.vector.tensor_tensor(
                     out=w_bf[i][:, n].rearrange("p (c i) r -> p c r i", i=WALK),
-                    in0=p_rows[i][:, n].rearrange("p r (c i) -> p c r i", i=WALK),
+                    in0=p_rows[:].rearrange("p r (c i) -> p c r i", i=WALK),
                     in1=t_abs[:].unsqueeze(1).unsqueeze(3).to_broadcast([P, QT // WALK, PACK, WALK]),
                     op=ALU.mult,
                 )
@@ -284,7 +295,8 @@ def tile_rows_sink_cap_gqa_kernel(tc, qT, kT, t, v, sink, out):
             nc.sync.dma_start(out=k_raw[i][:], in_=k_src[:, :, a:b])
         nc.sync.dma_start(out=q_raw[0][tile0, :, QT : 2 * QT], in_=q_src[tile0, :, QT : 2 * QT])
         nc.sync.dma_start(out=t_sb[:], in_=t.rearrange("(p j) o -> p (j o)", j=PACK))
-        nc.sync.dma_start(out=q_raw[1][:], in_=q_src[:, :, NQ // 2 : NQ])
+        for c in range(2):
+            nc.sync.dma_start(out=q_raw[1][:, :, c * QT : (c + 1) * QT], in_=q_src[:, :, (c + 2) * QT : (c + 3) * QT])
         nc.sync.dma_start(out=v_raw[:], in_=v[0].rearrange("(p j) e -> p j e", j=PACK))
 
         nc.vector.memset(warm_bf[:].bitcast(I32), 0)
@@ -319,22 +331,30 @@ def tile_rows_sink_cap_gqa_kernel(tc, qT, kT, t, v, sink, out):
                 for n in range(2):
                     score_pass(bank[:, n, :], 0, c, 2 * pair + n)
                 nc.scalar.activation(
-                    out=capped_rows[c // 2][:, c % 2, 2 * pair : 2 * pair + 2, :], in_=bank[:, 0:2, :], func=ACT.Tanh, scale=1.0 / CAP
+                    out=capped0[:, 2 * pair : 2 * pair + 2, :], in_=bank[:, 0:2, :], func=ACT.Tanh, scale=1.0 / CAP
                 )
 
-        def first_exp(c):
-            for pair in range(2):
-                places = slice(2 * pair, 2 * pair + 2)
-                nc.scalar.activation(
-                    out=p_rows[c // 2][:, c % 2, places, :], in_=capped_rows[c // 2][:, c % 2, places, :], func=ACT.Exp, scale=CAP
-                )
+        def first_exp(pair):
+            places = slice(2 * pair, 2 * pair + 2)
+            nc.scalar.activation(out=p_rows[:, places, :], in_=capped0[:, places, :], func=ACT.Exp, scale=CAP)
+
+        def head0_cap(c):
+            bank = score_banks[0 if c % 2 else H]
+            for r in range(PACK):
+                score_pass(bank[:, r, :], 0, c, r)
+            nc.scalar.activation(
+                out=head0_capped[c][:], in_=bank[:].rearrange("p r q -> p q r"), func=ACT.Tanh, scale=1.0 / CAP
+            )
+
+        def head0_exp(c):
+            nc.scalar.activation(out=head0_p[c][:], in_=head0_capped[c][:], func=ACT.Exp, scale=CAP)
 
         first_cap(0)
+        first_exp(0)
         nc.scalar.activation(out=t_inv[:], in_=t_guess[:], func=ACT.Exp, scale=-1.0)
         nc.scalar.activation(out=t_sign[:], in_=t_sb[:], func=ACT.Sign)
-        first_exp(0)
-        first_cap(1)
         first_exp(1)
+        head0_cap(1)
         for g in OTHER_HEADS:
             nc.sync.dma_start(out=k_mx[g * ROWS : (g + 1) * ROWS, :], in_=k_mx[tile0, :])
         with nc.allow_non_contiguous_dma(reason="one sink a query row"):
@@ -342,10 +362,15 @@ def tile_rows_sink_cap_gqa_kernel(tc, qT, kT, t, v, sink, out):
         for rows in (slice(ROWS, 3 * ROWS), slice(3 * ROWS, P)):
             nc.sync.dma_start(out=q_raw[0][rows], in_=q_src[rows, :, 0 : NQ // 2])
         round_q(2)
-        round_q(3)
         quantize_q(2)
+        round_q(3)
         nc.vector.tensor_tensor(out=t_near1[:], in0=t_inv[:], in1=t_abs[:], op=ALU.mult)
         quantize_q(3)
+        head0_cap(2)
+        head0_exp(1)
+        head0_cap(3)
+        head0_exp(2)
+        head0_exp(3)
         nc.vector.tensor_scalar(out=t_rest[:], in0=t_near1[:], scalar1=-1.0, scalar2=None, op0=ALU.add)
         nc.vector.tensor_tensor(
             out=v_bf[:],
@@ -366,9 +391,6 @@ def tile_rows_sink_cap_gqa_kernel(tc, qT, kT, t, v, sink, out):
         quantize_w(0, 1)
         ln_step(4)
 
-        for c in (2, 3):
-            first_cap(c)
-            first_exp(c)
 
         member = {unit: (i, n) for i, g in enumerate(GROUPS) for n, unit in enumerate(g)}
         turn = [member[unit] for unit in TURNS]

@@ -346,15 +346,25 @@ def tile_rows_sink_cap_gqa_kernel(tc, qT, kT, t, v, sink, out):
                 out=head0_capped[c][:], in_=bank[:].rearrange("p r q -> p q r"), func=ACT.Tanh, scale=1.0 / CAP
             )
 
+        def warm_rows(rounds):
+            for rep in range(rounds):
+                for g in OTHER_HEADS:
+                    rows = slice(ROWS * g, ROWS * (g + 1))
+                    whole_pass(
+                        score_banks[g][:, 0, :], warm_codes[rows], warm_scales[rows], warm_codes[rows], warm_scales[rows]
+                    )
+
         def head0_exp(c):
             nc.scalar.activation(out=head0_p[c][:], in_=head0_capped[c][:], func=ACT.Exp, scale=CAP)
 
         first_cap(0)
+        warm_rows(4)
         first_exp(0)
         nc.scalar.activation(out=t_inv[:], in_=t_guess[:], func=ACT.Exp, scale=-1.0)
         nc.scalar.activation(out=t_sign[:], in_=t_sb[:], func=ACT.Sign)
         first_exp(1)
         head0_cap(1)
+        warm_rows(4)
         for g in OTHER_HEADS:
             nc.sync.dma_start(out=k_mx[g * ROWS : (g + 1) * ROWS, :], in_=k_mx[tile0, :])
         with nc.allow_non_contiguous_dma(reason="one sink a query row"):
@@ -367,6 +377,7 @@ def tile_rows_sink_cap_gqa_kernel(tc, qT, kT, t, v, sink, out):
         nc.vector.tensor_tensor(out=t_near1[:], in0=t_inv[:], in1=t_abs[:], op=ALU.mult)
         quantize_q(3)
         head0_cap(2)
+        warm_rows(4)
         head0_exp(1)
         head0_cap(3)
         head0_exp(2)

@@ -37,10 +37,6 @@ GROUPS = HEAD0_GROUPS + BY_PLACE + SUMMED
 FIRST_SUMMED = len(GROUPS) - len(SUMMED)
 Y_BANKS = 3
 
-WARM_START = 22
-WARM_LONG_GAP = 4
-WARM_SHORT_GAP = 2
-
 
 def tile_rows_sink_cap_gqa_kernel(tc, qT, kT, t, v, sink, out):
     nc = tc.nc
@@ -73,9 +69,6 @@ def tile_rows_sink_cap_gqa_kernel(tc, qT, kT, t, v, sink, out):
         k_mx = sb.tile([P, N + N // PACK], I32, align_bytes=64)
         k_codes = k_mx[:, 0:N]
         k_scales = k_mx[:, N:].bitcast(U8)
-        warm_bf = sb.tile([P, QT * PACK], BF16, align_bytes=64)
-        warm_codes = sb.tile([P, QT], I32, align_bytes=64)
-        warm_scales = sb.tile([P, QT], U8, align_bytes=64)
         v_bf = sb.tile([P, D, PACK], BF16, align_bytes=64)
         v_codes = sb.tile([P, D], I32, align_bytes=64)
         v_scales = sb.tile([P, D], U8, align_bytes=64)
@@ -251,11 +244,6 @@ def tile_rows_sink_cap_gqa_kernel(tc, qT, kT, t, v, sink, out):
             dst = y_banks[i % Y_BANKS][:, sorted(GROUPS[i]).index(GROUPS[i][n]), :]
             whole_pass(dst, w_codes[i][:, n, :], w_scales[i][:, n, :], v_codes[:], v_scales[:])
 
-        def keep_warm(i, bank_of, passes):
-            dst = y_banks[bank_of % Y_BANKS][:, PACK - 1, :]
-            for rep in range(passes):
-                whole_pass(dst, w_codes[i][:, 0, :], w_scales[i][:, 0, :], v_codes[:], v_scales[:])
-
         def units_in_out(i):
             first, final = [CHUNKS * h + c for h, c in (min(GROUPS[i]), max(GROUPS[i]))]
             return slice(first, final + 1, max(final - first, 1))
@@ -299,13 +287,7 @@ def tile_rows_sink_cap_gqa_kernel(tc, qT, kT, t, v, sink, out):
             nc.sync.dma_start(out=q_raw[1][:, :, c * QT : (c + 1) * QT], in_=q_src[:, :, (c + 2) * QT : (c + 3) * QT])
         nc.sync.dma_start(out=v_raw[:], in_=v[0].rearrange("(p j) e -> p j e", j=PACK))
 
-        nc.vector.memset(warm_bf[:].bitcast(I32), 0)
         nc.vector.memset(k_mx[tile0, N:], 0)
-        nc.vector.quantize_mx(out=warm_codes[:].bitcast(FP8X4), scales=warm_scales[:], in_=warm_bf[:])
-        for rep in range(WARM_START):
-            whole_pass(
-                y_banks[Y_BANKS - 1][:, PACK - 1, :], warm_codes[:], warm_scales[:], warm_codes[:], warm_scales[:]
-            )
 
         round_q(0, early=True)
         round_k(1, 0, nc.scalar.copy)
@@ -346,25 +328,15 @@ def tile_rows_sink_cap_gqa_kernel(tc, qT, kT, t, v, sink, out):
                 out=head0_capped[c][:], in_=bank[:].rearrange("p r q -> p q r"), func=ACT.Tanh, scale=1.0 / CAP
             )
 
-        def warm_rows(rounds):
-            for rep in range(rounds):
-                for g in OTHER_HEADS:
-                    rows = slice(ROWS * g, ROWS * (g + 1))
-                    whole_pass(
-                        score_banks[g][:, 0, :], warm_codes[rows], warm_scales[rows], warm_codes[rows], warm_scales[rows]
-                    )
-
         def head0_exp(c):
             nc.scalar.activation(out=head0_p[c][:], in_=head0_capped[c][:], func=ACT.Exp, scale=CAP)
 
         first_cap(0)
-        warm_rows(4)
         first_exp(0)
         nc.scalar.activation(out=t_inv[:], in_=t_guess[:], func=ACT.Exp, scale=-1.0)
         nc.scalar.activation(out=t_sign[:], in_=t_sb[:], func=ACT.Sign)
         first_exp(1)
         head0_cap(1)
-        warm_rows(4)
         for g in OTHER_HEADS:
             nc.sync.dma_start(out=k_mx[g * ROWS : (g + 1) * ROWS, :], in_=k_mx[tile0, :])
         with nc.allow_non_contiguous_dma(reason="one sink a query row"):
@@ -377,7 +349,6 @@ def tile_rows_sink_cap_gqa_kernel(tc, qT, kT, t, v, sink, out):
         nc.vector.tensor_tensor(out=t_near1[:], in0=t_inv[:], in1=t_abs[:], op=ALU.mult)
         quantize_q(3)
         head0_cap(2)
-        warm_rows(4)
         head0_exp(1)
         head0_cap(3)
         head0_exp(2)
@@ -462,12 +433,10 @@ def tile_rows_sink_cap_gqa_kernel(tc, qT, kT, t, v, sink, out):
         cap(single2, 0)
         values(placed, 0)
         values(placed, 1)
-        keep_warm(placed, pair2, WARM_LONG_GAP)
         add_ln(single1, 0)
         for n in range(2):
             quantize_w(pair1, n)
             values(pair1, n)
-        keep_warm(pair1, pair2, WARM_SHORT_GAP)
         add_sink(placed)
         add_ln(single2, 0)
         weigh_summed(pair2, 0)
@@ -482,7 +451,6 @@ def tile_rows_sink_cap_gqa_kernel(tc, qT, kT, t, v, sink, out):
         quantize_w(pair2, 1)
         values(pair2, 1)
         divide(placed)
-        keep_warm(pair1, single1, WARM_SHORT_GAP)
         invert(pair1)
         quantize_w(single1, 0)
         values(single1, 0)

@@ -30,12 +30,14 @@ LN_DEGREE = 5
 
 OTHER_HEADS = (2, 3, 1)
 TURNS = [(h, c) for c in (2, 3, 0, 1) for h in OTHER_HEADS]
-HEAD0_GROUPS = [[(0, 0), (0, 1)], [(0, 2), (0, 3)]]
+MULTIPLIED = [[(0, 0), (0, 1)], [(0, 2), (0, 3)]]
 BY_PLACE = [TURNS[u : u + 2] for u in (0, 3, 6)]
-SUMMED = [[TURNS[5], TURNS[8]], [TURNS[2], TURNS[9]], [TURNS[10]], [TURNS[11]]]
-GROUPS = HEAD0_GROUPS + BY_PLACE + SUMMED
+SUMMED = [[TURNS[2], TURNS[5]], [TURNS[8], TURNS[9]], [TURNS[10]], [TURNS[11]]]
+GROUPS = MULTIPLIED + BY_PLACE + SUMMED
 FIRST_SUMMED = len(GROUPS) - len(SUMMED)
+FIRST_BY_PLACE = len(MULTIPLIED)
 Y_BANKS = 3
+HEAD0_FILLS = ((0, 2), (2, 4), (4, 7), (7, 10), (10, 13), (13, 16))
 
 
 def tile_rows_sink_cap_gqa_kernel(tc, qT, kT, t, v, sink, out):
@@ -79,12 +81,10 @@ def tile_rows_sink_cap_gqa_kernel(tc, qT, kT, t, v, sink, out):
                 for i in range(first, end)
             }
 
-        capped_rows = per_group("capped_rows", [PACK, QT], F32, first=2, end=FIRST_SUMMED)
-        w_rows = per_group("w_rows", [PACK, QT], BF16, first=2, end=FIRST_SUMMED)
-        p_rows = sb.tile([P, PACK, QT], F32, align_bytes=64)
-        capped0 = sb.tile([P, PACK, QT], F32, align_bytes=64)
-        head0_capped = {c: sb.tile([P, QT, PACK], F32, align_bytes=64, name="head0_capped%d" % c) for c in (1, 2, 3)}
-        head0_p = {c: sb.tile([P, QT, PACK], F32, align_bytes=64, name="head0_p%d" % c) for c in (1, 2, 3)}
+        head0_rows = sb.tile([P, CHUNKS * PACK, QT], F32)
+        p_rows = sb.tile([P, CHUNKS * PACK, QT], F32)
+        capped_rows = per_group("capped_rows", [PACK, QT], F32, first=FIRST_BY_PLACE, end=FIRST_SUMMED)
+        w_rows = per_group("w_rows", [PACK, QT], BF16, first=FIRST_BY_PLACE, end=FIRST_SUMMED)
         capped_words = per_group("capped_words", [QT, PACK], F32, first=FIRST_SUMMED)
         logits = per_group("logits", [QT, PACK], F32, first=FIRST_SUMMED)
         w_bf = per_group("w_bf", [QT, PACK], BF16)
@@ -153,16 +153,31 @@ def tile_rows_sink_cap_gqa_kernel(tc, qT, kT, t, v, sink, out):
                 stop=True,
             )
 
-        def cap_head0_place(i, r):
-            bank = score_banks[H if r % 2 else 0]
-            for n, (h, c) in enumerate(GROUPS[i]):
-                score_pass(bank[:, n, :], h, c, r)
-            nc.scalar.activation(out=capped_rows[i][:, :, r, :], in_=bank[:, 0:2, :], func=ACT.Tanh, scale=1.0 / CAP)
-
         def scores(i, n):
             h, c = GROUPS[i][n]
             for r in range(PACK):
                 score_pass(score_banks[h][:, r, :], h, c, r)
+
+        def head0_scores(fill):
+            first, end = HEAD0_FILLS[fill]
+            for row in range(first, end):
+                score_pass(score_banks[H * (fill % 2)][:, row - first, :], 0, row // PACK, row % PACK)
+
+        def head0_cap(fill):
+            first, end = HEAD0_FILLS[fill]
+            src = score_banks[H * (fill % 2)][:, 0 : end - first, :]
+            nc.scalar.activation(out=head0_rows[:, first:end, :], in_=src, func=ACT.Tanh, scale=1.0 / CAP)
+
+        def head0_exp(first, end):
+            nc.scalar.activation(out=p_rows[:, first:end, :], in_=head0_rows[:, first:end, :], func=ACT.Exp, scale=CAP)
+
+        def multiply(c):
+            nc.vector.tensor_tensor(
+                out=w_bf[c // 2][:, c % 2].rearrange("p (c i) r -> p c r i", i=WALK),
+                in0=p_rows[:, PACK * c : PACK * (c + 1), :].rearrange("p r (c i) -> p c r i", i=WALK),
+                in1=t_abs[:].unsqueeze(1).unsqueeze(3).to_broadcast([P, QT // WALK, PACK, WALK]),
+                op=ALU.mult,
+            )
 
         def cap(i, n):
             bank = score_banks[GROUPS[i][n][0]]
@@ -181,26 +196,17 @@ def tile_rows_sink_cap_gqa_kernel(tc, qT, kT, t, v, sink, out):
                 bias=t_ln[:, r : r + 1],
             )
 
-        def interleave(i, n):
-            if i < 2 and (i, n) != (0, 0):
-                nc.vector.tensor_tensor(
-                    out=w_bf[i][:, n],
-                    in0=head0_p[2 * i + n][:],
-                    in1=t_abs[:].unsqueeze(1).to_broadcast([P, QT, PACK]),
-                    op=ALU.mult,
-                )
-                return
-            if i < 2:
-                nc.vector.tensor_tensor(
-                    out=w_bf[i][:, n].rearrange("p (c i) r -> p c r i", i=WALK),
-                    in0=p_rows[:].rearrange("p r (c i) -> p c r i", i=WALK),
-                    in1=t_abs[:].unsqueeze(1).unsqueeze(3).to_broadcast([P, QT // WALK, PACK, WALK]),
-                    op=ALU.mult,
-                )
-                return
+        def interleave(i):
             nc.vector.tensor_copy(
-                out=w_bf[i][:, n].rearrange("p (c i) r -> p c r i", i=WALK),
-                in_=w_rows[i][:, n].rearrange("p r (c i) -> p c r i", i=WALK),
+                out=w_bf[i][:].rearrange("p n (c i) r -> p n c r i", i=WALK),
+                in_=w_rows[i][:].rearrange("p n r (c i) -> p n c r i", i=WALK),
+            )
+
+        def quantize_group(i):
+            nc.vector.quantize_mx(
+                out=w_codes[i][:].rearrange("p n q -> p (n q)").bitcast(FP8X4),
+                scales=w_scales[i][:].rearrange("p n q -> p (n q)"),
+                in_=w_bf[i][:].rearrange("p n q r -> p (n q r)"),
             )
 
         def ln_step(k):
@@ -300,79 +306,22 @@ def tile_rows_sink_cap_gqa_kernel(tc, qT, kT, t, v, sink, out):
         round_k(1, 1)
         for r in range(PACK):
             quantize_k(r)
-        nc.vector.scalar_tensor_tensor(
-            out=t_abs[:], in0=t_sb[:], scalar=-1.0, in1=t_sb[:], op0=ALU.mult, op1=ALU.max
-        )
         quantize_q(1, early=True)
-        nc.vector.tensor_scalar(
-            out=t_guess[:], in0=t_abs[:].bitcast(I32), scalar1=BITS_TO_LN, scalar2=BITS_OFFSET, op0=ALU.mult, op1=ALU.add
-        )
-
-        def first_cap(c):
-            for pair, bank in enumerate((score_banks[0], score_banks[H])):
-                for n in range(2):
-                    score_pass(bank[:, n, :], 0, c, 2 * pair + n)
-                nc.scalar.activation(
-                    out=capped0[:, 2 * pair : 2 * pair + 2, :], in_=bank[:, 0:2, :], func=ACT.Tanh, scale=1.0 / CAP
-                )
-
-        def first_exp(pair):
-            places = slice(2 * pair, 2 * pair + 2)
-            nc.scalar.activation(out=p_rows[:, places, :], in_=capped0[:, places, :], func=ACT.Exp, scale=CAP)
-
-        def head0_cap(c):
-            bank = score_banks[0 if c % 2 else H]
-            for r in range(PACK):
-                score_pass(bank[:, r, :], 0, c, r)
-            nc.scalar.activation(
-                out=head0_capped[c][:], in_=bank[:].rearrange("p r q -> p q r"), func=ACT.Tanh, scale=1.0 / CAP
-            )
-
-        def head0_exp(c):
-            nc.scalar.activation(out=head0_p[c][:], in_=head0_capped[c][:], func=ACT.Exp, scale=CAP)
-
-        first_cap(0)
-        first_exp(0)
-        nc.scalar.activation(out=t_inv[:], in_=t_guess[:], func=ACT.Exp, scale=-1.0)
-        nc.scalar.activation(out=t_sign[:], in_=t_sb[:], func=ACT.Sign)
-        first_exp(1)
-        head0_cap(1)
         for g in OTHER_HEADS:
             nc.sync.dma_start(out=k_mx[g * ROWS : (g + 1) * ROWS, :], in_=k_mx[tile0, :])
         with nc.allow_non_contiguous_dma(reason="one sink a query row"):
             nc.sync.dma_start(out=sink_sb[:], in_=sink.rearrange("h (c p) o -> p (h c o)", p=QT))
         for rows in (slice(ROWS, 3 * ROWS), slice(3 * ROWS, P)):
             nc.sync.dma_start(out=q_raw[0][rows], in_=q_src[rows, :, 0 : NQ // 2])
+        nc.vector.scalar_tensor_tensor(
+            out=t_abs[:], in0=t_sb[:], scalar=-1.0, in1=t_sb[:], op0=ALU.mult, op1=ALU.max
+        )
         round_q(2)
+        nc.vector.tensor_scalar(
+            out=t_guess[:], in0=t_abs[:].bitcast(I32), scalar1=BITS_TO_LN, scalar2=BITS_OFFSET, op0=ALU.mult, op1=ALU.add
+        )
         quantize_q(2)
         round_q(3)
-        nc.vector.tensor_tensor(out=t_near1[:], in0=t_inv[:], in1=t_abs[:], op=ALU.mult)
-        quantize_q(3)
-        head0_cap(2)
-        head0_exp(1)
-        head0_cap(3)
-        head0_exp(2)
-        head0_exp(3)
-        nc.vector.tensor_scalar(out=t_rest[:], in0=t_near1[:], scalar1=-1.0, scalar2=None, op0=ALU.add)
-        nc.vector.tensor_tensor(
-            out=v_bf[:],
-            in0=v_raw[:].rearrange("p j e -> p e j"),
-            in1=t_sign[:].unsqueeze(1).to_broadcast([P, D, PACK]),
-            op=ALU.mult,
-        )
-        ln_step(0)
-        interleave(0, 0)
-        nc.vector.quantize_mx(
-            out=v_codes[:].bitcast(FP8X4), scales=v_scales[:], in_=v_bf[:].rearrange("p e j -> p (e j)")
-        )
-        ln_step(1)
-        interleave(0, 1)
-        ln_step(2)
-        quantize_w(0, 0)
-        ln_step(3)
-        quantize_w(0, 1)
-        ln_step(4)
-
 
         member = {unit: (i, n) for i, g in enumerate(GROUPS) for n, unit in enumerate(g)}
         turn = [member[unit] for unit in TURNS]
@@ -383,32 +332,71 @@ def tile_rows_sink_cap_gqa_kernel(tc, qT, kT, t, v, sink, out):
             if u + ahead < len(turn):
                 scores(*turn[u + ahead])
 
-        def finish_by_place(i):
-            interleave(i, 0)
-            invert(i - 1)
-            interleave(i, 1)
-            divide(i - 1)
-            quantize_w(i, 0)
-            quantize_w(i, 1)
-
+        head0_scores(0)
+        head0_scores(1)
+        head0_cap(0)
+        head0_scores(2)
+        head0_cap(1)
+        head0_scores(3)
+        head0_exp(0, 2)
+        head0_exp(2, 4)
+        nc.scalar.activation(out=t_inv[:], in_=t_guess[:], func=ACT.Exp, scale=-1.0)
+        nc.scalar.activation(out=t_sign[:], in_=t_sb[:], func=ACT.Sign)
+        nc.vector.tensor_tensor(out=t_near1[:], in0=t_inv[:], in1=t_abs[:], op=ALU.mult)
+        quantize_q(3)
+        nc.vector.tensor_scalar(out=t_rest[:], in0=t_near1[:], scalar1=-1.0, scalar2=None, op0=ALU.add)
+        head0_cap(2)
+        head0_scores(4)
+        head0_cap(3)
+        head0_scores(5)
+        head0_exp(4, 7)
+        head0_exp(7, 8)
+        head0_cap(4)
+        head0_cap(5)
+        head0_exp(8, 12)
+        head0_exp(12, 16)
         for u in range(ahead):
             scores(*turn[u])
+
+        multiply(0)
+        ln_step(0)
+        quantize_w(0, 0)
+        ln_step(1)
+        nc.vector.tensor_tensor(
+            out=v_bf[:],
+            in0=v_raw[:].rearrange("p j e -> p e j"),
+            in1=t_sign[:].unsqueeze(1).to_broadcast([P, D, PACK]),
+            op=ALU.mult,
+        )
+        ln_step(2)
+        nc.vector.quantize_mx(
+            out=v_codes[:].bitcast(FP8X4), scales=v_scales[:], in_=v_bf[:].rearrange("p e j -> p (e j)")
+        )
+        ln_step(3)
+        multiply(1)
+        ln_step(4)
+        quantize_w(0, 1)
         values(0, 0)
         values(0, 1)
-        interleave(1, 0)
-        interleave(1, 1)
+        multiply(2)
+        multiply(3)
         add_sink(0)
-        quantize_w(1, 0)
+        quantize_group(1)
         invert(0)
-        quantize_w(1, 1)
         round_q(0)
         divide(0)
         round_q(1)
         quantize_q(0)
         quantize_q(1)
 
-        for i in range(len(HEAD0_GROUPS), FIRST_SUMMED):
-            u = ahead * (i - len(HEAD0_GROUPS))
+        def finish_by_place(i):
+            invert(i - 1)
+            interleave(i)
+            divide(i - 1)
+            quantize_group(i)
+
+        for i in range(FIRST_BY_PLACE, FIRST_SUMMED):
+            u = ahead * (i - FIRST_BY_PLACE)
             cap_and_refill(u)
             cap_and_refill(u + 1)
             values(i - 1, 0)

@@ -21,6 +21,7 @@ PACK = 4
 ROWS = D // PACK
 QT = 128
 CHUNKS = NQ // QT
+EARLY = 3
 K_PIECES = ((0, 256), (256, 384), (384, 512))
 WALK = 4
 
@@ -29,7 +30,7 @@ BITS_OFFSET = -127.0 * math.log(2.0) + 0.0298
 LN_DEGREE = 5
 
 OTHER_HEADS = (2, 3, 1)
-TURNS = [(h, c) for c in (2, 3, 0, 1) for h in OTHER_HEADS]
+TURNS = [(h, c) for c in (3, 2, 0, 1) for h in OTHER_HEADS]
 MULTIPLIED = [[(0, 0), (0, 1)], [(0, 2), (0, 3)]]
 BY_PLACE = [TURNS[u : u + 2] for u in (0, 3, 6)]
 SUMMED = [[TURNS[2], TURNS[5]], [TURNS[8], TURNS[9]], [TURNS[10]], [TURNS[11]]]
@@ -49,7 +50,8 @@ def tile_rows_sink_cap_gqa_kernel(tc, qT, kT, t, v, sink, out):
 
         q_src = qT.rearrange("h (p j) q -> (h p) j q", j=PACK)
         k_src = kT[0].rearrange("(p j) i -> p j i", j=PACK)
-        q_raw = [sb.tile([P, PACK, NQ // 2], F32, name="q_raw%d" % i) for i in range(2)]
+        q_raw = sb.tile([P, PACK, EARLY * QT], F32)
+        q_last = sb.tile([P, PACK, QT], F32)
         k_raw = [sb.tile([ROWS, PACK, b - a], F32, name="k_raw%d" % a) for a, b in K_PIECES]
         v_raw = sb.tile([P, PACK, D], F32)
         t_sb = sb.tile([P, PACK], F32)
@@ -63,7 +65,7 @@ def tile_rows_sink_cap_gqa_kernel(tc, qT, kT, t, v, sink, out):
         t_horner = [sb.tile([P, PACK], F32, name="t_horner%d" % i) for i in range(LN_DEGREE - 1)]
         sink_sb = sb.tile([P, H * CHUNKS], F32)
 
-        q_slots = range(CHUNKS + 2)
+        q_slots = range(CHUNKS + EARLY)
         q_bf = [sb.tile([P, QT, PACK], BF16, align_bytes=64, name="q_bf%d" % c) for c in q_slots]
         q_codes = [sb.tile([P, QT], I32, align_bytes=64, name="q_codes%d" % c) for c in q_slots]
         q_scales = [sb.tile([P, QT], U8, align_bytes=64, name="q_scales%d" % c) for c in q_slots]
@@ -98,11 +100,11 @@ def tile_rows_sink_cap_gqa_kernel(tc, qT, kT, t, v, sink, out):
 
         tile0 = slice(0, ROWS)
 
-        def round_q(c, early=False, copy=nc.vector.tensor_copy):
+        def round_q(c, early=False, copy=nc.vector.tensor_copy, q0=0, q1=QT):
             rows = tile0 if early else slice(0, P)
-            src = q_raw[c // 2][rows, :, (c % 2) * QT : (c % 2 + 1) * QT]
+            src = q_raw[rows, :, c * QT + q0 : c * QT + q1] if c < EARLY else q_last[rows]
             copy(
-                out=q_bf[c + CHUNKS * early][rows].rearrange("p (c i) j -> p c j i", i=WALK),
+                out=q_bf[c + CHUNKS * early][rows, q0:q1].rearrange("p (c i) j -> p c j i", i=WALK),
                 in_=src.rearrange("p j (c i) -> p c j i", i=WALK),
             )
 
@@ -131,7 +133,7 @@ def tile_rows_sink_cap_gqa_kernel(tc, qT, kT, t, v, sink, out):
         def score_pass(dst, h, c, r):
             rows = slice(ROWS * h, ROWS * (h + 1))
             cols = slice(r * P, (r + 1) * P)
-            slot = c + CHUNKS * (h == 0 and c < 2)
+            slot = c + CHUNKS * (h == 0 and c < EARLY)
             nc.tensor.matmul_mx(
                 out=dst,
                 lhsT=k_codes[rows, cols].bitcast(FP8X4),
@@ -284,13 +286,12 @@ def tile_rows_sink_cap_gqa_kernel(tc, qT, kT, t, v, sink, out):
                 )
             store(i)
 
-        nc.sync.dma_start(out=q_raw[0][tile0, :, 0:QT], in_=q_src[tile0, :, 0:QT])
+        nc.sync.dma_start(out=q_raw[tile0, :, 0:QT], in_=q_src[tile0, :, 0:QT])
         for i, (a, b) in enumerate(K_PIECES):
             nc.sync.dma_start(out=k_raw[i][:], in_=k_src[:, :, a:b])
-        nc.sync.dma_start(out=q_raw[0][tile0, :, QT : 2 * QT], in_=q_src[tile0, :, QT : 2 * QT])
+        nc.sync.dma_start(out=q_raw[tile0, :, QT:], in_=q_src[tile0, :, QT : EARLY * QT])
         nc.sync.dma_start(out=t_sb[:], in_=t.rearrange("(p j) o -> p (j o)", j=PACK))
-        for c in range(2):
-            nc.sync.dma_start(out=q_raw[1][:, :, c * QT : (c + 1) * QT], in_=q_src[:, :, (c + 2) * QT : (c + 3) * QT])
+        nc.sync.dma_start(out=q_last[:], in_=q_src[:, :, EARLY * QT :])
         nc.sync.dma_start(out=v_raw[:], in_=v[0].rearrange("(p j) e -> p j e", j=PACK))
 
         nc.vector.memset(k_mx[tile0, N:], 0)
@@ -298,7 +299,7 @@ def tile_rows_sink_cap_gqa_kernel(tc, qT, kT, t, v, sink, out):
         round_q(0, early=True)
         round_k(1, 0, nc.scalar.copy)
         round_k(1, 2, nc.scalar.copy)
-        round_q(1, early=True, copy=nc.scalar.copy)
+        round_q(1, early=True, copy=nc.scalar.copy, q1=QT // 2)
         quantize_q(0, early=True)
         round_k(0, 0)
         round_k(0, 1)
@@ -306,21 +307,26 @@ def tile_rows_sink_cap_gqa_kernel(tc, qT, kT, t, v, sink, out):
         round_k(1, 1)
         for r in range(PACK):
             quantize_k(r)
+        round_q(1, early=True, q0=QT // 2)
+        round_q(2, early=True)
         quantize_q(1, early=True)
+        nc.vector.scalar_tensor_tensor(
+            out=t_abs[:], in0=t_sb[:], scalar=-1.0, in1=t_sb[:], op0=ALU.mult, op1=ALU.max
+        )
+        quantize_q(2, early=True)
+        nc.vector.tensor_scalar(
+            out=t_guess[:], in0=t_abs[:].bitcast(I32), scalar1=BITS_TO_LN, scalar2=BITS_OFFSET, op0=ALU.mult, op1=ALU.add
+        )
         for g in OTHER_HEADS:
             nc.sync.dma_start(out=k_mx[g * ROWS : (g + 1) * ROWS, :], in_=k_mx[tile0, :])
         with nc.allow_non_contiguous_dma(reason="one sink a query row"):
             nc.sync.dma_start(out=sink_sb[:], in_=sink.rearrange("h (c p) o -> p (h c o)", p=QT))
-        for rows in (slice(ROWS, 3 * ROWS), slice(3 * ROWS, P)):
-            nc.sync.dma_start(out=q_raw[0][rows], in_=q_src[rows, :, 0 : NQ // 2])
-        nc.vector.scalar_tensor_tensor(
-            out=t_abs[:], in0=t_sb[:], scalar=-1.0, in1=t_sb[:], op0=ALU.mult, op1=ALU.max
-        )
-        round_q(2)
-        nc.vector.tensor_scalar(
-            out=t_guess[:], in0=t_abs[:].bitcast(I32), scalar1=BITS_TO_LN, scalar2=BITS_OFFSET, op0=ALU.mult, op1=ALU.add
-        )
-        quantize_q(2)
+        for rows, cols in (
+            (slice(ROWS, 3 * ROWS), slice(0, EARLY * QT)),
+            (slice(3 * ROWS, P), slice(2 * QT, EARLY * QT)),
+            (slice(3 * ROWS, P), slice(0, 2 * QT)),
+        ):
+            nc.sync.dma_start(out=q_raw[rows, :, cols], in_=q_src[rows, :, cols])
         round_q(3)
 
         member = {unit: (i, n) for i, g in enumerate(GROUPS) for n, unit in enumerate(g)}
@@ -342,8 +348,9 @@ def tile_rows_sink_cap_gqa_kernel(tc, qT, kT, t, v, sink, out):
         head0_exp(2, 4)
         nc.scalar.activation(out=t_inv[:], in_=t_guess[:], func=ACT.Exp, scale=-1.0)
         nc.scalar.activation(out=t_sign[:], in_=t_sb[:], func=ACT.Sign)
-        nc.vector.tensor_tensor(out=t_near1[:], in0=t_inv[:], in1=t_abs[:], op=ALU.mult)
         quantize_q(3)
+        nc.vector.tensor_tensor(out=t_near1[:], in0=t_inv[:], in1=t_abs[:], op=ALU.mult)
+        multiply(0)
         nc.vector.tensor_scalar(out=t_rest[:], in0=t_near1[:], scalar1=-1.0, scalar2=None, op0=ALU.add)
         head0_cap(2)
         head0_scores(4)
@@ -358,28 +365,29 @@ def tile_rows_sink_cap_gqa_kernel(tc, qT, kT, t, v, sink, out):
         for u in range(ahead):
             scores(*turn[u])
 
-        multiply(0)
-        ln_step(0)
         quantize_w(0, 0)
-        ln_step(1)
+        ln_step(0)
         nc.vector.tensor_tensor(
             out=v_bf[:],
             in0=v_raw[:].rearrange("p j e -> p e j"),
             in1=t_sign[:].unsqueeze(1).to_broadcast([P, D, PACK]),
             op=ALU.mult,
         )
-        ln_step(2)
+        ln_step(1)
         nc.vector.quantize_mx(
             out=v_codes[:].bitcast(FP8X4), scales=v_scales[:], in_=v_bf[:].rearrange("p e j -> p (e j)")
         )
-        ln_step(3)
+        ln_step(2)
         multiply(1)
-        ln_step(4)
+        ln_step(3)
         quantize_w(0, 1)
+        ln_step(4)
         values(0, 0)
         values(0, 1)
         multiply(2)
+        round_q(2)
         multiply(3)
+        quantize_q(2)
         add_sink(0)
         quantize_group(1)
         invert(0)

@@ -31,7 +31,7 @@ LN_DEGREE = 5
 
 OTHER_HEADS = (2, 3, 1)
 TURNS = [(h, c) for c in (3, 2, 0, 1) for h in OTHER_HEADS]
-MULTIPLIED = [[(0, 0), (0, 1)], [(0, 2), (0, 3)]]
+MULTIPLIED = [[(0, c) for c in range(CHUNKS)]]
 BY_PLACE = [TURNS[u : u + 2] for u in (0, 3, 6)]
 SUMMED = [[TURNS[2], TURNS[5]], [TURNS[8], TURNS[9]], [TURNS[10]], [TURNS[11]]]
 GROUPS = MULTIPLIED + BY_PLACE + SUMMED
@@ -175,7 +175,7 @@ def tile_rows_sink_cap_gqa_kernel(tc, qT, kT, t, v, sink, out):
 
         def multiply(c):
             nc.vector.tensor_tensor(
-                out=w_bf[c // 2][:, c % 2].rearrange("p (c i) r -> p c r i", i=WALK),
+                out=w_bf[0][:, c].rearrange("p (c i) r -> p c r i", i=WALK),
                 in0=p_rows[:, PACK * c : PACK * (c + 1), :].rearrange("p r (c i) -> p c r i", i=WALK),
                 in1=t_abs[:].unsqueeze(1).unsqueeze(3).to_broadcast([P, QT // WALK, PACK, WALK]),
                 op=ALU.mult,
@@ -254,7 +254,7 @@ def tile_rows_sink_cap_gqa_kernel(tc, qT, kT, t, v, sink, out):
 
         def units_in_out(i):
             first, final = [CHUNKS * h + c for h, c in (min(GROUPS[i]), max(GROUPS[i]))]
-            return slice(first, final + 1, max(final - first, 1))
+            return slice(first, final + 1, max((final - first) // max(len(GROUPS[i]) - 1, 1), 1))
 
         def add_sink(i):
             y = y_banks[i % Y_BANKS]
@@ -292,6 +292,9 @@ def tile_rows_sink_cap_gqa_kernel(tc, qT, kT, t, v, sink, out):
         nc.sync.dma_start(out=q_raw[tile0, :, QT:], in_=q_src[tile0, :, QT : EARLY * QT])
         nc.sync.dma_start(out=t_sb[:], in_=t.rearrange("(p j) o -> p (j o)", j=PACK))
         nc.sync.dma_start(out=q_last[:], in_=q_src[:, :, EARLY * QT :])
+        other_rows = (slice(ROWS, 3 * ROWS), slice(3 * ROWS, P))
+        for rows in other_rows:
+            nc.sync.dma_start(out=q_raw[rows, :, 2 * QT :], in_=q_src[rows, :, 2 * QT : EARLY * QT])
         nc.sync.dma_start(out=v_raw[:], in_=v[0].rearrange("(p j) e -> p j e", j=PACK))
 
         nc.vector.memset(k_mx[tile0, N:], 0)
@@ -321,12 +324,8 @@ def tile_rows_sink_cap_gqa_kernel(tc, qT, kT, t, v, sink, out):
             nc.sync.dma_start(out=k_mx[g * ROWS : (g + 1) * ROWS, :], in_=k_mx[tile0, :])
         with nc.allow_non_contiguous_dma(reason="one sink a query row"):
             nc.sync.dma_start(out=sink_sb[:], in_=sink.rearrange("h (c p) o -> p (h c o)", p=QT))
-        for rows, cols in (
-            (slice(ROWS, 3 * ROWS), slice(0, EARLY * QT)),
-            (slice(3 * ROWS, P), slice(2 * QT, EARLY * QT)),
-            (slice(3 * ROWS, P), slice(0, 2 * QT)),
-        ):
-            nc.sync.dma_start(out=q_raw[rows, :, cols], in_=q_src[rows, :, cols])
+        for rows in other_rows:
+            nc.sync.dma_start(out=q_raw[rows, :, 0 : 2 * QT], in_=q_src[rows, :, 0 : 2 * QT])
         round_q(3)
 
         member = {unit: (i, n) for i, g in enumerate(GROUPS) for n, unit in enumerate(g)}
@@ -367,35 +366,27 @@ def tile_rows_sink_cap_gqa_kernel(tc, qT, kT, t, v, sink, out):
 
         quantize_w(0, 0)
         ln_step(0)
+        round_q(2)
+        ln_step(1)
+        quantize_q(2)
+        ln_step(2)
         nc.vector.tensor_tensor(
             out=v_bf[:],
             in0=v_raw[:].rearrange("p j e -> p e j"),
             in1=t_sign[:].unsqueeze(1).to_broadcast([P, D, PACK]),
             op=ALU.mult,
         )
-        ln_step(1)
+        ln_step(3)
+        multiply(1)
+        ln_step(4)
         nc.vector.quantize_mx(
             out=v_codes[:].bitcast(FP8X4), scales=v_scales[:], in_=v_bf[:].rearrange("p e j -> p (e j)")
         )
-        ln_step(2)
-        multiply(1)
-        ln_step(3)
         quantize_w(0, 1)
-        ln_step(4)
-        values(0, 0)
-        values(0, 1)
         multiply(2)
-        round_q(2)
         multiply(3)
-        quantize_q(2)
-        add_sink(0)
-        quantize_group(1)
-        invert(0)
-        round_q(0)
-        divide(0)
-        round_q(1)
-        quantize_q(0)
-        quantize_q(1)
+        quantize_w(0, 2)
+        quantize_w(0, 3)
 
         def finish_by_place(i):
             invert(i - 1)
@@ -407,11 +398,17 @@ def tile_rows_sink_cap_gqa_kernel(tc, qT, kT, t, v, sink, out):
             u = ahead * (i - FIRST_BY_PLACE)
             cap_and_refill(u)
             cap_and_refill(u + 1)
-            values(i - 1, 0)
-            values(i - 1, 1)
+            for n in range(len(GROUPS[i - 1])):
+                values(i - 1, n)
             cap_and_refill(u + 2)
             add_ln(*turn[u + 2])
+            if i == FIRST_BY_PLACE:
+                round_q(0)
+                round_q(1)
+                quantize_q(0)
             add_sink(i - 1)
+            if i == FIRST_BY_PLACE:
+                quantize_q(1)
             weigh_place(i, 0)
             weigh_place(i, 1)
             if i + 1 == FIRST_SUMMED:

@@ -40,6 +40,9 @@ FIRST_BY_PLACE = len(MULTIPLIED)
 Y_BANKS = 3
 HEAD0_FILLS = ((0, 2), (2, 4), (4, 7), (7, 10), (10, 13), (13, 16))
 
+WARM_LONG_GAP = 4
+WARM_SHORT_GAP = 2
+
 
 def tile_rows_sink_cap_gqa_kernel(tc, qT, kT, t, v, sink, out):
     nc = tc.nc
@@ -252,6 +255,11 @@ def tile_rows_sink_cap_gqa_kernel(tc, qT, kT, t, v, sink, out):
             dst = y_banks[i % Y_BANKS][:, sorted(GROUPS[i]).index(GROUPS[i][n]), :]
             whole_pass(dst, w_codes[i][:, n, :], w_scales[i][:, n, :], v_codes[:], v_scales[:])
 
+        def keep_warm(i, bank_of, passes):
+            dst = y_banks[bank_of % Y_BANKS][:, PACK - 1, :]
+            for rep in range(passes):
+                whole_pass(dst, w_codes[i][:, 0, :], w_scales[i][:, 0, :], v_codes[:], v_scales[:])
+
         def units_in_out(i):
             first, final = [CHUNKS * h + c for h, c in (min(GROUPS[i]), max(GROUPS[i]))]
             return slice(first, final + 1, max((final - first) // max(len(GROUPS[i]) - 1, 1), 1))
@@ -426,10 +434,12 @@ def tile_rows_sink_cap_gqa_kernel(tc, qT, kT, t, v, sink, out):
         cap(single2, 0)
         values(placed, 0)
         values(placed, 1)
+        keep_warm(placed, pair2, WARM_LONG_GAP)
         add_ln(single1, 0)
         for n in range(2):
             quantize_w(pair1, n)
             values(pair1, n)
+        keep_warm(pair1, pair2, WARM_SHORT_GAP)
         add_sink(placed)
         add_ln(single2, 0)
         weigh_summed(pair2, 0)
@@ -444,6 +454,7 @@ def tile_rows_sink_cap_gqa_kernel(tc, qT, kT, t, v, sink, out):
         quantize_w(pair2, 1)
         values(pair2, 1)
         divide(placed)
+        keep_warm(pair1, single1, WARM_SHORT_GAP)
         invert(pair1)
         quantize_w(single1, 0)
         values(single1, 0)

@@ -22,7 +22,7 @@ ROWS = D // PACK
 QT = 128
 CHUNKS = NQ // QT
 EARLY = 3
-K_PIECES = ((0, 256), (256, 384), (384, 512))
+K_PIECES = ((0, 384), (384, 512))
 WALK = 4
 
 BITS_TO_LN = math.log(2.0) / 2.0**23
@@ -294,10 +294,12 @@ def tile_rows_sink_cap_gqa_kernel(tc, qT, kT, t, v, sink, out):
                 )
             store(i)
 
-        nc.sync.dma_start(out=q_raw[tile0, :, 0:QT], in_=q_src[tile0, :, 0:QT])
         for i, (a, b) in enumerate(K_PIECES):
             nc.sync.dma_start(out=k_raw[i][:], in_=k_src[:, :, a:b])
-        nc.sync.dma_start(out=q_raw[tile0, :, QT:], in_=q_src[tile0, :, QT : EARLY * QT])
+            if i == 0:
+                nc.sync.dma_start(out=q_raw[tile0, :, 0:QT], in_=q_src[tile0, :, 0:QT])
+        for c in range(1, EARLY):
+            nc.sync.dma_start(out=q_raw[tile0, :, c * QT : (c + 1) * QT], in_=q_src[tile0, :, c * QT : (c + 1) * QT])
         nc.sync.dma_start(out=t_sb[:], in_=t.rearrange("(p j) o -> p (j o)", j=PACK))
         nc.sync.dma_start(out=q_last[:], in_=q_src[:, :, EARLY * QT :])
         other_rows = (slice(ROWS, 3 * ROWS), slice(3 * ROWS, P))
@@ -307,18 +309,15 @@ def tile_rows_sink_cap_gqa_kernel(tc, qT, kT, t, v, sink, out):
 
         nc.vector.memset(k_mx[tile0, N:], 0)
 
-        round_q(0, early=True)
         round_k(1, 0, nc.scalar.copy)
-        round_k(1, 2, nc.scalar.copy)
-        round_q(1, early=True, copy=nc.scalar.copy, q1=QT // 2)
-        quantize_q(0, early=True)
+        round_k(1, 1, nc.scalar.copy)
+        round_q(1, early=True, copy=nc.scalar.copy)
         round_k(0, 0)
+        round_q(0, early=True)
         round_k(0, 1)
-        round_k(0, 2)
-        round_k(1, 1)
+        quantize_q(0, early=True)
         for r in range(PACK):
             quantize_k(r)
-        round_q(1, early=True, q0=QT // 2)
         round_q(2, early=True)
         quantize_q(1, early=True)
         nc.vector.scalar_tensor_tensor(

@@ -318,8 +318,8 @@ def tile_rows_sink_cap_gqa_kernel(tc, qT, kT, t, v, sink, out):
         quantize_q(0, early=True)
         for r in range(PACK):
             quantize_k(r)
-        round_q(2, early=True)
         quantize_q(1, early=True)
+        round_q(2, early=True)
         nc.vector.scalar_tensor_tensor(
             out=t_abs[:], in0=t_sb[:], scalar=-1.0, in1=t_sb[:], op0=ALU.mult, op1=ALU.max
         )

@@ -363,11 +363,11 @@ def tile_rows_sink_cap_gqa_kernel(tc, qT, kT, t, v, sink, out):
         head0_cap(3)
         head0_scores(5)
         head0_exp(4, 7)
-        head0_exp(7, 8)
+        head0_exp(7, 10)
         head0_cap(4)
         head0_cap(5)
-        head0_exp(8, 12)
-        head0_exp(12, 16)
+        head0_exp(10, 13)
+        head0_exp(13, 16)
         for u in range(ahead):
             scores(*turn[u])
 

@@ -11,7 +11,6 @@ F32 = mybir.dt.float32
 BF16 = mybir.dt.bfloat16
 I32 = mybir.dt.int32
 U8 = mybir.dt.uint8
-U32 = mybir.dt.uint32
 FP8X4 = mybir.dt.float8_e4m3fn_x4
 ACT = mybir.ActivationFunctionType
 ALU = mybir.AluOpType
@@ -22,7 +21,8 @@ ROWS = D // PACK
 QT = 128
 CHUNKS = NQ // QT
 EARLY = 3
-K_PIECES = ((0, 384), (384, 512))
+K_PIECES = ((0, 256), (256, 384), (384, 512))
+WINDOW = 64
 WALK = 4
 
 BITS_TO_LN = math.log(2.0) / 2.0**23
@@ -30,18 +30,12 @@ BITS_OFFSET = -127.0 * math.log(2.0) + 0.0298
 LN_DEGREE = 5
 
 OTHER_HEADS = (2, 3, 1)
-TURNS = [(h, c) for c in (3, 2, 0, 1) for h in OTHER_HEADS]
-MULTIPLIED = [[(0, c) for c in range(CHUNKS)]]
-BY_PLACE = [TURNS[u : u + 2] for u in (0, 3, 6)]
-SUMMED = [[TURNS[2], TURNS[5]], [TURNS[8], TURNS[9]], [TURNS[10]], [TURNS[11]]]
-GROUPS = MULTIPLIED + BY_PLACE + SUMMED
-FIRST_SUMMED = len(GROUPS) - len(SUMMED)
-FIRST_BY_PLACE = len(MULTIPLIED)
+TURN_CHUNKS = (3, 3, 3, 2, 2, 2, 1, 0, 0, 0, 1, 1)
+TURNS = [(OTHER_HEADS[u % 3], c) for u, c in enumerate(TURN_CHUNKS)]
+GROUPS = [[(0, c) for c in range(CHUNKS)], TURNS[0:3], TURNS[3:5], TURNS[5:7], TURNS[7:9], TURNS[9:10], TURNS[10:11], TURNS[11:12]]
+HEAD0, PLACED, FIRST_SUMMED = 0, 1, 2
 Y_BANKS = 3
 HEAD0_FILLS = ((0, 2), (2, 4), (4, 7), (7, 10), (10, 13), (13, 16))
-
-WARM_LONG_GAP = 4
-WARM_SHORT_GAP = 2
 
 
 def tile_rows_sink_cap_gqa_kernel(tc, qT, kT, t, v, sink, out):
@@ -72,7 +66,8 @@ def tile_rows_sink_cap_gqa_kernel(tc, qT, kT, t, v, sink, out):
         q_bf = [sb.tile([P, QT, PACK], BF16, align_bytes=64, name="q_bf%d" % c) for c in q_slots]
         q_codes = [sb.tile([P, QT], I32, align_bytes=64, name="q_codes%d" % c) for c in q_slots]
         q_scales = [sb.tile([P, QT], U8, align_bytes=64, name="q_scales%d" % c) for c in q_slots]
-        k_bf = [sb.tile([ROWS, 2, P, PACK], BF16, align_bytes=64, name="k_bf%d" % i) for i in range(2)]
+        k_win = [sb.tile([P, 2, WINDOW, PACK], BF16, align_bytes=64, name="k_win%d" % w) for w in range(2)]
+        k_late = sb.tile([ROWS, 2, P, PACK], BF16, align_bytes=64)
         k_mx = sb.tile([P, N + N // PACK], I32, align_bytes=64)
         k_codes = k_mx[:, 0:N]
         k_scales = k_mx[:, N:].bitcast(U8)
@@ -80,16 +75,16 @@ def tile_rows_sink_cap_gqa_kernel(tc, qT, kT, t, v, sink, out):
         v_codes = sb.tile([P, D], I32, align_bytes=64)
         v_scales = sb.tile([P, D], U8, align_bytes=64)
 
-        def per_group(name, shape, dtype, first=0, end=len(GROUPS)):
+        def per_group(name, shape, dtype, first=0):
             return {
                 i: sb.tile([P, len(GROUPS[i])] + shape, dtype, align_bytes=64, name="%s%d" % (name, i))
-                for i in range(first, end)
+                for i in range(first, len(GROUPS))
             }
 
         head0_rows = sb.tile([P, CHUNKS * PACK, QT], F32)
         p_rows = sb.tile([P, CHUNKS * PACK, QT], F32)
-        capped_rows = per_group("capped_rows", [PACK, QT], F32, first=FIRST_BY_PLACE, end=FIRST_SUMMED)
-        w_rows = per_group("w_rows", [PACK, QT], BF16, first=FIRST_BY_PLACE, end=FIRST_SUMMED)
+        capped_rows = sb.tile([P, len(GROUPS[PLACED]), PACK, QT], F32)
+        w_rows = sb.tile([P, len(GROUPS[PLACED]), PACK, QT], BF16)
         capped_words = per_group("capped_words", [QT, PACK], F32, first=FIRST_SUMMED)
         logits = per_group("logits", [QT, PACK], F32, first=FIRST_SUMMED)
         w_bf = per_group("w_bf", [QT, PACK], BF16)
@@ -102,6 +97,29 @@ def tile_rows_sink_cap_gqa_kernel(tc, qT, kT, t, v, sink, out):
         y_banks = [ps.tile([P, PACK, D], F32, name="y%d" % i) for i in range(Y_BANKS)]
 
         tile0 = slice(0, ROWS)
+        member = {unit: (i, n) for i, g in enumerate(GROUPS) for n, unit in enumerate(g)}
+        turn = [member[unit] for unit in TURNS]
+
+        def round_k(piece, first, end, copy=nc.vector.tensor_copy):
+            a, b = [x // PACK for x in K_PIECES[piece]]
+            src = k_raw[piece][:].rearrange("p j (s r) -> p s j r", r=PACK)[:, :, :, first:end]
+            if first < 2:
+                w = a // WINDOW
+                dst = k_win[w][tile0, first:end, a - w * WINDOW : b - w * WINDOW, :]
+            else:
+                dst = k_late[:, first - 2 : end - 2, a:b, :]
+            copy(out=dst.rearrange("p r s j -> p s j r"), in_=src)
+
+        def quantize_k(r, w=None):
+            if w is None:
+                rows, cols, src = tile0, slice(r * P, (r + 1) * P), k_late[:, r - 2]
+            else:
+                rows, cols, src = slice(0, P), slice(r * P + w * WINDOW, r * P + (w + 1) * WINDOW), k_win[w][:, r]
+            nc.vector.quantize_mx(
+                out=k_codes[rows, cols].bitcast(FP8X4),
+                scales=k_scales[rows, cols],
+                in_=src.rearrange("p s j -> p (s j)"),
+            )
 
         def round_q(c, early=False, copy=nc.vector.tensor_copy, q0=0, q1=QT):
             rows = tile0 if early else slice(0, P)
@@ -118,19 +136,6 @@ def tile_rows_sink_cap_gqa_kernel(tc, qT, kT, t, v, sink, out):
                 out=q_codes[slot][rows].bitcast(FP8X4),
                 scales=q_scales[slot][rows],
                 in_=q_bf[slot][rows].rearrange("p q j -> p (q j)"),
-            )
-
-        def round_k(pair, half, copy=nc.vector.tensor_copy):
-            src = k_raw[half][:].rearrange("p j (s r) -> p s j r", r=PACK)[:, :, :, 2 * pair : 2 * pair + 2]
-            dst = k_bf[pair][:, :, K_PIECES[half][0] // PACK : K_PIECES[half][1] // PACK, :]
-            copy(out=dst.rearrange("p r s j -> p s j r"), in_=src)
-
-        def quantize_k(r):
-            cols = slice(r * P, (r + 1) * P)
-            nc.vector.quantize_mx(
-                out=k_codes[tile0, cols].bitcast(FP8X4),
-                scales=k_scales[tile0, cols],
-                in_=k_bf[r // 2][tile0, r % 2].rearrange("p s j -> p (s j)"),
             )
 
         def score_pass(dst, h, c, r):
@@ -182,36 +187,6 @@ def tile_rows_sink_cap_gqa_kernel(tc, qT, kT, t, v, sink, out):
                 in0=p_rows[:, PACK * c : PACK * (c + 1), :].rearrange("p r (c i) -> p c r i", i=WALK),
                 in1=t_abs[:].unsqueeze(1).unsqueeze(3).to_broadcast([P, QT // WALK, PACK, WALK]),
                 op=ALU.mult,
-            )
-
-        def cap(i, n):
-            bank = score_banks[GROUPS[i][n][0]]
-            if i < FIRST_SUMMED:
-                dst, src = capped_rows[i][:, n], bank[:]
-            else:
-                dst, src = capped_words[i][:, n], bank[:].rearrange("p r q -> p q r")
-            nc.scalar.activation(out=dst, in_=src, func=ACT.Tanh, scale=1.0 / CAP)
-
-        def weigh_place(i, r):
-            nc.scalar.activation(
-                out=w_rows[i][:, :, r, :],
-                in_=capped_rows[i][:, :, r, :],
-                func=ACT.Exp,
-                scale=CAP,
-                bias=t_ln[:, r : r + 1],
-            )
-
-        def interleave(i):
-            nc.vector.tensor_copy(
-                out=w_bf[i][:].rearrange("p n (c i) r -> p n c r i", i=WALK),
-                in_=w_rows[i][:].rearrange("p n r (c i) -> p n c r i", i=WALK),
-            )
-
-        def quantize_group(i):
-            nc.vector.quantize_mx(
-                out=w_codes[i][:].rearrange("p n q -> p (n q)").bitcast(FP8X4),
-                scales=w_scales[i][:].rearrange("p n q -> p (n q)"),
-                in_=w_bf[i][:].rearrange("p n q r -> p (n q r)"),
             )
 
         def ln_step(k):
@@ -294,55 +269,90 @@ def tile_rows_sink_cap_gqa_kernel(tc, qT, kT, t, v, sink, out):
                 )
             store(i)
 
-        for i, (a, b) in enumerate(K_PIECES):
-            nc.sync.dma_start(out=k_raw[i][:], in_=k_src[:, :, a:b])
-            if i == 0:
-                nc.sync.dma_start(out=q_raw[tile0, :, 0:QT], in_=q_src[tile0, :, 0:QT])
-        for c in range(1, EARLY):
-            nc.sync.dma_start(out=q_raw[tile0, :, c * QT : (c + 1) * QT], in_=q_src[tile0, :, c * QT : (c + 1) * QT])
+        def cap(u):
+            i, n = turn[u]
+            bank = score_banks[TURNS[u][0]]
+            if i == PLACED:
+                dst, src = capped_rows[:, n], bank[:]
+            else:
+                dst, src = capped_words[i][:, n], bank[:].rearrange("p r q -> p q r")
+            nc.scalar.activation(out=dst, in_=src, func=ACT.Tanh, scale=1.0 / CAP)
+            if u + len(OTHER_HEADS) < len(TURNS):
+                scores(*turn[u + len(OTHER_HEADS)])
+
+        def weigh_place(r):
+            nc.scalar.activation(
+                out=w_rows[:, :, r, :], in_=capped_rows[:, :, r, :], func=ACT.Exp, scale=CAP, bias=t_ln[:, r : r + 1]
+            )
+
+        def weigh_group(i):
+            nc.scalar.activation(out=w_bf[i][:], in_=logits[i][:], func=ACT.Exp)
+
+        def interleave(first, end):
+            nc.vector.tensor_copy(
+                out=w_bf[PLACED][:, first:end].rearrange("p n (c i) r -> p n c r i", i=WALK),
+                in_=w_rows[:, first:end].rearrange("p n r (c i) -> p n c r i", i=WALK),
+            )
+
+        def quantize_and_values(i):
+            for n in range(len(GROUPS[i])):
+                quantize_w(i, n)
+                values(i, n)
+
+        def load_k(piece):
+            a, b = K_PIECES[piece]
+            nc.sync.dma_start(out=k_raw[piece][:], in_=k_src[:, :, a:b])
+
+        def load_q(rows, first, end):
+            nc.sync.dma_start(out=q_raw[rows, :, first * QT : end * QT], in_=q_src[rows, :, first * QT : end * QT])
+
+        load_k(0)
+        load_q(tile0, 0, 1)
+        load_k(1)
+        load_k(2)
+        load_q(tile0, 1, EARLY)
         nc.sync.dma_start(out=t_sb[:], in_=t.rearrange("(p j) o -> p (j o)", j=PACK))
         nc.sync.dma_start(out=q_last[:], in_=q_src[:, :, EARLY * QT :])
         other_rows = (slice(ROWS, 3 * ROWS), slice(3 * ROWS, P))
         for rows in other_rows:
-            nc.sync.dma_start(out=q_raw[rows, :, 2 * QT :], in_=q_src[rows, :, 2 * QT : EARLY * QT])
+            load_q(rows, 2, 3)
         nc.sync.dma_start(out=v_raw[:], in_=v[0].rearrange("(p j) e -> p j e", j=PACK))
 
+        for w in range(2):
+            nc.vector.memset(k_win[w][:], 0.0)
         nc.vector.memset(k_mx[tile0, N:], 0)
 
-        round_k(1, 0, nc.scalar.copy)
-        round_k(1, 1, nc.scalar.copy)
+        for piece in range(len(K_PIECES)):
+            round_k(piece, 2, 4, nc.scalar.copy)
         round_q(1, early=True, copy=nc.scalar.copy)
-        round_k(0, 0)
+        round_k(0, 0, 2)
         round_q(0, early=True)
-        round_k(0, 1)
+        round_k(1, 0, 2)
+        quantize_k(0, 0)
+        round_k(2, 0, 1)
+        round_k(2, 1, 2)
         quantize_q(0, early=True)
-        for r in range(PACK):
-            quantize_k(r)
-        quantize_q(1, early=True)
+        quantize_k(0, 1)
+        quantize_k(1, 0)
+        quantize_k(1, 1)
+        quantize_k(2)
+        quantize_k(3)
         round_q(2, early=True)
         nc.vector.scalar_tensor_tensor(
             out=t_abs[:], in0=t_sb[:], scalar=-1.0, in1=t_sb[:], op0=ALU.mult, op1=ALU.max
         )
-        quantize_q(2, early=True)
+        quantize_q(1, early=True)
         nc.vector.tensor_scalar(
             out=t_guess[:], in0=t_abs[:].bitcast(I32), scalar1=BITS_TO_LN, scalar2=BITS_OFFSET, op0=ALU.mult, op1=ALU.add
         )
+        quantize_q(2, early=True)
         for g in OTHER_HEADS:
             nc.sync.dma_start(out=k_mx[g * ROWS : (g + 1) * ROWS, :], in_=k_mx[tile0, :])
+        for rows in other_rows:
+            load_q(rows, 0, 2)
         with nc.allow_non_contiguous_dma(reason="one sink a query row"):
             nc.sync.dma_start(out=sink_sb[:], in_=sink.rearrange("h (c p) o -> p (h c o)", p=QT))
-        for rows in other_rows:
-            nc.sync.dma_start(out=q_raw[rows, :, 0 : 2 * QT], in_=q_src[rows, :, 0 : 2 * QT])
         round_q(3)
-
-        member = {unit: (i, n) for i, g in enumerate(GROUPS) for n, unit in enumerate(g)}
-        turn = [member[unit] for unit in TURNS]
-        ahead = len(OTHER_HEADS)
-
-        def cap_and_refill(u):
-            cap(*turn[u])
-            if u + ahead < len(turn):
-                scores(*turn[u + ahead])
 
         head0_scores(0)
         head0_scores(1)
@@ -355,8 +365,9 @@ def tile_rows_sink_cap_gqa_kernel(tc, qT, kT, t, v, sink, out):
         nc.scalar.activation(out=t_inv[:], in_=t_guess[:], func=ACT.Exp, scale=-1.0)
         nc.scalar.activation(out=t_sign[:], in_=t_sb[:], func=ACT.Sign)
         quantize_q(3)
-        nc.vector.tensor_tensor(out=t_near1[:], in0=t_inv[:], in1=t_abs[:], op=ALU.mult)
         multiply(0)
+        nc.vector.tensor_tensor(out=t_near1[:], in0=t_inv[:], in1=t_abs[:], op=ALU.mult)
+        round_q(2)
         nc.vector.tensor_scalar(out=t_rest[:], in0=t_near1[:], scalar1=-1.0, scalar2=None, op0=ALU.add)
         head0_cap(2)
         head0_scores(4)
@@ -367,106 +378,106 @@ def tile_rows_sink_cap_gqa_kernel(tc, qT, kT, t, v, sink, out):
         head0_cap(4)
         head0_cap(5)
         head0_exp(10, 13)
-        head0_exp(13, 16)
-        for u in range(ahead):
+        for u in range(len(OTHER_HEADS)):
             scores(*turn[u])
 
         quantize_w(0, 0)
         ln_step(0)
-        round_q(2)
-        ln_step(1)
         quantize_q(2)
-        ln_step(2)
+        ln_step(1)
         nc.vector.tensor_tensor(
             out=v_bf[:],
             in0=v_raw[:].rearrange("p j e -> p e j"),
             in1=t_sign[:].unsqueeze(1).to_broadcast([P, D, PACK]),
             op=ALU.mult,
         )
-        ln_step(3)
+        ln_step(2)
         multiply(1)
-        ln_step(4)
+        ln_step(3)
         nc.vector.quantize_mx(
             out=v_codes[:].bitcast(FP8X4), scales=v_scales[:], in_=v_bf[:].rearrange("p e j -> p (e j)")
         )
+        ln_step(4)
         quantize_w(0, 1)
         multiply(2)
-        multiply(3)
+        cap(0)
+        cap(1)
+        head0_exp(13, 16)
+        round_q(1)
         quantize_w(0, 2)
+        for n in range(CHUNKS - 1):
+            values(HEAD0, n)
+        round_q(0)
+        multiply(3)
+        quantize_q(1)
+        quantize_q(0)
         quantize_w(0, 3)
 
-        def finish_by_place(i):
-            invert(i - 1)
-            interleave(i)
-            divide(i - 1)
-            quantize_group(i)
-
-        for i in range(FIRST_BY_PLACE, FIRST_SUMMED):
-            u = ahead * (i - FIRST_BY_PLACE)
-            cap_and_refill(u)
-            cap_and_refill(u + 1)
-            for n in range(len(GROUPS[i - 1])):
-                values(i - 1, n)
-            cap_and_refill(u + 2)
-            add_ln(*turn[u + 2])
-            if i == FIRST_BY_PLACE:
-                round_q(0)
-                round_q(1)
-                quantize_q(0)
-            add_sink(i - 1)
-            if i == FIRST_BY_PLACE:
-                quantize_q(1)
-            weigh_place(i, 0)
-            weigh_place(i, 1)
-            if i + 1 == FIRST_SUMMED:
-                cap_and_refill(u + 3)
-                add_ln(*turn[u + 3])
-            weigh_place(i, 2)
-            weigh_place(i, 3)
-            finish_by_place(i)
-
-        placed = FIRST_SUMMED - 1
-        pair1, pair2, single1, single2 = range(FIRST_SUMMED, len(GROUPS))
+        pair1, pair2, pair3, single1, single2, last = range(FIRST_SUMMED, len(GROUPS))
         half_q = QT // 2
-        cap(single1, 0)
-        nc.scalar.activation(out=w_bf[pair1][:], in_=logits[pair1][:], func=ACT.Exp)
-        cap(single2, 0)
-        values(placed, 0)
-        values(placed, 1)
-        keep_warm(placed, pair2, WARM_LONG_GAP)
-        add_ln(single1, 0)
-        for n in range(2):
-            quantize_w(pair1, n)
-            values(pair1, n)
-        keep_warm(pair1, pair2, WARM_SHORT_GAP)
-        add_sink(placed)
-        add_ln(single2, 0)
-        weigh_summed(pair2, 0)
-        weigh_summed(pair2, 1)
-        weigh_summed(single1, 0)
-        weigh_summed(single2, 0, 0, half_q)
-        weigh_summed(single2, 0, half_q, QT)
-        invert(placed)
-        quantize_w(pair2, 0)
-        values(pair2, 0)
+        cap(2)
+        values(HEAD0, CHUNKS - 1)
+        cap(3)
+        add_ln(*turn[3])
+        cap(4)
+        add_ln(*turn[4])
+        add_sink(HEAD0)
+        invert(HEAD0)
+        for r in range(PACK):
+            weigh_place(r)
+        divide(HEAD0)
+        interleave(0, 2)
+        interleave(2, 3)
+        cap(5)
+        add_ln(*turn[5])
+        cap(6)
+        weigh_group(pair1)
+        add_ln(*turn[6])
+        quantize_and_values(PLACED)
+        cap(7)
+        quantize_and_values(pair1)
+        cap(8)
+        weigh_group(pair2)
+        add_ln(*turn[7])
+        add_sink(PLACED)
+        add_ln(*turn[8])
+        invert(PLACED)
         add_sink(pair1)
-        quantize_w(pair2, 1)
-        values(pair2, 1)
-        divide(placed)
-        keep_warm(pair1, single1, WARM_SHORT_GAP)
+        divide(PLACED)
         invert(pair1)
-        quantize_w(single1, 0)
-        values(single1, 0)
-        divide_on_scalar(pair1)
-        quantize_w(single2, 0, 0, half_q)
+        cap(9)
+        cap(10)
+        weigh_group(pair3)
+        add_ln(*turn[9])
+        quantize_and_values(pair2)
+        divide(pair1)
+        keep_warm(pair2, single1, 5)
+        add_ln(*turn[10])
         add_sink(pair2)
-        quantize_w(single2, 0, half_q, QT)
-        values(single2, 0)
+        quantize_and_values(pair3)
+        keep_warm(pair2, single1, 3)
         invert(pair2)
-        divide_on_scalar(pair2)
+        cap(11)
+        add_ln(*turn[11])
+        weigh_summed(single1, 0)
+        weigh_summed(single2, 0)
+        weigh_summed(last, 0, 0, half_q)
+        weigh_summed(last, 0, half_q, QT)
+        quantize_and_values(single1)
+        add_sink(pair3)
+        divide(pair2)
+        invert(pair3)
+        quantize_and_values(single2)
+        divide_on_scalar(pair3)
+        quantize_w(last, 0, 0, half_q)
         add_sink(single1)
+        quantize_w(last, 0, half_q, QT)
+        values(last, 0)
         invert(single1)
         divide_on_scalar(single1)
         add_sink(single2)
         invert(single2)
-        divide(single2)
+        divide_on_scalar(single2)
+        add_sink(last)
+        invert(last)
+        divide(last)

@@ -21,8 +21,7 @@ ROWS = D // PACK
 QT = 128
 CHUNKS = NQ // QT
 EARLY = 3
-K_PIECES = ((0, 256), (256, 384), (384, 512))
-WINDOW = 64
+K_PIECES = ((0, 384), (384, 512))
 WALK = 4
 
 BITS_TO_LN = math.log(2.0) / 2.0**23
@@ -66,8 +65,7 @@ def tile_rows_sink_cap_gqa_kernel(tc, qT, kT, t, v, sink, out):
         q_bf = [sb.tile([P, QT, PACK], BF16, align_bytes=64, name="q_bf%d" % c) for c in q_slots]
         q_codes = [sb.tile([P, QT], I32, align_bytes=64, name="q_codes%d" % c) for c in q_slots]
         q_scales = [sb.tile([P, QT], U8, align_bytes=64, name="q_scales%d" % c) for c in q_slots]
-        k_win = [sb.tile([P, 2, WINDOW, PACK], BF16, align_bytes=64, name="k_win%d" % w) for w in range(2)]
-        k_late = sb.tile([ROWS, 2, P, PACK], BF16, align_bytes=64)
+        k_bf = [sb.tile([ROWS, 2, P, PACK], BF16, align_bytes=64, name="k_bf%d" % i) for i in range(2)]
         k_mx = sb.tile([P, N + N // PACK], I32, align_bytes=64)
         k_codes = k_mx[:, 0:N]
         k_scales = k_mx[:, N:].bitcast(U8)
@@ -100,25 +98,17 @@ def tile_rows_sink_cap_gqa_kernel(tc, qT, kT, t, v, sink, out):
         member = {unit: (i, n) for i, g in enumerate(GROUPS) for n, unit in enumerate(g)}
         turn = [member[unit] for unit in TURNS]
 
-        def round_k(piece, first, end, copy=nc.vector.tensor_copy):
-            a, b = [x // PACK for x in K_PIECES[piece]]
-            src = k_raw[piece][:].rearrange("p j (s r) -> p s j r", r=PACK)[:, :, :, first:end]
-            if first < 2:
-                w = a // WINDOW
-                dst = k_win[w][tile0, first:end, a - w * WINDOW : b - w * WINDOW, :]
-            else:
-                dst = k_late[:, first - 2 : end - 2, a:b, :]
+        def round_k(pair, half, copy=nc.vector.tensor_copy):
+            src = k_raw[half][:].rearrange("p j (s r) -> p s j r", r=PACK)[:, :, :, 2 * pair : 2 * pair + 2]
+            dst = k_bf[pair][:, :, K_PIECES[half][0] // PACK : K_PIECES[half][1] // PACK, :]
             copy(out=dst.rearrange("p r s j -> p s j r"), in_=src)
 
-        def quantize_k(r, w=None):
-            if w is None:
-                rows, cols, src = tile0, slice(r * P, (r + 1) * P), k_late[:, r - 2]
-            else:
-                rows, cols, src = slice(0, P), slice(r * P + w * WINDOW, r * P + (w + 1) * WINDOW), k_win[w][:, r]
+        def quantize_k(r):
+            cols = slice(r * P, (r + 1) * P)
             nc.vector.quantize_mx(
-                out=k_codes[rows, cols].bitcast(FP8X4),
-                scales=k_scales[rows, cols],
-                in_=src.rearrange("p s j -> p (s j)"),
+                out=k_codes[tile0, cols].bitcast(FP8X4),
+                scales=k_scales[tile0, cols],
+                in_=k_bf[r // 2][tile0, r % 2].rearrange("p s j -> p (s j)"),
             )
 
         def round_q(c, early=False, copy=nc.vector.tensor_copy, q0=0, q1=QT):
@@ -309,8 +299,8 @@ def tile_rows_sink_cap_gqa_kernel(tc, qT, kT, t, v, sink, out):
         load_k(0)
         load_q(tile0, 0, 1)
         load_k(1)
-        load_k(2)
-        load_q(tile0, 1, EARLY)
+        load_q(tile0, 1, 2)
+        load_q(tile0, 2, 3)
         nc.sync.dma_start(out=t_sb[:], in_=t.rearrange("(p j) o -> p (j o)", j=PACK))
         nc.sync.dma_start(out=q_last[:], in_=q_src[:, :, EARLY * QT :])
         other_rows = (slice(ROWS, 3 * ROWS), slice(3 * ROWS, P))
@@ -318,34 +308,26 @@ def tile_rows_sink_cap_gqa_kernel(tc, qT, kT, t, v, sink, out):
             load_q(rows, 2, 3)
         nc.sync.dma_start(out=v_raw[:], in_=v[0].rearrange("(p j) e -> p j e", j=PACK))
 
-        for w in range(2):
-            nc.vector.memset(k_win[w][:], 0.0)
         nc.vector.memset(k_mx[tile0, N:], 0)
 
-        for piece in range(len(K_PIECES)):
-            round_k(piece, 2, 4, nc.scalar.copy)
+        round_k(1, 0, nc.scalar.copy)
+        round_k(1, 1, nc.scalar.copy)
         round_q(1, early=True, copy=nc.scalar.copy)
-        round_k(0, 0, 2)
+        round_k(0, 0)
         round_q(0, early=True)
-        round_k(1, 0, 2)
-        quantize_k(0, 0)
-        round_k(2, 0, 1)
-        round_k(2, 1, 2)
+        round_k(0, 1)
         quantize_q(0, early=True)
-        quantize_k(0, 1)
-        quantize_k(1, 0)
-        quantize_k(1, 1)
-        quantize_k(2)
-        quantize_k(3)
+        for r in range(PACK):
+            quantize_k(r)
+        quantize_q(1, early=True)
         round_q(2, early=True)
         nc.vector.scalar_tensor_tensor(
             out=t_abs[:], in0=t_sb[:], scalar=-1.0, in1=t_sb[:], op0=ALU.mult, op1=ALU.max
         )
-        quantize_q(1, early=True)
+        quantize_q(2, early=True)
         nc.vector.tensor_scalar(
             out=t_guess[:], in0=t_abs[:].bitcast(I32), scalar1=BITS_TO_LN, scalar2=BITS_OFFSET, op0=ALU.mult, op1=ALU.add
         )
-        quantize_q(2, early=True)
         for g in OTHER_HEADS:
             nc.sync.dma_start(out=k_mx[g * ROWS : (g + 1) * ROWS, :], in_=k_mx[tile0, :])
         for rows in other_rows:

@@ -29,9 +29,9 @@ BITS_OFFSET = -127.0 * math.log(2.0) + 0.0298
 LN_DEGREE = 5
 
 OTHER_HEADS = (2, 3, 1)
-TURN_CHUNKS = (3, 3, 3, 2, 2, 2, 1, 0, 0, 0, 1, 1)
+TURN_CHUNKS = (3, 3, 2, 2, 2, 3, 0, 0, 0, 1, 1, 1)
 TURNS = [(OTHER_HEADS[u % 3], c) for u, c in enumerate(TURN_CHUNKS)]
-GROUPS = [[(0, c) for c in range(CHUNKS)], TURNS[0:3], TURNS[3:5], TURNS[5:7], TURNS[7:9], TURNS[9:10], TURNS[10:11], TURNS[11:12]]
+GROUPS = [[(0, c) for c in range(CHUNKS)], TURNS[0:2], TURNS[2:5], TURNS[5:7], TURNS[7:9], TURNS[9:11], TURNS[11:12]]
 HEAD0, PLACED, FIRST_SUMMED = 0, 1, 2
 Y_BANKS = 3
 HEAD0_FILLS = ((0, 2), (2, 4), (4, 7), (7, 10), (10, 13), (13, 16))
@@ -196,12 +196,12 @@ def tile_rows_sink_cap_gqa_kernel(tc, qT, kT, t, v, sink, out):
                 op1=ALU.mult,
             )
 
-        def add_ln(i, n):
+        def add_ln(i, n, q0=0, q1=QT):
             nc.vector.scalar_tensor_tensor(
-                out=logits[i][:, n],
-                in0=capped_words[i][:, n],
+                out=logits[i][:, n, q0:q1],
+                in0=capped_words[i][:, n, q0:q1],
                 scalar=CAP,
-                in1=t_ln[:].unsqueeze(1).to_broadcast([P, QT, PACK]),
+                in1=t_ln[:].unsqueeze(1).to_broadcast([P, q1 - q0, PACK]),
                 op0=ALU.mult,
                 op1=ALU.add,
             )
@@ -238,9 +238,9 @@ def tile_rows_sink_cap_gqa_kernel(tc, qT, kT, t, v, sink, out):
         def invert(i):
             nc.vector.reciprocal(out=rec[i][:], in_=den[i][:])
 
-        def store(i):
+        def store(i, first=0, end=None):
             dst = out.rearrange("h (c p) e -> p (h c) e", p=QT)[:, units_in_out(i), :]
-            nc.sync.dma_start(out=dst, in_=res[i][:])
+            nc.sync.dma_start(out=dst[:, first:end], in_=res[i][:, first:end])
 
         def divide(i):
             n = len(GROUPS[i])
@@ -252,12 +252,15 @@ def tile_rows_sink_cap_gqa_kernel(tc, qT, kT, t, v, sink, out):
             )
             store(i)
 
-        def divide_on_scalar(i):
+        def divide_on_scalar(i, unit_stores=False):
             for n in range(len(GROUPS[i])):
                 nc.scalar.activation(
                     out=res[i][:, n, :], in_=y_banks[i % Y_BANKS][:, n, :], func=ACT.Copy, scale=rec[i][:, n : n + 1]
                 )
-            store(i)
+                if unit_stores:
+                    store(i, n, n + 1)
+            if not unit_stores:
+                store(i)
 
         def cap(u):
             i, n = turn[u]
@@ -319,15 +322,15 @@ def tile_rows_sink_cap_gqa_kernel(tc, qT, kT, t, v, sink, out):
         quantize_q(0, early=True)
         for r in range(PACK):
             quantize_k(r)
-        quantize_q(1, early=True)
         round_q(2, early=True)
         nc.vector.scalar_tensor_tensor(
             out=t_abs[:], in0=t_sb[:], scalar=-1.0, in1=t_sb[:], op0=ALU.mult, op1=ALU.max
         )
-        quantize_q(2, early=True)
+        quantize_q(1, early=True)
         nc.vector.tensor_scalar(
             out=t_guess[:], in0=t_abs[:].bitcast(I32), scalar1=BITS_TO_LN, scalar2=BITS_OFFSET, op0=ALU.mult, op1=ALU.add
         )
+        quantize_q(2, early=True)
         for g in OTHER_HEADS:
             nc.sync.dma_start(out=k_mx[g * ROWS : (g + 1) * ROWS, :], in_=k_mx[tile0, :])
         for rows in other_rows:
@@ -346,11 +349,24 @@ def tile_rows_sink_cap_gqa_kernel(tc, qT, kT, t, v, sink, out):
         head0_exp(2, 4)
         nc.scalar.activation(out=t_inv[:], in_=t_guess[:], func=ACT.Exp, scale=-1.0)
         nc.scalar.activation(out=t_sign[:], in_=t_sb[:], func=ACT.Sign)
+        round_q(2)
         quantize_q(3)
+        quantize_q(2)
         multiply(0)
         nc.vector.tensor_tensor(out=t_near1[:], in0=t_inv[:], in1=t_abs[:], op=ALU.mult)
-        round_q(2)
+        nc.vector.tensor_tensor(
+            out=v_bf[:],
+            in0=v_raw[:].rearrange("p j e -> p e j"),
+            in1=t_sign[:].unsqueeze(1).to_broadcast([P, D, PACK]),
+            op=ALU.mult,
+        )
         nc.vector.tensor_scalar(out=t_rest[:], in0=t_near1[:], scalar1=-1.0, scalar2=None, op0=ALU.add)
+        quantize_w(0, 0)
+        ln_step(0)
+        nc.vector.quantize_mx(
+            out=v_codes[:].bitcast(FP8X4), scales=v_scales[:], in_=v_bf[:].rearrange("p e j -> p (e j)")
+        )
+        ln_step(1)
         head0_cap(2)
         head0_scores(4)
         head0_cap(3)
@@ -362,104 +378,92 @@ def tile_rows_sink_cap_gqa_kernel(tc, qT, kT, t, v, sink, out):
         head0_exp(10, 13)
         for u in range(len(OTHER_HEADS)):
             scores(*turn[u])
-
-        quantize_w(0, 0)
-        ln_step(0)
-        quantize_q(2)
-        ln_step(1)
-        nc.vector.tensor_tensor(
-            out=v_bf[:],
-            in0=v_raw[:].rearrange("p j e -> p e j"),
-            in1=t_sign[:].unsqueeze(1).to_broadcast([P, D, PACK]),
-            op=ALU.mult,
-        )
-        ln_step(2)
-        multiply(1)
-        ln_step(3)
-        nc.vector.quantize_mx(
-            out=v_codes[:].bitcast(FP8X4), scales=v_scales[:], in_=v_bf[:].rearrange("p e j -> p (e j)")
-        )
-        ln_step(4)
-        quantize_w(0, 1)
-        multiply(2)
         cap(0)
-        cap(1)
         head0_exp(13, 16)
-        round_q(1)
+        multiply(1)
+        ln_step(2)
+        quantize_w(0, 1)
+        ln_step(3)
+        multiply(2)
+        ln_step(4)
+        round_q(0)
         quantize_w(0, 2)
         for n in range(CHUNKS - 1):
             values(HEAD0, n)
-        round_q(0)
+        cap(1)
         multiply(3)
-        quantize_q(1)
         quantize_q(0)
+        round_q(1)
         quantize_w(0, 3)
 
-        pair1, pair2, pair3, single1, single2, last = range(FIRST_SUMMED, len(GROUPS))
+        triple, pair2, pair3, pair4, last = range(FIRST_SUMMED, len(GROUPS))
         half_q = QT // 2
         cap(2)
         values(HEAD0, CHUNKS - 1)
-        cap(3)
-        add_ln(*turn[3])
-        cap(4)
-        add_ln(*turn[4])
-        add_sink(HEAD0)
-        invert(HEAD0)
+        add_ln(*turn[2])
+        quantize_q(1)
         for r in range(PACK):
             weigh_place(r)
-        divide(HEAD0)
         interleave(0, 2)
-        interleave(2, 3)
+        add_sink(HEAD0)
+        cap(3)
+        add_ln(*turn[3])
+        invert(HEAD0)
+        cap(4)
+        add_ln(*turn[4])
         cap(5)
+        weigh_summed(triple, 0)
+        quantize_and_values(PLACED)
+        quantize_w(triple, 0)
+        values(triple, 0)
+        divide(HEAD0)
         add_ln(*turn[5])
         cap(6)
-        weigh_group(pair1)
+        nc.scalar.activation(out=w_bf[triple][:, 1:3], in_=logits[triple][:, 1:3], func=ACT.Exp)
+        add_sink(PLACED)
         add_ln(*turn[6])
-        quantize_and_values(PLACED)
+        invert(PLACED)
+        for n in (1, 2):
+            quantize_w(triple, n)
+            values(triple, n)
         cap(7)
-        quantize_and_values(pair1)
         cap(8)
         weigh_group(pair2)
-        add_ln(*turn[7])
-        add_sink(PLACED)
-        add_ln(*turn[8])
-        invert(PLACED)
-        add_sink(pair1)
         divide(PLACED)
-        invert(pair1)
+        add_ln(*turn[7])
+        add_sink(triple)
+        add_ln(*turn[8])
+        invert(triple)
+        divide(triple)
         cap(9)
         cap(10)
         weigh_group(pair3)
         add_ln(*turn[9])
         quantize_and_values(pair2)
-        divide(pair1)
-        keep_warm(pair2, single1, 5)
+        keep_warm(pair2, pair4, 4)
         add_ln(*turn[10])
-        add_sink(pair2)
         quantize_and_values(pair3)
-        keep_warm(pair2, single1, 3)
-        invert(pair2)
+        keep_warm(pair2, pair4, 4)
+        add_sink(pair2)
         cap(11)
-        add_ln(*turn[11])
-        weigh_summed(single1, 0)
-        weigh_summed(single2, 0)
+        add_ln(last, 0, 0, half_q)
+        invert(pair2)
+        add_ln(last, 0, half_q, QT)
+        weigh_summed(pair4, 0)
+        weigh_summed(pair4, 1)
         weigh_summed(last, 0, 0, half_q)
         weigh_summed(last, 0, half_q, QT)
-        quantize_and_values(single1)
         add_sink(pair3)
         divide(pair2)
         invert(pair3)
-        quantize_and_values(single2)
+        quantize_and_values(pair4)
         divide_on_scalar(pair3)
         quantize_w(last, 0, 0, half_q)
-        add_sink(single1)
         quantize_w(last, 0, half_q, QT)
         values(last, 0)
-        invert(single1)
-        divide_on_scalar(single1)
-        add_sink(single2)
-        invert(single2)
-        divide_on_scalar(single2)
+        add_sink(pair4)
+        invert(pair4)
+        divide_on_scalar(pair4, unit_stores=True)
         add_sink(last)
         invert(last)
         divide(last)

@@ -21,7 +21,8 @@ ROWS = D // PACK
 QT = 128
 CHUNKS = NQ // QT
 EARLY = 3
-K_PIECES = ((0, 384), (384, 512))
+K_PIECES = ((0, 256), (256, 384), (384, 512))
+WINDOW = 64
 WALK = 4
 
 BITS_TO_LN = math.log(2.0) / 2.0**23
@@ -29,10 +30,10 @@ BITS_OFFSET = -127.0 * math.log(2.0) + 0.0298
 LN_DEGREE = 5
 
 OTHER_HEADS = (2, 3, 1)
-TURN_CHUNKS = (3, 3, 2, 2, 2, 3, 0, 0, 0, 1, 1, 1)
-TURNS = [(OTHER_HEADS[u % 3], c) for u, c in enumerate(TURN_CHUNKS)]
-GROUPS = [[(0, c) for c in range(CHUNKS)], TURNS[0:2], TURNS[2:5], TURNS[5:7], TURNS[7:9], TURNS[9:11], TURNS[11:12]]
-HEAD0, PLACED, FIRST_SUMMED = 0, 1, 2
+TURNS = [(h, c) for c in (3, 2, 0, 1) for h in OTHER_HEADS]
+UNITS = [(0, c) for c in range(CHUNKS)] + TURNS
+PLACED = 2
+GROUPS = [UNITS[0:4], TURNS[0:3], TURNS[3:6], TURNS[6:9], TURNS[9:11], TURNS[11:12]]
 Y_BANKS = 3
 HEAD0_FILLS = ((0, 2), (2, 4), (4, 7), (7, 10), (10, 13), (13, 16))
 
@@ -65,7 +66,8 @@ def tile_rows_sink_cap_gqa_kernel(tc, qT, kT, t, v, sink, out):
         q_bf = [sb.tile([P, QT, PACK], BF16, align_bytes=64, name="q_bf%d" % c) for c in q_slots]
         q_codes = [sb.tile([P, QT], I32, align_bytes=64, name="q_codes%d" % c) for c in q_slots]
         q_scales = [sb.tile([P, QT], U8, align_bytes=64, name="q_scales%d" % c) for c in q_slots]
-        k_bf = [sb.tile([ROWS, 2, P, PACK], BF16, align_bytes=64, name="k_bf%d" % i) for i in range(2)]
+        k_win = [sb.tile([P, 2, WINDOW, PACK], BF16, align_bytes=64, name="k_win%d" % w) for w in range(2)]
+        k_late = sb.tile([ROWS, 2, P, PACK], BF16, align_bytes=64)
         k_mx = sb.tile([P, N + N // PACK], I32, align_bytes=64)
         k_codes = k_mx[:, 0:N]
         k_scales = k_mx[:, N:].bitcast(U8)
@@ -73,42 +75,46 @@ def tile_rows_sink_cap_gqa_kernel(tc, qT, kT, t, v, sink, out):
         v_codes = sb.tile([P, D], I32, align_bytes=64)
         v_scales = sb.tile([P, D], U8, align_bytes=64)
 
-        def per_group(name, shape, dtype, first=0):
-            return {
-                i: sb.tile([P, len(GROUPS[i])] + shape, dtype, align_bytes=64, name="%s%d" % (name, i))
-                for i in range(first, len(GROUPS))
-            }
+        def per_group(name, shape):
+            return [sb.tile([P, len(g)] + shape, F32, name="%s%d" % (name, i)) for i, g in enumerate(GROUPS)]
 
         head0_rows = sb.tile([P, CHUNKS * PACK, QT], F32)
         p_rows = sb.tile([P, CHUNKS * PACK, QT], F32)
-        capped_rows = sb.tile([P, len(GROUPS[PLACED]), PACK, QT], F32)
-        w_rows = sb.tile([P, len(GROUPS[PLACED]), PACK, QT], BF16)
-        capped_words = per_group("capped_words", [QT, PACK], F32, first=FIRST_SUMMED)
-        logits = per_group("logits", [QT, PACK], F32, first=FIRST_SUMMED)
-        w_bf = per_group("w_bf", [QT, PACK], BF16)
-        w_codes = per_group("w_codes", [QT], I32)
-        w_scales = per_group("w_scales", [QT], U8)
-        den = per_group("den", [], F32)
-        rec = per_group("rec", [], F32)
-        res = per_group("res", [D], F32)
+        capped_rows = sb.tile([P, PLACED, PACK, QT], F32)
+        w_rows = sb.tile([P, PLACED, PACK, QT], BF16)
+        capped_words = sb.tile([P, len(TURNS), QT, PACK], F32)
+        logits = sb.tile([P, len(TURNS), QT, PACK], F32)
+        w_bf = sb.tile([P, len(UNITS), QT, PACK], BF16, align_bytes=64)
+        w_codes = sb.tile([P, len(UNITS), QT], I32, align_bytes=64)
+        w_scales = sb.tile([P, len(UNITS), QT], U8, align_bytes=64)
+        den = per_group("den", [])
+        rec = per_group("rec", [])
+        res = per_group("res", [D])
         score_banks = [ps.tile([P, PACK, QT], F32, name="score%d" % g) for g in range(H + 1)]
         y_banks = [ps.tile([P, PACK, D], F32, name="y%d" % i) for i in range(Y_BANKS)]
 
         tile0 = slice(0, ROWS)
-        member = {unit: (i, n) for i, g in enumerate(GROUPS) for n, unit in enumerate(g)}
-        turn = [member[unit] for unit in TURNS]
+        group_of = {unit: i for i, g in enumerate(GROUPS) for unit in g}
 
-        def round_k(pair, half, copy=nc.vector.tensor_copy):
-            src = k_raw[half][:].rearrange("p j (s r) -> p s j r", r=PACK)[:, :, :, 2 * pair : 2 * pair + 2]
-            dst = k_bf[pair][:, :, K_PIECES[half][0] // PACK : K_PIECES[half][1] // PACK, :]
+        def round_k(piece, first, end, copy=nc.vector.tensor_copy):
+            a, b = [x // PACK for x in K_PIECES[piece]]
+            src = k_raw[piece][:].rearrange("p j (s r) -> p s j r", r=PACK)[:, :, :, first:end]
+            if first < 2:
+                w = a // WINDOW
+                dst = k_win[w][tile0, first:end, a - w * WINDOW : b - w * WINDOW, :]
+            else:
+                dst = k_late[:, first - 2 : end - 2, a:b, :]
             copy(out=dst.rearrange("p r s j -> p s j r"), in_=src)
 
-        def quantize_k(r):
-            cols = slice(r * P, (r + 1) * P)
+        def quantize_k(r, w=None):
+            if w is None:
+                rows, cols, src = tile0, slice(r * P, (r + 1) * P), k_late[:, r - 2]
+            else:
+                rows, cols, src = slice(0, P), slice(r * P + w * WINDOW, r * P + (w + 1) * WINDOW), k_win[w][:, r]
             nc.vector.quantize_mx(
-                out=k_codes[tile0, cols].bitcast(FP8X4),
-                scales=k_scales[tile0, cols],
-                in_=k_bf[r // 2][tile0, r % 2].rearrange("p s j -> p (s j)"),
+                out=k_codes[rows, cols].bitcast(FP8X4),
+                scales=k_scales[rows, cols],
+                in_=src.rearrange("p s j -> p (s j)"),
             )
 
         def round_q(c, early=False, copy=nc.vector.tensor_copy, q0=0, q1=QT):
@@ -153,8 +159,8 @@ def tile_rows_sink_cap_gqa_kernel(tc, qT, kT, t, v, sink, out):
                 stop=True,
             )
 
-        def scores(i, n):
-            h, c = GROUPS[i][n]
+        def scores(u):
+            h, c = TURNS[u]
             for r in range(PACK):
                 score_pass(score_banks[h][:, r, :], h, c, r)
 
@@ -173,7 +179,7 @@ def tile_rows_sink_cap_gqa_kernel(tc, qT, kT, t, v, sink, out):
 
         def multiply(c):
             nc.vector.tensor_tensor(
-                out=w_bf[0][:, c].rearrange("p (c i) r -> p c r i", i=WALK),
+                out=w_bf[:, c].rearrange("p (c i) r -> p c r i", i=WALK),
                 in0=p_rows[:, PACK * c : PACK * (c + 1), :].rearrange("p r (c i) -> p c r i", i=WALK),
                 in1=t_abs[:].unsqueeze(1).unsqueeze(3).to_broadcast([P, QT // WALK, PACK, WALK]),
                 op=ALU.mult,
@@ -196,34 +202,37 @@ def tile_rows_sink_cap_gqa_kernel(tc, qT, kT, t, v, sink, out):
                 op1=ALU.mult,
             )
 
-        def add_ln(i, n, q0=0, q1=QT):
+        def add_ln(u, q0=0, q1=QT):
             nc.vector.scalar_tensor_tensor(
-                out=logits[i][:, n, q0:q1],
-                in0=capped_words[i][:, n, q0:q1],
+                out=logits[:, u, q0:q1],
+                in0=capped_words[:, u, q0:q1],
                 scalar=CAP,
                 in1=t_ln[:].unsqueeze(1).to_broadcast([P, q1 - q0, PACK]),
                 op0=ALU.mult,
                 op1=ALU.add,
             )
 
-        def weigh_summed(i, n, q0=0, q1=QT):
-            nc.scalar.activation(out=w_bf[i][:, n, q0:q1, :], in_=logits[i][:, n, q0:q1, :], func=ACT.Exp)
-
-        def quantize_w(i, n, q0=0, q1=QT):
-            nc.vector.quantize_mx(
-                out=w_codes[i][:, n, q0:q1].bitcast(FP8X4),
-                scales=w_scales[i][:, n, q0:q1],
-                in_=w_bf[i][:, n, q0:q1, :].rearrange("p q r -> p (q r)"),
+        def weigh(first, end, q0=0, q1=QT):
+            nc.scalar.activation(
+                out=w_bf[:, CHUNKS + first : CHUNKS + end, q0:q1], in_=logits[:, first:end, q0:q1], func=ACT.Exp
             )
 
-        def values(i, n):
-            dst = y_banks[i % Y_BANKS][:, sorted(GROUPS[i]).index(GROUPS[i][n]), :]
-            whole_pass(dst, w_codes[i][:, n, :], w_scales[i][:, n, :], v_codes[:], v_scales[:])
+        def quantize_w(n, q0=0, q1=QT):
+            nc.vector.quantize_mx(
+                out=w_codes[:, n, q0:q1].bitcast(FP8X4),
+                scales=w_scales[:, n, q0:q1],
+                in_=w_bf[:, n, q0:q1, :].rearrange("p q r -> p (q r)"),
+            )
 
-        def keep_warm(i, bank_of, passes):
+        def values(n):
+            i = group_of[UNITS[n]]
+            dst = y_banks[i % Y_BANKS][:, sorted(GROUPS[i]).index(UNITS[n]), :]
+            whole_pass(dst, w_codes[:, n, :], w_scales[:, n, :], v_codes[:], v_scales[:])
+
+        def keep_warm(bank_of, passes):
             dst = y_banks[bank_of % Y_BANKS][:, PACK - 1, :]
             for rep in range(passes):
-                whole_pass(dst, w_codes[i][:, 0, :], w_scales[i][:, 0, :], v_codes[:], v_scales[:])
+                whole_pass(dst, w_codes[:, 0, :], w_scales[:, 0, :], v_codes[:], v_scales[:])
 
         def units_in_out(i):
             first, final = [CHUNKS * h + c for h, c in (min(GROUPS[i]), max(GROUPS[i]))]
@@ -263,34 +272,30 @@ def tile_rows_sink_cap_gqa_kernel(tc, qT, kT, t, v, sink, out):
                 store(i)
 
         def cap(u):
-            i, n = turn[u]
             bank = score_banks[TURNS[u][0]]
-            if i == PLACED:
-                dst, src = capped_rows[:, n], bank[:]
+            if u < PLACED:
+                dst, src = capped_rows[:, u], bank[:]
             else:
-                dst, src = capped_words[i][:, n], bank[:].rearrange("p r q -> p q r")
+                dst, src = capped_words[:, u], bank[:].rearrange("p r q -> p q r")
             nc.scalar.activation(out=dst, in_=src, func=ACT.Tanh, scale=1.0 / CAP)
             if u + len(OTHER_HEADS) < len(TURNS):
-                scores(*turn[u + len(OTHER_HEADS)])
+                scores(u + len(OTHER_HEADS))
 
         def weigh_place(r):
             nc.scalar.activation(
                 out=w_rows[:, :, r, :], in_=capped_rows[:, :, r, :], func=ACT.Exp, scale=CAP, bias=t_ln[:, r : r + 1]
             )
 
-        def weigh_group(i):
-            nc.scalar.activation(out=w_bf[i][:], in_=logits[i][:], func=ACT.Exp)
-
-        def interleave(first, end):
+        def interleave():
             nc.vector.tensor_copy(
-                out=w_bf[PLACED][:, first:end].rearrange("p n (c i) r -> p n c r i", i=WALK),
-                in_=w_rows[:, first:end].rearrange("p n r (c i) -> p n c r i", i=WALK),
+                out=w_bf[:, CHUNKS : CHUNKS + PLACED].rearrange("p n (c i) r -> p n c r i", i=WALK),
+                in_=w_rows[:].rearrange("p n r (c i) -> p n c r i", i=WALK),
             )
 
-        def quantize_and_values(i):
-            for n in range(len(GROUPS[i])):
-                quantize_w(i, n)
-                values(i, n)
+        def quantize_and_values(first, end):
+            for u in range(first, end):
+                quantize_w(CHUNKS + u)
+                values(CHUNKS + u)
 
         def load_k(piece):
             a, b = K_PIECES[piece]
@@ -302,6 +307,7 @@ def tile_rows_sink_cap_gqa_kernel(tc, qT, kT, t, v, sink, out):
         load_k(0)
         load_q(tile0, 0, 1)
         load_k(1)
+        load_k(2)
         load_q(tile0, 1, 2)
         load_q(tile0, 2, 3)
         nc.sync.dma_start(out=t_sb[:], in_=t.rearrange("(p j) o -> p (j o)", j=PACK))
@@ -311,26 +317,33 @@ def tile_rows_sink_cap_gqa_kernel(tc, qT, kT, t, v, sink, out):
             load_q(rows, 2, 3)
         nc.sync.dma_start(out=v_raw[:], in_=v[0].rearrange("(p j) e -> p j e", j=PACK))
 
+        for w in range(2):
+            nc.vector.memset(k_win[w][:].rearrange("p r s j -> p (r s j)").bitcast(I32), 0)
         nc.vector.memset(k_mx[tile0, N:], 0)
 
-        round_k(1, 0, nc.scalar.copy)
-        round_k(1, 1, nc.scalar.copy)
+        for piece in range(len(K_PIECES)):
+            round_k(piece, 2, 4, nc.scalar.copy)
         round_q(1, early=True, copy=nc.scalar.copy)
-        round_k(0, 0)
+        round_k(0, 0, 2)
         round_q(0, early=True)
-        round_k(0, 1)
+        round_k(1, 0, 2)
+        quantize_k(0, 0)
+        round_k(2, 0, 2)
         quantize_q(0, early=True)
-        for r in range(PACK):
-            quantize_k(r)
+        quantize_k(1, 0)
+        quantize_k(0, 1)
+        quantize_k(1, 1)
+        quantize_k(2)
+        quantize_k(3)
         round_q(2, early=True)
+        quantize_q(1, early=True)
         nc.vector.scalar_tensor_tensor(
             out=t_abs[:], in0=t_sb[:], scalar=-1.0, in1=t_sb[:], op0=ALU.mult, op1=ALU.max
         )
-        quantize_q(1, early=True)
+        quantize_q(2, early=True)
         nc.vector.tensor_scalar(
             out=t_guess[:], in0=t_abs[:].bitcast(I32), scalar1=BITS_TO_LN, scalar2=BITS_OFFSET, op0=ALU.mult, op1=ALU.add
         )
-        quantize_q(2, early=True)
         for g in OTHER_HEADS:
             nc.sync.dma_start(out=k_mx[g * ROWS : (g + 1) * ROWS, :], in_=k_mx[tile0, :])
         for rows in other_rows:
@@ -349,11 +362,11 @@ def tile_rows_sink_cap_gqa_kernel(tc, qT, kT, t, v, sink, out):
         head0_exp(2, 4)
         nc.scalar.activation(out=t_inv[:], in_=t_guess[:], func=ACT.Exp, scale=-1.0)
         nc.scalar.activation(out=t_sign[:], in_=t_sb[:], func=ACT.Sign)
-        round_q(2)
         quantize_q(3)
-        quantize_q(2)
+        round_q(2)
         multiply(0)
         nc.vector.tensor_tensor(out=t_near1[:], in0=t_inv[:], in1=t_abs[:], op=ALU.mult)
+        quantize_q(2)
         nc.vector.tensor_tensor(
             out=v_bf[:],
             in0=v_raw[:].rearrange("p j e -> p e j"),
@@ -361,7 +374,7 @@ def tile_rows_sink_cap_gqa_kernel(tc, qT, kT, t, v, sink, out):
             op=ALU.mult,
         )
         nc.vector.tensor_scalar(out=t_rest[:], in0=t_near1[:], scalar1=-1.0, scalar2=None, op0=ALU.add)
-        quantize_w(0, 0)
+        quantize_w(0)
         ln_step(0)
         nc.vector.quantize_mx(
             out=v_codes[:].bitcast(FP8X4), scales=v_scales[:], in_=v_bf[:].rearrange("p e j -> p (e j)")
@@ -377,93 +390,87 @@ def tile_rows_sink_cap_gqa_kernel(tc, qT, kT, t, v, sink, out):
         head0_cap(5)
         head0_exp(10, 13)
         for u in range(len(OTHER_HEADS)):
-            scores(*turn[u])
+            scores(u)
         cap(0)
         head0_exp(13, 16)
         multiply(1)
         ln_step(2)
-        quantize_w(0, 1)
+        quantize_w(1)
         ln_step(3)
         multiply(2)
         ln_step(4)
         round_q(0)
-        quantize_w(0, 2)
+        quantize_w(2)
         for n in range(CHUNKS - 1):
-            values(HEAD0, n)
+            values(n)
         cap(1)
         multiply(3)
         quantize_q(0)
         round_q(1)
-        quantize_w(0, 3)
+        quantize_w(3)
 
-        triple, pair2, pair3, pair4, last = range(FIRST_SUMMED, len(GROUPS))
+        head0, first, second, third, pair, last = range(len(GROUPS))
         half_q = QT // 2
         cap(2)
-        values(HEAD0, CHUNKS - 1)
-        add_ln(*turn[2])
+        values(CHUNKS - 1)
+        add_ln(2)
         quantize_q(1)
         for r in range(PACK):
             weigh_place(r)
-        interleave(0, 2)
-        add_sink(HEAD0)
+        interleave()
+        add_sink(head0)
         cap(3)
-        add_ln(*turn[3])
-        invert(HEAD0)
+        add_ln(3)
+        invert(head0)
         cap(4)
-        add_ln(*turn[4])
+        add_ln(4)
         cap(5)
-        weigh_summed(triple, 0)
-        quantize_and_values(PLACED)
-        quantize_w(triple, 0)
-        values(triple, 0)
-        divide(HEAD0)
-        add_ln(*turn[5])
+        weigh(2, 3)
+        quantize_and_values(0, 3)
+        divide(head0)
+        add_ln(5)
         cap(6)
-        nc.scalar.activation(out=w_bf[triple][:, 1:3], in_=logits[triple][:, 1:3], func=ACT.Exp)
-        add_sink(PLACED)
-        add_ln(*turn[6])
-        invert(PLACED)
-        for n in (1, 2):
-            quantize_w(triple, n)
-            values(triple, n)
+        weigh(3, 5)
+        add_sink(first)
+        add_ln(6)
+        invert(first)
+        quantize_and_values(3, 5)
         cap(7)
         cap(8)
-        weigh_group(pair2)
-        divide(PLACED)
-        add_ln(*turn[7])
-        add_sink(triple)
-        add_ln(*turn[8])
-        invert(triple)
-        divide(triple)
+        weigh(5, 7)
+        divide(first)
+        add_ln(7)
+        add_ln(8)
         cap(9)
         cap(10)
-        weigh_group(pair3)
-        add_ln(*turn[9])
-        quantize_and_values(pair2)
-        keep_warm(pair2, pair4, 4)
-        add_ln(*turn[10])
-        quantize_and_values(pair3)
-        keep_warm(pair2, pair4, 4)
-        add_sink(pair2)
+        weigh(7, 9)
+        add_ln(9)
+        quantize_and_values(5, 7)
+        keep_warm(pair, 4)
+        add_ln(10)
+        add_sink(second)
+        quantize_and_values(7, 9)
+        keep_warm(pair, 4)
+        invert(second)
         cap(11)
-        add_ln(last, 0, 0, half_q)
-        invert(pair2)
-        add_ln(last, 0, half_q, QT)
-        weigh_summed(pair4, 0)
-        weigh_summed(pair4, 1)
-        weigh_summed(last, 0, 0, half_q)
-        weigh_summed(last, 0, half_q, QT)
-        add_sink(pair3)
-        divide(pair2)
-        invert(pair3)
-        quantize_and_values(pair4)
-        divide_on_scalar(pair3)
-        quantize_w(last, 0, 0, half_q)
-        quantize_w(last, 0, half_q, QT)
-        values(last, 0)
-        add_sink(pair4)
-        invert(pair4)
-        divide_on_scalar(pair4, unit_stores=True)
+        add_ln(11, 0, half_q)
+        add_ln(11, half_q, QT)
+        weigh(9, 10)
+        weigh(10, 11)
+        weigh(11, 12, 0, half_q)
+        weigh(11, 12, half_q, QT)
+        quantize_and_values(9, 10)
+        add_sink(third)
+        divide(second)
+        quantize_and_values(10, 11)
+        invert(third)
+        divide_on_scalar(third)
+        quantize_w(len(UNITS) - 1, 0, half_q)
+        quantize_w(len(UNITS) - 1, half_q, QT)
+        values(len(UNITS) - 1)
+        add_sink(pair)
+        invert(pair)
+        divide_on_scalar(pair, unit_stores=True)
         add_sink(last)
         invert(last)
         divide(last)

@@ -21,8 +21,7 @@ ROWS = D // PACK
 QT = 128
 CHUNKS = NQ // QT
 EARLY = 3
-K_PIECES = ((0, 256), (256, 384), (384, 512))
-WINDOW = 64
+K_PIECES = ((0, 384), (384, 512))
 WALK = 4
 
 BITS_TO_LN = math.log(2.0) / 2.0**23
@@ -33,8 +32,10 @@ OTHER_HEADS = (2, 3, 1)
 TURNS = [(h, c) for c in (3, 2, 0, 1) for h in OTHER_HEADS]
 UNITS = [(0, c) for c in range(CHUNKS)] + TURNS
 PLACED = 2
-GROUPS = [UNITS[0:4], TURNS[0:3], TURNS[3:6], TURNS[6:9], TURNS[9:11], TURNS[11:12]]
+GROUPS = [UNITS[0:4], TURNS[0:3], TURNS[3:5], TURNS[5:7], TURNS[7:9], TURNS[9:10], TURNS[10:11], TURNS[11:12]]
 Y_BANKS = 3
+BANK_OF = (0, 1, 2, 0, 1, 2, 2, 0)
+SLOT_OF = (0, 0, 0, 0, 0, 0, 1, 0)
 HEAD0_FILLS = ((0, 2), (2, 4), (4, 7), (7, 10), (10, 13), (13, 16))
 
 
@@ -66,8 +67,7 @@ def tile_rows_sink_cap_gqa_kernel(tc, qT, kT, t, v, sink, out):
         q_bf = [sb.tile([P, QT, PACK], BF16, align_bytes=64, name="q_bf%d" % c) for c in q_slots]
         q_codes = [sb.tile([P, QT], I32, align_bytes=64, name="q_codes%d" % c) for c in q_slots]
         q_scales = [sb.tile([P, QT], U8, align_bytes=64, name="q_scales%d" % c) for c in q_slots]
-        k_win = [sb.tile([P, 2, WINDOW, PACK], BF16, align_bytes=64, name="k_win%d" % w) for w in range(2)]
-        k_late = sb.tile([ROWS, 2, P, PACK], BF16, align_bytes=64)
+        k_bf = [sb.tile([ROWS, 2, P, PACK], BF16, align_bytes=64, name="k_bf%d" % i) for i in range(2)]
         k_mx = sb.tile([P, N + N // PACK], I32, align_bytes=64)
         k_codes = k_mx[:, 0:N]
         k_scales = k_mx[:, N:].bitcast(U8)
@@ -96,25 +96,17 @@ def tile_rows_sink_cap_gqa_kernel(tc, qT, kT, t, v, sink, out):
         tile0 = slice(0, ROWS)
         group_of = {unit: i for i, g in enumerate(GROUPS) for unit in g}
 
-        def round_k(piece, first, end, copy=nc.vector.tensor_copy):
-            a, b = [x // PACK for x in K_PIECES[piece]]
-            src = k_raw[piece][:].rearrange("p j (s r) -> p s j r", r=PACK)[:, :, :, first:end]
-            if first < 2:
-                w = a // WINDOW
-                dst = k_win[w][tile0, first:end, a - w * WINDOW : b - w * WINDOW, :]
-            else:
-                dst = k_late[:, first - 2 : end - 2, a:b, :]
+        def round_k(pair, half, copy=nc.vector.tensor_copy):
+            src = k_raw[half][:].rearrange("p j (s r) -> p s j r", r=PACK)[:, :, :, 2 * pair : 2 * pair + 2]
+            dst = k_bf[pair][:, :, K_PIECES[half][0] // PACK : K_PIECES[half][1] // PACK, :]
             copy(out=dst.rearrange("p r s j -> p s j r"), in_=src)
 
-        def quantize_k(r, w=None):
-            if w is None:
-                rows, cols, src = tile0, slice(r * P, (r + 1) * P), k_late[:, r - 2]
-            else:
-                rows, cols, src = slice(0, P), slice(r * P + w * WINDOW, r * P + (w + 1) * WINDOW), k_win[w][:, r]
+        def quantize_k(r):
+            cols = slice(r * P, (r + 1) * P)
             nc.vector.quantize_mx(
-                out=k_codes[rows, cols].bitcast(FP8X4),
-                scales=k_scales[rows, cols],
-                in_=src.rearrange("p s j -> p (s j)"),
+                out=k_codes[tile0, cols].bitcast(FP8X4),
+                scales=k_scales[tile0, cols],
+                in_=k_bf[r // 2][tile0, r % 2].rearrange("p s j -> p (s j)"),
             )
 
         def round_q(c, early=False, copy=nc.vector.tensor_copy, q0=0, q1=QT):
@@ -226,11 +218,11 @@ def tile_rows_sink_cap_gqa_kernel(tc, qT, kT, t, v, sink, out):
 
         def values(n):
             i = group_of[UNITS[n]]
-            dst = y_banks[i % Y_BANKS][:, sorted(GROUPS[i]).index(UNITS[n]), :]
+            dst = y_banks[BANK_OF[i]][:, SLOT_OF[i] + sorted(GROUPS[i]).index(UNITS[n]), :]
             whole_pass(dst, w_codes[:, n, :], w_scales[:, n, :], v_codes[:], v_scales[:])
 
         def keep_warm(bank_of, passes):
-            dst = y_banks[bank_of % Y_BANKS][:, PACK - 1, :]
+            dst = y_banks[BANK_OF[bank_of]][:, PACK - 1, :]
             for rep in range(passes):
                 whole_pass(dst, w_codes[:, 0, :], w_scales[:, 0, :], v_codes[:], v_scales[:])
 
@@ -239,44 +231,41 @@ def tile_rows_sink_cap_gqa_kernel(tc, qT, kT, t, v, sink, out):
             return slice(first, final + 1, max((final - first) // max(len(GROUPS[i]) - 1, 1), 1))
 
         def add_sink(i):
-            y = y_banks[i % Y_BANKS]
+            y = y_banks[BANK_OF[i]]
             nc.vector.tensor_tensor(
-                out=den[i][:], in0=y[:, 0 : len(GROUPS[i]), D - 1], in1=sink_sb[:, units_in_out(i)], op=ALU.add
+                out=den[i][:], in0=y[:, SLOT_OF[i] : SLOT_OF[i] + len(GROUPS[i]), D - 1], in1=sink_sb[:, units_in_out(i)], op=ALU.add
             )
 
         def invert(i):
             nc.vector.reciprocal(out=rec[i][:], in_=den[i][:])
 
-        def store(i, first=0, end=None):
+        def store(i):
             dst = out.rearrange("h (c p) e -> p (h c) e", p=QT)[:, units_in_out(i), :]
-            nc.sync.dma_start(out=dst[:, first:end], in_=res[i][:, first:end])
+            nc.sync.dma_start(out=dst, in_=res[i][:])
 
         def divide(i):
             n = len(GROUPS[i])
             nc.vector.tensor_tensor(
                 out=res[i][:],
-                in0=y_banks[i % Y_BANKS][:, 0:n, :],
+                in0=y_banks[BANK_OF[i]][:, SLOT_OF[i] : SLOT_OF[i] + n, :],
                 in1=rec[i][:].unsqueeze(2).to_broadcast([P, n, D]),
                 op=ALU.mult,
             )
             store(i)
 
-        def divide_on_scalar(i, unit_stores=False):
+        def divide_on_scalar(i):
             for n in range(len(GROUPS[i])):
                 nc.scalar.activation(
-                    out=res[i][:, n, :], in_=y_banks[i % Y_BANKS][:, n, :], func=ACT.Copy, scale=rec[i][:, n : n + 1]
+                    out=res[i][:, n, :], in_=y_banks[BANK_OF[i]][:, SLOT_OF[i] + n, :], func=ACT.Copy, scale=rec[i][:, n : n + 1]
                 )
-                if unit_stores:
-                    store(i, n, n + 1)
-            if not unit_stores:
-                store(i)
+            store(i)
 
-        def cap(u):
+        def cap(u, q0=0, q1=QT):
             bank = score_banks[TURNS[u][0]]
             if u < PLACED:
                 dst, src = capped_rows[:, u], bank[:]
             else:
-                dst, src = capped_words[:, u], bank[:].rearrange("p r q -> p q r")
+                dst, src = capped_words[:, u, q0:q1], bank[:, :, q0:q1].rearrange("p r q -> p q r")
             nc.scalar.activation(out=dst, in_=src, func=ACT.Tanh, scale=1.0 / CAP)
             if u + len(OTHER_HEADS) < len(TURNS):
                 scores(u + len(OTHER_HEADS))
@@ -307,7 +296,6 @@ def tile_rows_sink_cap_gqa_kernel(tc, qT, kT, t, v, sink, out):
         load_k(0)
         load_q(tile0, 0, 1)
         load_k(1)
-        load_k(2)
         load_q(tile0, 1, 2)
         load_q(tile0, 2, 3)
         nc.sync.dma_start(out=t_sb[:], in_=t.rearrange("(p j) o -> p (j o)", j=PACK))
@@ -317,24 +305,17 @@ def tile_rows_sink_cap_gqa_kernel(tc, qT, kT, t, v, sink, out):
             load_q(rows, 2, 3)
         nc.sync.dma_start(out=v_raw[:], in_=v[0].rearrange("(p j) e -> p j e", j=PACK))
 
-        for w in range(2):
-            nc.vector.memset(k_win[w][:].rearrange("p r s j -> p (r s j)").bitcast(I32), 0)
         nc.vector.memset(k_mx[tile0, N:], 0)
 
-        for piece in range(len(K_PIECES)):
-            round_k(piece, 2, 4, nc.scalar.copy)
+        round_k(1, 0, nc.scalar.copy)
+        round_k(1, 1, nc.scalar.copy)
         round_q(1, early=True, copy=nc.scalar.copy)
-        round_k(0, 0, 2)
+        round_k(0, 0)
         round_q(0, early=True)
-        round_k(1, 0, 2)
-        quantize_k(0, 0)
-        round_k(2, 0, 2)
+        round_k(0, 1)
         quantize_q(0, early=True)
-        quantize_k(1, 0)
-        quantize_k(0, 1)
-        quantize_k(1, 1)
-        quantize_k(2)
-        quantize_k(3)
+        for r in range(PACK):
+            quantize_k(r)
         round_q(2, early=True)
         quantize_q(1, early=True)
         nc.vector.scalar_tensor_tensor(
@@ -409,7 +390,7 @@ def tile_rows_sink_cap_gqa_kernel(tc, qT, kT, t, v, sink, out):
         round_q(1)
         quantize_w(3)
 
-        head0, first, second, third, pair, last = range(len(GROUPS))
+        head0, first, pair1, pair2, pair3, single1, single2, last = range(len(GROUPS))
         half_q = QT // 2
         cap(2)
         values(CHUNKS - 1)
@@ -440,37 +421,45 @@ def tile_rows_sink_cap_gqa_kernel(tc, qT, kT, t, v, sink, out):
         weigh(5, 7)
         divide(first)
         add_ln(7)
+        add_sink(pair1)
         add_ln(8)
+        invert(pair1)
+        quantize_and_values(5, 7)
         cap(9)
         cap(10)
         weigh(7, 9)
         add_ln(9)
-        quantize_and_values(5, 7)
-        keep_warm(pair, 4)
-        add_ln(10)
-        add_sink(second)
-        quantize_and_values(7, 9)
-        keep_warm(pair, 4)
-        invert(second)
-        cap(11)
-        add_ln(11, 0, half_q)
-        add_ln(11, half_q, QT)
         weigh(9, 10)
+        divide(pair1)
+        keep_warm(single1, 4)
+        add_sink(pair2)
+        add_ln(10, 0, half_q)
+        invert(pair2)
+        add_ln(10, half_q, QT)
+        quantize_and_values(7, 9)
+        keep_warm(single1, 2)
+        divide(pair2)
+        quantize_and_values(9, 10)
+        keep_warm(last, 2)
+        for q0 in range(0, QT, QT // 4):
+            cap(11, q0, q0 + QT // 4)
+            add_ln(11, q0, q0 + QT // 4)
         weigh(10, 11)
         weigh(11, 12, 0, half_q)
         weigh(11, 12, half_q, QT)
-        quantize_and_values(9, 10)
-        add_sink(third)
-        divide(second)
+        add_sink(pair3)
+        add_sink(single1)
         quantize_and_values(10, 11)
-        invert(third)
-        divide_on_scalar(third)
+        invert(pair3)
+        invert(single1)
+        divide_on_scalar(pair3)
         quantize_w(len(UNITS) - 1, 0, half_q)
         quantize_w(len(UNITS) - 1, half_q, QT)
         values(len(UNITS) - 1)
-        add_sink(pair)
-        invert(pair)
-        divide_on_scalar(pair, unit_stores=True)
+        add_sink(single2)
+        divide(single1)
+        invert(single2)
+        divide_on_scalar(single2)
         add_sink(last)
         invert(last)
         divide(last)

@@ -31,11 +31,8 @@ LN_DEGREE = 5
 OTHER_HEADS = (2, 3, 1)
 TURNS = [(h, c) for c in (3, 2, 0, 1) for h in OTHER_HEADS]
 UNITS = [(0, c) for c in range(CHUNKS)] + TURNS
-PLACED = 2
-GROUPS = [UNITS[0:4], TURNS[0:3], TURNS[3:5], TURNS[5:7], TURNS[7:9], TURNS[9:10], TURNS[10:11], TURNS[11:12]]
+GROUPS = [UNITS[0:4], TURNS[0:3], TURNS[3:5], TURNS[5:7], TURNS[7:9], TURNS[9:11], TURNS[11:12]]
 Y_BANKS = 3
-BANK_OF = (0, 1, 2, 0, 1, 2, 2, 0)
-SLOT_OF = (0, 0, 0, 0, 0, 0, 1, 0)
 HEAD0_FILLS = ((0, 2), (2, 4), (4, 7), (7, 10), (10, 13), (13, 16))
 
 
@@ -80,8 +77,6 @@ def tile_rows_sink_cap_gqa_kernel(tc, qT, kT, t, v, sink, out):
 
         head0_rows = sb.tile([P, CHUNKS * PACK, QT], F32)
         p_rows = sb.tile([P, CHUNKS * PACK, QT], F32)
-        capped_rows = sb.tile([P, PLACED, PACK, QT], F32)
-        w_rows = sb.tile([P, PLACED, PACK, QT], BF16)
         capped_words = sb.tile([P, len(TURNS), QT, PACK], F32)
         logits = sb.tile([P, len(TURNS), QT, PACK], F32)
         w_bf = sb.tile([P, len(UNITS), QT, PACK], BF16, align_bytes=64)
@@ -218,11 +213,11 @@ def tile_rows_sink_cap_gqa_kernel(tc, qT, kT, t, v, sink, out):
 
         def values(n):
             i = group_of[UNITS[n]]
-            dst = y_banks[BANK_OF[i]][:, SLOT_OF[i] + sorted(GROUPS[i]).index(UNITS[n]), :]
+            dst = y_banks[i % Y_BANKS][:, sorted(GROUPS[i]).index(UNITS[n]), :]
             whole_pass(dst, w_codes[:, n, :], w_scales[:, n, :], v_codes[:], v_scales[:])
 
         def keep_warm(bank_of, passes):
-            dst = y_banks[BANK_OF[bank_of]][:, PACK - 1, :]
+            dst = y_banks[bank_of % Y_BANKS][:, PACK - 1, :]
             for rep in range(passes):
                 whole_pass(dst, w_codes[:, 0, :], w_scales[:, 0, :], v_codes[:], v_scales[:])
 
@@ -231,55 +226,43 @@ def tile_rows_sink_cap_gqa_kernel(tc, qT, kT, t, v, sink, out):
             return slice(first, final + 1, max((final - first) // max(len(GROUPS[i]) - 1, 1), 1))
 
         def add_sink(i):
-            y = y_banks[BANK_OF[i]]
+            y = y_banks[i % Y_BANKS]
             nc.vector.tensor_tensor(
-                out=den[i][:], in0=y[:, SLOT_OF[i] : SLOT_OF[i] + len(GROUPS[i]), D - 1], in1=sink_sb[:, units_in_out(i)], op=ALU.add
+                out=den[i][:], in0=y[:, 0 : len(GROUPS[i]), D - 1], in1=sink_sb[:, units_in_out(i)], op=ALU.add
             )
 
         def invert(i):
             nc.vector.reciprocal(out=rec[i][:], in_=den[i][:])
 
-        def store(i):
+        def store(i, first=0, end=None):
             dst = out.rearrange("h (c p) e -> p (h c) e", p=QT)[:, units_in_out(i), :]
-            nc.sync.dma_start(out=dst, in_=res[i][:])
+            nc.sync.dma_start(out=dst[:, first:end], in_=res[i][:, first:end])
 
         def divide(i):
             n = len(GROUPS[i])
             nc.vector.tensor_tensor(
                 out=res[i][:],
-                in0=y_banks[BANK_OF[i]][:, SLOT_OF[i] : SLOT_OF[i] + n, :],
+                in0=y_banks[i % Y_BANKS][:, 0 : n, :],
                 in1=rec[i][:].unsqueeze(2).to_broadcast([P, n, D]),
                 op=ALU.mult,
             )
             store(i)
 
-        def divide_on_scalar(i):
+        def divide_on_scalar(i, unit_stores=False):
             for n in range(len(GROUPS[i])):
                 nc.scalar.activation(
-                    out=res[i][:, n, :], in_=y_banks[BANK_OF[i]][:, SLOT_OF[i] + n, :], func=ACT.Copy, scale=rec[i][:, n : n + 1]
+                    out=res[i][:, n, :], in_=y_banks[i % Y_BANKS][:, n, :], func=ACT.Copy, scale=rec[i][:, n : n + 1]
                 )
-            store(i)
+                if unit_stores:
+                    store(i, n, n + 1)
+            if not unit_stores:
+                store(i)
 
-        def cap(u, q0=0, q1=QT):
-            bank = score_banks[TURNS[u][0]]
-            if u < PLACED:
-                dst, src = capped_rows[:, u], bank[:]
-            else:
-                dst, src = capped_words[:, u, q0:q1], bank[:, :, q0:q1].rearrange("p r q -> p q r")
-            nc.scalar.activation(out=dst, in_=src, func=ACT.Tanh, scale=1.0 / CAP)
+        def cap(u):
+            src = score_banks[TURNS[u][0]][:].rearrange("p r q -> p q r")
+            nc.scalar.activation(out=capped_words[:, u], in_=src, func=ACT.Tanh, scale=1.0 / CAP)
             if u + len(OTHER_HEADS) < len(TURNS):
                 scores(u + len(OTHER_HEADS))
-
-        def weigh_place(r):
-            nc.scalar.activation(
-                out=w_rows[:, :, r, :], in_=capped_rows[:, :, r, :], func=ACT.Exp, scale=CAP, bias=t_ln[:, r : r + 1]
-            )
-
-        def interleave():
-            nc.vector.tensor_copy(
-                out=w_bf[:, CHUNKS : CHUNKS + PLACED].rearrange("p n (c i) r -> p n c r i", i=WALK),
-                in_=w_rows[:].rearrange("p n r (c i) -> p n c r i", i=WALK),
-            )
 
         def quantize_and_values(first, end):
             for u in range(first, end):
@@ -345,22 +328,20 @@ def tile_rows_sink_cap_gqa_kernel(tc, qT, kT, t, v, sink, out):
         nc.scalar.activation(out=t_sign[:], in_=t_sb[:], func=ACT.Sign)
         quantize_q(3)
         round_q(2)
-        multiply(0)
         nc.vector.tensor_tensor(out=t_near1[:], in0=t_inv[:], in1=t_abs[:], op=ALU.mult)
+        multiply(0)
+        nc.vector.tensor_scalar(out=t_rest[:], in0=t_near1[:], scalar1=-1.0, scalar2=None, op0=ALU.add)
         quantize_q(2)
+        ln_step(0)
+        quantize_w(0)
+        ln_step(1)
         nc.vector.tensor_tensor(
             out=v_bf[:],
             in0=v_raw[:].rearrange("p j e -> p e j"),
             in1=t_sign[:].unsqueeze(1).to_broadcast([P, D, PACK]),
             op=ALU.mult,
         )
-        nc.vector.tensor_scalar(out=t_rest[:], in0=t_near1[:], scalar1=-1.0, scalar2=None, op0=ALU.add)
-        quantize_w(0)
-        ln_step(0)
-        nc.vector.quantize_mx(
-            out=v_codes[:].bitcast(FP8X4), scales=v_scales[:], in_=v_bf[:].rearrange("p e j -> p (e j)")
-        )
-        ln_step(1)
+        ln_step(2)
         head0_cap(2)
         head0_scores(4)
         head0_cap(3)
@@ -375,91 +356,99 @@ def tile_rows_sink_cap_gqa_kernel(tc, qT, kT, t, v, sink, out):
         cap(0)
         head0_exp(13, 16)
         multiply(1)
-        ln_step(2)
-        quantize_w(1)
         ln_step(3)
-        multiply(2)
-        ln_step(4)
+        nc.vector.quantize_mx(
+            out=v_codes[:].bitcast(FP8X4), scales=v_scales[:], in_=v_bf[:].rearrange("p e j -> p (e j)")
+        )
         round_q(0)
-        quantize_w(2)
-        for n in range(CHUNKS - 1):
-            values(n)
-        cap(1)
-        multiply(3)
+        ln_step(4)
+        quantize_w(1)
+        multiply(2)
+        add_ln(0)
         quantize_q(0)
-        round_q(1)
-        quantize_w(3)
-
-        head0, first, pair1, pair2, pair3, single1, single2, last = range(len(GROUPS))
+        values(0)
+        values(1)
+        cap(1)
+        add_ln(1)
+        head0, first, pair1, pair2, pair3, pair4, last = range(len(GROUPS))
         half_q = QT // 2
         cap(2)
-        values(CHUNKS - 1)
+        weigh(0, 1)
         add_ln(2)
-        quantize_q(1)
-        for r in range(PACK):
-            weigh_place(r)
-        interleave()
-        add_sink(head0)
+        multiply(3)
         cap(3)
+        quantize_w(2)
+        values(2)
+        quantize_and_values(0, 1)
+        quantize_w(3)
+        values(3)
         add_ln(3)
-        invert(head0)
         cap(4)
+        weigh(1, 3)
         add_ln(4)
+        add_sink(head0)
+        round_q(1)
+        invert(head0)
+        quantize_w(CHUNKS + 1)
+        quantize_w(CHUNKS + 2)
         cap(5)
-        weigh(2, 3)
-        quantize_and_values(0, 3)
-        divide(head0)
+        values(CHUNKS + 1)
+        values(CHUNKS + 2)
         add_ln(5)
+        quantize_q(1)
         cap(6)
         weigh(3, 5)
-        add_sink(first)
         add_ln(6)
+        add_sink(first)
+        divide(head0)
         invert(first)
-        quantize_and_values(3, 5)
+        quantize_w(CHUNKS + 3)
+        quantize_w(CHUNKS + 4)
         cap(7)
+        values(CHUNKS + 3)
+        values(CHUNKS + 4)
         cap(8)
         weigh(5, 7)
-        divide(first)
         add_ln(7)
-        add_sink(pair1)
         add_ln(8)
+        add_sink(pair1)
+        divide(first)
         invert(pair1)
-        quantize_and_values(5, 7)
+        quantize_w(CHUNKS + 5)
+        quantize_w(CHUNKS + 6)
         cap(9)
         cap(10)
         weigh(7, 9)
         add_ln(9)
-        weigh(9, 10)
         divide(pair1)
-        keep_warm(single1, 4)
-        add_sink(pair2)
-        add_ln(10, 0, half_q)
-        invert(pair2)
-        add_ln(10, half_q, QT)
+        keep_warm(pair4, 1)
+        values(CHUNKS + 5)
+        values(CHUNKS + 6)
+        keep_warm(pair4, 3)
+        add_ln(10)
         quantize_and_values(7, 9)
-        keep_warm(single1, 2)
-        divide(pair2)
-        quantize_and_values(9, 10)
-        keep_warm(last, 2)
-        for q0 in range(0, QT, QT // 4):
-            cap(11, q0, q0 + QT // 4)
-            add_ln(11, q0, q0 + QT // 4)
+        keep_warm(pair4, 4)
+        add_sink(pair2)
+        cap(11)
+        add_ln(11, 0, half_q)
+        invert(pair2)
+        add_ln(11, half_q, QT)
+        weigh(9, 10)
         weigh(10, 11)
         weigh(11, 12, 0, half_q)
         weigh(11, 12, half_q, QT)
+        quantize_and_values(9, 10)
+        divide(pair2)
         add_sink(pair3)
-        add_sink(single1)
         quantize_and_values(10, 11)
-        invert(pair3)
-        invert(single1)
-        divide_on_scalar(pair3)
         quantize_w(len(UNITS) - 1, 0, half_q)
+        invert(pair3)
+        divide_on_scalar(pair3)
         quantize_w(len(UNITS) - 1, half_q, QT)
         values(len(UNITS) - 1)
-        add_sink(single2)
-        divide(single1)
-        invert(single2)
-        divide_on_scalar(single2)
+        add_sink(pair4)
+        invert(pair4)
+        divide_on_scalar(pair4, unit_stores=True)
         add_sink(last)
         invert(last)
         divide(last)

@@ -211,6 +211,13 @@ def tile_rows_sink_cap_gqa_kernel(tc, qT, kT, t, v, sink, out):
                 in_=w_bf[:, n, q0:q1, :].rearrange("p q r -> p (q r)"),
             )
 
+        def quantize_pair(n):
+            nc.vector.quantize_mx(
+                out=w_codes[:, n : n + 2].rearrange("p n q -> p (n q)").bitcast(FP8X4),
+                scales=w_scales[:, n : n + 2].rearrange("p n q -> p (n q)"),
+                in_=w_bf[:, n : n + 2].rearrange("p n q r -> p (n q r)"),
+            )
+
         def values(n):
             i = group_of[UNITS[n]]
             dst = y_banks[i % Y_BANKS][:, sorted(GROUPS[i]).index(UNITS[n]), :]
@@ -360,16 +367,16 @@ def tile_rows_sink_cap_gqa_kernel(tc, qT, kT, t, v, sink, out):
         nc.vector.quantize_mx(
             out=v_codes[:].bitcast(FP8X4), scales=v_scales[:], in_=v_bf[:].rearrange("p e j -> p (e j)")
         )
-        round_q(0)
-        ln_step(4)
         quantize_w(1)
+        ln_step(4)
         multiply(2)
         add_ln(0)
-        quantize_q(0)
+        round_q(0)
         values(0)
         values(1)
         cap(1)
         add_ln(1)
+        quantize_q(0)
         head0, first, pair1, pair2, pair3, pair4, last = range(len(GROUPS))
         half_q = QT // 2
         cap(2)
@@ -379,18 +386,17 @@ def tile_rows_sink_cap_gqa_kernel(tc, qT, kT, t, v, sink, out):
         cap(3)
         quantize_w(2)
         values(2)
-        quantize_and_values(0, 1)
-        quantize_w(3)
-        values(3)
         add_ln(3)
+        quantize_pair(3)
+        values(3)
+        values(CHUNKS)
         cap(4)
         weigh(1, 3)
         add_ln(4)
-        add_sink(head0)
         round_q(1)
+        add_sink(head0)
+        quantize_pair(CHUNKS + 1)
         invert(head0)
-        quantize_w(CHUNKS + 1)
-        quantize_w(CHUNKS + 2)
         cap(5)
         values(CHUNKS + 1)
         values(CHUNKS + 2)
@@ -402,8 +408,7 @@ def tile_rows_sink_cap_gqa_kernel(tc, qT, kT, t, v, sink, out):
         add_sink(first)
         divide(head0)
         invert(first)
-        quantize_w(CHUNKS + 3)
-        quantize_w(CHUNKS + 4)
+        quantize_pair(CHUNKS + 3)
         cap(7)
         values(CHUNKS + 3)
         values(CHUNKS + 4)
@@ -414,24 +419,24 @@ def tile_rows_sink_cap_gqa_kernel(tc, qT, kT, t, v, sink, out):
         add_sink(pair1)
         divide(first)
         invert(pair1)
-        quantize_w(CHUNKS + 5)
-        quantize_w(CHUNKS + 6)
+        quantize_pair(CHUNKS + 5)
+        values(CHUNKS + 5)
+        values(CHUNKS + 6)
         cap(9)
         cap(10)
         weigh(7, 9)
         add_ln(9)
         divide(pair1)
-        keep_warm(pair4, 1)
-        values(CHUNKS + 5)
-        values(CHUNKS + 6)
-        keep_warm(pair4, 3)
-        add_ln(10)
-        quantize_and_values(7, 9)
         keep_warm(pair4, 4)
+        add_ln(10)
         add_sink(pair2)
+        quantize_pair(CHUNKS + 7)
+        values(CHUNKS + 7)
+        values(CHUNKS + 8)
+        keep_warm(pair4, 4)
+        invert(pair2)
         cap(11)
         add_ln(11, 0, half_q)
-        invert(pair2)
         add_ln(11, half_q, QT)
         weigh(9, 10)
         weigh(10, 11)

@@ -420,20 +420,22 @@ def tile_rows_sink_cap_gqa_kernel(tc, qT, kT, t, v, sink, out):
         divide(first)
         invert(pair1)
         quantize_pair(CHUNKS + 5)
-        values(CHUNKS + 5)
-        values(CHUNKS + 6)
         cap(9)
         cap(10)
         weigh(7, 9)
-        add_ln(9)
         divide(pair1)
-        keep_warm(pair4, 4)
+        keep_warm(pair4, 1)
+        values(CHUNKS + 5)
+        values(CHUNKS + 6)
+        keep_warm(pair4, 2)
+        add_ln(9)
         add_ln(10)
         add_sink(pair2)
+        keep_warm(pair2, 2)
         quantize_pair(CHUNKS + 7)
         values(CHUNKS + 7)
         values(CHUNKS + 8)
-        keep_warm(pair4, 4)
+        keep_warm(pair4, 3)
         invert(pair2)
         cap(11)
         add_ln(11, 0, half_q)

@@ -27,6 +27,8 @@ WALK = 4
 BITS_TO_LN = math.log(2.0) / 2.0**23
 BITS_OFFSET = -127.0 * math.log(2.0) + 0.0298
 LN_DEGREE = 5
+LN_SCALE = 60
+LN_SERIES = [(-1) ** (k + 1) * (LN_SCALE // k) for k in range(LN_DEGREE, 0, -1)] + [0]
 
 OTHER_HEADS = (2, 3, 1)
 TURNS = [(h, c) for c in (3, 2, 0, 1) for h in OTHER_HEADS]
@@ -56,8 +58,9 @@ def tile_rows_sink_cap_gqa_kernel(tc, qT, kT, t, v, sink, out):
         t_guess = sb.tile([P, PACK], F32)
         t_inv = sb.tile([P, PACK], F32)
         t_near1 = sb.tile([P, PACK], F32)
-        t_rest = sb.tile([P, PACK], F32)
-        t_horner = [sb.tile([P, PACK], F32, name="t_horner%d" % i) for i in range(LN_DEGREE - 1)]
+        t_rest = sb.tile([P, PACK, len(LN_SERIES)], F32)
+        series = sb.tile([P, PACK, len(LN_SERIES)], F32)
+        t_horner = sb.tile([P, PACK, len(LN_SERIES)], F32)
         sink_sb = sb.tile([P, H * CHUNKS], F32)
 
         q_slots = range(CHUNKS + EARLY)
@@ -172,21 +175,28 @@ def tile_rows_sink_cap_gqa_kernel(tc, qT, kT, t, v, sink, out):
                 op=ALU.mult,
             )
 
-        def ln_step(k):
-            lead = (-1.0) ** (LN_DEGREE + 1) / LN_DEGREE
-            if k == LN_DEGREE - 1:
-                nc.vector.scalar_tensor_tensor(
-                    out=t_ln[:], in0=t_horner[k - 1][:], scalar=lead, in1=t_guess[:], op0=ALU.mult, op1=ALU.add
-                )
-                return
-            power = LN_DEGREE - 1 - k
+        def rest_of_t():
+            src = t_near1[:].unsqueeze(2).to_broadcast([P, PACK, LN_DEGREE])
+            nc.vector.tensor_scalar(out=t_rest[:, :, 1:], in0=src, scalar1=-1.0, scalar2=None, op0=ALU.add)
+
+        def horner():
+            nc.vector.tensor_tensor_scan(
+                out=t_horner[:].rearrange("p r k -> p (r k)"),
+                data0=t_rest[:].rearrange("p r k -> p (r k)"),
+                data1=series[:].rearrange("p r k -> p (r k)"),
+                initial=0.0,
+                op0=ALU.mult,
+                op1=ALU.add,
+            )
+
+        def finish_ln():
             nc.vector.scalar_tensor_tensor(
-                out=t_horner[k][:],
-                in0=t_horner[k - 1][:] if k else t_rest[:],
-                scalar=(-1.0) ** (power + 1) / power / lead,
-                in1=t_rest[:],
-                op0=ALU.add,
-                op1=ALU.mult,
+                out=t_ln[:],
+                in0=t_horner[:, :, LN_DEGREE],
+                scalar=1.0 / LN_SCALE,
+                in1=t_guess[:],
+                op0=ALU.mult,
+                op1=ALU.add,
             )
 
         def add_ln(u, q0=0, q1=QT):
@@ -222,11 +232,6 @@ def tile_rows_sink_cap_gqa_kernel(tc, qT, kT, t, v, sink, out):
             i = group_of[UNITS[n]]
             dst = y_banks[i % Y_BANKS][:, sorted(GROUPS[i]).index(UNITS[n]), :]
             whole_pass(dst, w_codes[:, n, :], w_scales[:, n, :], v_codes[:], v_scales[:])
-
-        def keep_warm(bank_of, passes):
-            dst = y_banks[bank_of % Y_BANKS][:, PACK - 1, :]
-            for rep in range(passes):
-                whole_pass(dst, w_codes[:, 0, :], w_scales[:, 0, :], v_codes[:], v_scales[:])
 
         def units_in_out(i):
             first, final = [CHUNKS * h + c for h, c in (min(GROUPS[i]), max(GROUPS[i]))]
@@ -296,6 +301,9 @@ def tile_rows_sink_cap_gqa_kernel(tc, qT, kT, t, v, sink, out):
         nc.sync.dma_start(out=v_raw[:], in_=v[0].rearrange("(p j) e -> p j e", j=PACK))
 
         nc.vector.memset(k_mx[tile0, N:], 0)
+        nc.vector.memset(t_rest[:, :, 0], 0.0)
+        for power, coefficient in enumerate(LN_SERIES):
+            nc.vector.memset(series[:, :, power], float(coefficient))
 
         round_k(1, 0, nc.scalar.copy)
         round_k(1, 1, nc.scalar.copy)
@@ -334,21 +342,20 @@ def tile_rows_sink_cap_gqa_kernel(tc, qT, kT, t, v, sink, out):
         nc.scalar.activation(out=t_inv[:], in_=t_guess[:], func=ACT.Exp, scale=-1.0)
         nc.scalar.activation(out=t_sign[:], in_=t_sb[:], func=ACT.Sign)
         quantize_q(3)
-        round_q(2)
         nc.vector.tensor_tensor(out=t_near1[:], in0=t_inv[:], in1=t_abs[:], op=ALU.mult)
         multiply(0)
-        nc.vector.tensor_scalar(out=t_rest[:], in0=t_near1[:], scalar1=-1.0, scalar2=None, op0=ALU.add)
-        quantize_q(2)
-        ln_step(0)
+        rest_of_t()
+        round_q(2)
         quantize_w(0)
-        ln_step(1)
+        horner()
+        quantize_q(2)
         nc.vector.tensor_tensor(
             out=v_bf[:],
             in0=v_raw[:].rearrange("p j e -> p e j"),
             in1=t_sign[:].unsqueeze(1).to_broadcast([P, D, PACK]),
             op=ALU.mult,
         )
-        ln_step(2)
+        finish_ln()
         head0_cap(2)
         head0_scores(4)
         head0_cap(3)
@@ -363,32 +370,30 @@ def tile_rows_sink_cap_gqa_kernel(tc, qT, kT, t, v, sink, out):
         cap(0)
         head0_exp(13, 16)
         multiply(1)
-        ln_step(3)
         nc.vector.quantize_mx(
             out=v_codes[:].bitcast(FP8X4), scales=v_scales[:], in_=v_bf[:].rearrange("p e j -> p (e j)")
         )
         quantize_w(1)
-        ln_step(4)
         multiply(2)
         add_ln(0)
-        round_q(0)
+        multiply(3)
         values(0)
         values(1)
         cap(1)
         add_ln(1)
-        quantize_q(0)
         head0, first, pair1, pair2, pair3, pair4, last = range(len(GROUPS))
         half_q = QT // 2
         cap(2)
         weigh(0, 1)
         add_ln(2)
-        multiply(3)
+        round_q(0)
+        quantize_pair(2)
+        quantize_q(0)
         cap(3)
-        quantize_w(2)
         values(2)
-        add_ln(3)
-        quantize_pair(3)
         values(3)
+        add_ln(3)
+        quantize_w(CHUNKS)
         values(CHUNKS)
         cap(4)
         weigh(1, 3)
@@ -424,18 +429,14 @@ def tile_rows_sink_cap_gqa_kernel(tc, qT, kT, t, v, sink, out):
         cap(10)
         weigh(7, 9)
         divide(pair1)
-        keep_warm(pair4, 1)
         values(CHUNKS + 5)
         values(CHUNKS + 6)
-        keep_warm(pair4, 2)
         add_ln(9)
         add_ln(10)
         add_sink(pair2)
-        keep_warm(pair2, 2)
         quantize_pair(CHUNKS + 7)
         values(CHUNKS + 7)
         values(CHUNKS + 8)
-        keep_warm(pair4, 3)
         invert(pair2)
         cap(11)
         add_ln(11, 0, half_q)

@@ -33,7 +33,7 @@ LN_SERIES = [(-1) ** (k + 1) * (LN_SCALE // k) for k in range(LN_DEGREE, 0, -1)]
 OTHER_HEADS = (2, 3, 1)
 TURNS = [(h, c) for c in (3, 2, 0, 1) for h in OTHER_HEADS]
 UNITS = [(0, c) for c in range(CHUNKS)] + TURNS
-GROUPS = [UNITS[0:4], TURNS[0:3], TURNS[3:5], TURNS[5:7], TURNS[7:9], TURNS[9:11], TURNS[11:12]]
+GROUPS = [UNITS[0:4], TURNS[0:3], TURNS[3:5], TURNS[5:7], TURNS[7:9], TURNS[9:10], TURNS[10:11], TURNS[11:12]]
 Y_BANKS = 3
 HEAD0_FILLS = ((0, 2), (2, 4), (4, 7), (7, 10), (10, 13), (13, 16))
 
@@ -381,7 +381,7 @@ def tile_rows_sink_cap_gqa_kernel(tc, qT, kT, t, v, sink, out):
         values(1)
         cap(1)
         add_ln(1)
-        head0, first, pair1, pair2, pair3, pair4, last = range(len(GROUPS))
+        head0, first, pair1, pair2, pair3, single1, single2, last = range(len(GROUPS))
         half_q = QT // 2
         cap(2)
         weigh(0, 1)
@@ -432,12 +432,13 @@ def tile_rows_sink_cap_gqa_kernel(tc, qT, kT, t, v, sink, out):
         values(CHUNKS + 5)
         values(CHUNKS + 6)
         add_ln(9)
-        add_ln(10)
         add_sink(pair2)
+        add_ln(10)
+        invert(pair2)
         quantize_pair(CHUNKS + 7)
         values(CHUNKS + 7)
         values(CHUNKS + 8)
-        invert(pair2)
+        divide(pair2)
         cap(11)
         add_ln(11, 0, half_q)
         add_ln(11, half_q, QT)
@@ -445,18 +446,20 @@ def tile_rows_sink_cap_gqa_kernel(tc, qT, kT, t, v, sink, out):
         weigh(10, 11)
         weigh(11, 12, 0, half_q)
         weigh(11, 12, half_q, QT)
-        quantize_and_values(9, 10)
-        divide(pair2)
         add_sink(pair3)
-        quantize_and_values(10, 11)
-        quantize_w(len(UNITS) - 1, 0, half_q)
+        quantize_and_values(9, 10)
         invert(pair3)
-        divide_on_scalar(pair3)
+        quantize_and_values(10, 11)
+        divide(pair3)
+        quantize_w(len(UNITS) - 1, 0, half_q)
         quantize_w(len(UNITS) - 1, half_q, QT)
         values(len(UNITS) - 1)
-        add_sink(pair4)
-        invert(pair4)
-        divide_on_scalar(pair4, unit_stores=True)
+        add_sink(single1)
+        add_sink(single2)
+        invert(single1)
+        divide_on_scalar(single1)
+        invert(single2)
+        divide_on_scalar(single2)
         add_sink(last)
         invert(last)
         divide(last)

@@ -243,6 +243,14 @@ def tile_rows_sink_cap_gqa_kernel(tc, qT, kT, t, v, sink, out):
                 out=den[i][:], in0=y[:, 0 : len(GROUPS[i]), D - 1], in1=sink_sb[:, units_in_out(i)], op=ALU.add
             )
 
+        def add_sink_on_scalar(i):
+            nc.scalar.activation(
+                out=den[i][:],
+                in_=y_banks[i % Y_BANKS][:, 0, D - 1 : D],
+                func=ACT.Identity,
+                bias=sink_sb[:, units_in_out(i)],
+            )
+
         def invert(i):
             nc.vector.reciprocal(out=rec[i][:], in_=den[i][:])
 
@@ -435,9 +443,7 @@ def tile_rows_sink_cap_gqa_kernel(tc, qT, kT, t, v, sink, out):
         add_sink(pair2)
         add_ln(10)
         invert(pair2)
-        quantize_pair(CHUNKS + 7)
-        values(CHUNKS + 7)
-        values(CHUNKS + 8)
+        quantize_and_values(7, 9)
         divide(pair2)
         cap(11)
         add_ln(11, 0, half_q)
@@ -454,12 +460,12 @@ def tile_rows_sink_cap_gqa_kernel(tc, qT, kT, t, v, sink, out):
         quantize_w(len(UNITS) - 1, 0, half_q)
         quantize_w(len(UNITS) - 1, half_q, QT)
         values(len(UNITS) - 1)
-        add_sink(single1)
-        add_sink(single2)
+        add_sink_on_scalar(single1)
         invert(single1)
+        add_sink(single2)
         divide_on_scalar(single1)
         invert(single2)
-        divide_on_scalar(single2)
         add_sink(last)
+        divide(single2)
         invert(last)
         divide(last)

import math
from contextlib import ExitStack

import concourse.mybir as mybir

H, D, NQ, N = 4, 128, 512, 512
CAP = 2.0
FLOPS = 2 * 2 * H * NQ * N * D

F32 = mybir.dt.float32
BF16 = mybir.dt.bfloat16
I32 = mybir.dt.int32
U8 = mybir.dt.uint8
FP8X4 = mybir.dt.float8_e4m3fn_x4
ACT = mybir.ActivationFunctionType
ALU = mybir.AluOpType

P = 128
PACK = 4
ROWS = D // PACK
QT = 128
CHUNKS = NQ // QT
EARLY = 3
K_PIECES = ((0, 384), (384, 512))
WALK = 4

BITS_TO_LN = math.log(2.0) / 2.0**23
BITS_OFFSET = -127.0 * math.log(2.0) + 0.0298
LN_DEGREE = 5
LN_SCALE = 60
LN_SERIES = [(-1) ** (k + 1) * (LN_SCALE // k) for k in range(LN_DEGREE, 0, -1)] + [0]

OTHER_HEADS = (2, 3, 1)
TURNS = [(h, c) for c in (3, 2, 0, 1) for h in OTHER_HEADS]
UNITS = [(0, c) for c in range(CHUNKS)] + TURNS
GROUPS = [UNITS[0:4], TURNS[0:3], TURNS[3:5], TURNS[5:7], TURNS[7:9], TURNS[9:10], TURNS[10:11], TURNS[11:12]]
Y_BANKS = 3
HEAD0_FILLS = ((0, 2), (2, 4), (4, 7), (7, 10), (10, 13), (13, 16))


def tile_rows_sink_cap_gqa_kernel(tc, qT, kT, t, v, sink, out):
    nc = tc.nc
    with ExitStack() as ctx:
        sb = ctx.enter_context(tc.tile_pool(name="sb", bufs=1))
        ps = ctx.enter_context(tc.psum_pool(name="ps", bufs=1))
        ctx.enter_context(tc.manual_schedule())

        q_src = qT.rearrange("h (p j) q -> (h p) j q", j=PACK)
        k_src = kT[0].rearrange("(p j) i -> p j i", j=PACK)
        q_raw = sb.tile([P, PACK, EARLY * QT], F32)
        q_last = sb.tile([P, PACK, QT], F32)
        k_raw = [sb.tile([ROWS, PACK, b - a], F32, name="k_raw%d" % a) for a, b in K_PIECES]
        v_raw = sb.tile([P, PACK, D], F32)
        t_sb = sb.tile([P, PACK], F32)
        t_abs = sb.tile([P, PACK], F32)
        t_ln = sb.tile([P, PACK], F32)
        t_sign = sb.tile([P, PACK], F32)
        t_guess = sb.tile([P, PACK], F32)
        t_inv = sb.tile([P, PACK], F32)
        t_near1 = sb.tile([P, PACK], F32)
        t_rest = sb.tile([P, PACK, len(LN_SERIES)], F32)
        series = sb.tile([P, PACK, len(LN_SERIES)], F32)
        t_horner = sb.tile([P, PACK, len(LN_SERIES)], F32)
        sink_sb = sb.tile([P, H * CHUNKS], F32)

        q_slots = range(CHUNKS + EARLY)
        q_bf = [sb.tile([P, QT, PACK], BF16, align_bytes=64, name="q_bf%d" % c) for c in q_slots]
        q_codes = [sb.tile([P, QT], I32, align_bytes=64, name="q_codes%d" % c) for c in q_slots]
        q_scales = [sb.tile([P, QT], U8, align_bytes=64, name="q_scales%d" % c) for c in q_slots]
        k_bf = [sb.tile([ROWS, 2, P, PACK], BF16, align_bytes=64, name="k_bf%d" % i) for i in range(2)]
        k_mx = sb.tile([P, N + N // PACK], I32, align_bytes=64)
        k_codes = k_mx[:, 0:N]
        k_scales = k_mx[:, N:].bitcast(U8)
        v_bf = sb.tile([P, D, PACK], BF16, align_bytes=64)
        v_codes = sb.tile([P, D], I32, align_bytes=64)
        v_scales = sb.tile([P, D], U8, align_bytes=64)

        def per_group(name, shape):
            return [sb.tile([P, len(g)] + shape, F32, name="%s%d" % (name, i)) for i, g in enumerate(GROUPS)]

        head0_rows = sb.tile([P, CHUNKS * PACK, QT], F32)
        p_rows = sb.tile([P, CHUNKS * PACK, QT], F32)
        capped_words = sb.tile([P, len(TURNS), QT, PACK], F32)
        logits = sb.tile([P, len(TURNS), QT, PACK], F32)
        w_bf = sb.tile([P, len(UNITS), QT, PACK], BF16, align_bytes=64)
        w_codes = sb.tile([P, len(UNITS), QT], I32, align_bytes=64)
        w_scales = sb.tile([P, len(UNITS), QT], U8, align_bytes=64)
        den = per_group("den", [])
        rec = per_group("rec", [])
        res = per_group("res", [D])
        score_banks = [ps.tile([P, PACK, QT], F32, name="score%d" % g) for g in range(H + 1)]
        y_banks = [ps.tile([P, PACK, D], F32, name="y%d" % i) for i in range(Y_BANKS)]

        tile0 = slice(0, ROWS)
        group_of = {unit: i for i, g in enumerate(GROUPS) for unit in g}

        def round_k(pair, half, copy=nc.vector.tensor_copy):
            src = k_raw[half][:].rearrange("p j (s r) -> p s j r", r=PACK)[:, :, :, 2 * pair : 2 * pair + 2]
            dst = k_bf[pair][:, :, K_PIECES[half][0] // PACK : K_PIECES[half][1] // PACK, :]
            copy(out=dst.rearrange("p r s j -> p s j r"), in_=src)

        def quantize_k(r):
            cols = slice(r * P, (r + 1) * P)
            nc.vector.quantize_mx(
                out=k_codes[tile0, cols].bitcast(FP8X4),
                scales=k_scales[tile0, cols],
                in_=k_bf[r // 2][tile0, r % 2].rearrange("p s j -> p (s j)"),
            )

        def round_q(c, early=False, copy=nc.vector.tensor_copy, q0=0, q1=QT):
            rows = tile0 if early else slice(0, P)
            src = q_raw[rows, :, c * QT + q0 : c * QT + q1] if c < EARLY else q_last[rows]
            copy(
                out=q_bf[c + CHUNKS * early][rows, q0:q1].rearrange("p (c i) j -> p c j i", i=WALK),
                in_=src.rearrange("p j (c i) -> p c j i", i=WALK),
            )

        def quantize_q(c, early=False):
            rows = tile0 if early else slice(0, P)
            slot = c + CHUNKS * early
            nc.vector.quantize_mx(
                out=q_codes[slot][rows].bitcast(FP8X4),
                scales=q_scales[slot][rows],
                in_=q_bf[slot][rows].rearrange("p q j -> p (q j)"),
            )

        def score_pass(dst, h, c, r):
            rows = slice(ROWS * h, ROWS * (h + 1))
            cols = slice(r * P, (r + 1) * P)
            slot = c + CHUNKS * (h == 0 and c < EARLY)
            nc.tensor.matmul_mx(
                out=dst,
                lhsT=k_codes[rows, cols].bitcast(FP8X4),
                lhsT_scale=k_scales[rows, cols],
                rhs=q_codes[slot][rows, :].bitcast(FP8X4),
                rhs_scale=q_scales[slot][rows, :],
                start=True,
                stop=True,
            )

        def whole_pass(dst, lhs_codes, lhs_scales, rhs_codes, rhs_scales):
            nc.tensor.matmul_mx(
                out=dst,
                lhsT=lhs_codes.bitcast(FP8X4),
                lhsT_scale=lhs_scales,
                rhs=rhs_codes.bitcast(FP8X4),
                rhs_scale=rhs_scales,
                start=True,
                stop=True,
            )

        def scores(u):
            h, c = TURNS[u]
            for r in range(PACK):
                score_pass(score_banks[h][:, r, :], h, c, r)

        def head0_scores(fill):
            first, end = HEAD0_FILLS[fill]
            for row in range(first, end):
                score_pass(score_banks[H * (fill % 2)][:, row - first, :], 0, row // PACK, row % PACK)

        def head0_cap(fill):
            first, end = HEAD0_FILLS[fill]
            src = score_banks[H * (fill % 2)][:, 0 : end - first, :]
            nc.scalar.activation(out=head0_rows[:, first:end, :], in_=src, func=ACT.Tanh, scale=1.0 / CAP)

        def head0_exp(first, end):
            nc.scalar.activation(out=p_rows[:, first:end, :], in_=head0_rows[:, first:end, :], func=ACT.Exp, scale=CAP)

        def multiply(c):
            nc.vector.tensor_tensor(
                out=w_bf[:, c].rearrange("p (c i) r -> p c r i", i=WALK),
                in0=p_rows[:, PACK * c : PACK * (c + 1), :].rearrange("p r (c i) -> p c r i", i=WALK),
                in1=t_abs[:].unsqueeze(1).unsqueeze(3).to_broadcast([P, QT // WALK, PACK, WALK]),
                op=ALU.mult,
            )

        def rest_of_t():
            src = t_near1[:].unsqueeze(2).to_broadcast([P, PACK, LN_DEGREE])
            nc.vector.tensor_scalar(out=t_rest[:, :, 1:], in0=src, scalar1=-1.0, scalar2=None, op0=ALU.add)

        def horner():
            nc.vector.tensor_tensor_scan(
                out=t_horner[:].rearrange("p r k -> p (r k)"),
                data0=t_rest[:].rearrange("p r k -> p (r k)"),
                data1=series[:].rearrange("p r k -> p (r k)"),
                initial=0.0,
                op0=ALU.mult,
                op1=ALU.add,
            )

        def finish_ln():
            nc.vector.scalar_tensor_tensor(
                out=t_ln[:],
                in0=t_horner[:, :, LN_DEGREE],
                scalar=1.0 / LN_SCALE,
                in1=t_guess[:],
                op0=ALU.mult,
                op1=ALU.add,
            )

        def add_ln(u, q0=0, q1=QT):
            nc.vector.scalar_tensor_tensor(
                out=logits[:, u, q0:q1],
                in0=capped_words[:, u, q0:q1],
                scalar=CAP,
                in1=t_ln[:].unsqueeze(1).to_broadcast([P, q1 - q0, PACK]),
                op0=ALU.mult,
                op1=ALU.add,
            )

        def weigh(first, end, q0=0, q1=QT):
            nc.scalar.activation(
                out=w_bf[:, CHUNKS + first : CHUNKS + end, q0:q1], in_=logits[:, first:end, q0:q1], func=ACT.Exp
            )

        def quantize_w(n, q0=0, q1=QT):
            nc.vector.quantize_mx(
                out=w_codes[:, n, q0:q1].bitcast(FP8X4),
                scales=w_scales[:, n, q0:q1],
                in_=w_bf[:, n, q0:q1, :].rearrange("p q r -> p (q r)"),
            )

        def quantize_pair(n):
            nc.vector.quantize_mx(
                out=w_codes[:, n : n + 2].rearrange("p n q -> p (n q)").bitcast(FP8X4),
                scales=w_scales[:, n : n + 2].rearrange("p n q -> p (n q)"),
                in_=w_bf[:, n : n + 2].rearrange("p n q r -> p (n q r)"),
            )

        def values(n):
            i = group_of[UNITS[n]]
            dst = y_banks[i % Y_BANKS][:, sorted(GROUPS[i]).index(UNITS[n]), :]
            whole_pass(dst, w_codes[:, n, :], w_scales[:, n, :], v_codes[:], v_scales[:])

        def units_in_out(i):
            first, final = [CHUNKS * h + c for h, c in (min(GROUPS[i]), max(GROUPS[i]))]
            return slice(first, final + 1, max((final - first) // max(len(GROUPS[i]) - 1, 1), 1))

        def add_sink(i):
            y = y_banks[i % Y_BANKS]
            nc.vector.tensor_tensor(
                out=den[i][:], in0=y[:, 0 : len(GROUPS[i]), D - 1], in1=sink_sb[:, units_in_out(i)], op=ALU.add
            )

        def add_sink_on_scalar(i):
            nc.scalar.activation(
                out=den[i][:],
                in_=y_banks[i % Y_BANKS][:, 0, D - 1 : D],
                func=ACT.Identity,
                bias=sink_sb[:, units_in_out(i)],
            )

        def invert(i):
            nc.vector.reciprocal(out=rec[i][:], in_=den[i][:])

        def store(i, first=0, end=None):
            dst = out.rearrange("h (c p) e -> p (h c) e", p=QT)[:, units_in_out(i), :]
            nc.sync.dma_start(out=dst[:, first:end], in_=res[i][:, first:end])

        def divide(i):
            n = len(GROUPS[i])
            nc.vector.tensor_tensor(
                out=res[i][:],
                in0=y_banks[i % Y_BANKS][:, 0 : n, :],
                in1=rec[i][:].unsqueeze(2).to_broadcast([P, n, D]),
                op=ALU.mult,
            )
            store(i)

        def divide_on_scalar(i, unit_stores=False):
            for n in range(len(GROUPS[i])):
                nc.scalar.activation(
                    out=res[i][:, n, :], in_=y_banks[i % Y_BANKS][:, n, :], func=ACT.Copy, scale=rec[i][:, n : n + 1]
                )
                if unit_stores:
                    store(i, n, n + 1)
            if not unit_stores:
                store(i)

        def cap(u):
            src = score_banks[TURNS[u][0]][:].rearrange("p r q -> p q r")
            nc.scalar.activation(out=capped_words[:, u], in_=src, func=ACT.Tanh, scale=1.0 / CAP)
            if u + len(OTHER_HEADS) < len(TURNS):
                scores(u + len(OTHER_HEADS))

        def quantize_and_values(first, end):
            for u in range(first, end):
                quantize_w(CHUNKS + u)
                values(CHUNKS + u)

        def load_k(piece):
            a, b = K_PIECES[piece]
            nc.sync.dma_start(out=k_raw[piece][:], in_=k_src[:, :, a:b])

        def load_q(rows, first, end):
            nc.sync.dma_start(out=q_raw[rows, :, first * QT : end * QT], in_=q_src[rows, :, first * QT : end * QT])

        load_k(0)
        load_q(tile0, 0, 1)
        load_k(1)
        load_q(tile0, 1, 2)
        load_q(tile0, 2, 3)
        nc.sync.dma_start(out=t_sb[:], in_=t.rearrange("(p j) o -> p (j o)", j=PACK))
        nc.sync.dma_start(out=q_last[:], in_=q_src[:, :, EARLY * QT :])
        other_rows = (slice(ROWS, 3 * ROWS), slice(3 * ROWS, P))
        for rows in other_rows:
            load_q(rows, 2, 3)
        nc.sync.dma_start(out=v_raw[:], in_=v[0].rearrange("(p j) e -> p j e", j=PACK))

        nc.vector.memset(k_mx[tile0, N:], 0)
        nc.vector.memset(t_rest[:, :, 0], 0.0)
        for power, coefficient in enumerate(LN_SERIES):
            nc.vector.memset(series[:, :, power], float(coefficient))

        round_k(1, 0, nc.scalar.copy)
        round_k(1, 1, nc.scalar.copy)
        round_q(1, early=True, copy=nc.scalar.copy)
        round_k(0, 0)
        round_q(0, early=True)
        round_k(0, 1)
        quantize_q(0, early=True)
        for r in range(PACK):
            quantize_k(r)
        round_q(2, early=True)
        quantize_q(1, early=True)
        nc.vector.scalar_tensor_tensor(
            out=t_abs[:], in0=t_sb[:], scalar=-1.0, in1=t_sb[:], op0=ALU.mult, op1=ALU.max
        )
        quantize_q(2, early=True)
        nc.vector.tensor_scalar(
            out=t_guess[:], in0=t_abs[:].bitcast(I32), scalar1=BITS_TO_LN, scalar2=BITS_OFFSET, op0=ALU.mult, op1=ALU.add
        )
        for g in OTHER_HEADS:
            nc.sync.dma_start(out=k_mx[g * ROWS : (g + 1) * ROWS, :], in_=k_mx[tile0, :])
        for rows in other_rows:
            load_q(rows, 0, 2)
        with nc.allow_non_contiguous_dma(reason="one sink a query row"):
            nc.sync.dma_start(out=sink_sb[:], in_=sink.rearrange("h (c p) o -> p (h c o)", p=QT))
        round_q(3)

        head0_scores(0)
        head0_scores(1)
        head0_cap(0)
        head0_scores(2)
        head0_cap(1)
        head0_scores(3)
        head0_exp(0, 2)
        head0_exp(2, 4)
        nc.scalar.activation(out=t_inv[:], in_=t_guess[:], func=ACT.Exp, scale=-1.0)
        nc.scalar.activation(out=t_sign[:], in_=t_sb[:], func=ACT.Sign)
        quantize_q(3)
        nc.vector.tensor_tensor(out=t_near1[:], in0=t_inv[:], in1=t_abs[:], op=ALU.mult)
        multiply(0)
        rest_of_t()
        round_q(2)
        quantize_w(0)
        horner()
        quantize_q(2)
        nc.vector.tensor_tensor(
            out=v_bf[:],
            in0=v_raw[:].rearrange("p j e -> p e j"),
            in1=t_sign[:].unsqueeze(1).to_broadcast([P, D, PACK]),
            op=ALU.mult,
        )
        finish_ln()
        head0_cap(2)
        head0_scores(4)
        head0_cap(3)
        head0_scores(5)
        head0_exp(4, 7)
        head0_exp(7, 10)
        head0_cap(4)
        head0_cap(5)
        head0_exp(10, 13)
        for u in range(len(OTHER_HEADS)):
            scores(u)
        cap(0)
        head0_exp(13, 16)
        multiply(1)
        nc.vector.quantize_mx(
            out=v_codes[:].bitcast(FP8X4), scales=v_scales[:], in_=v_bf[:].rearrange("p e j -> p (e j)")
        )
        quantize_w(1)
        multiply(2)
        add_ln(0)
        multiply(3)
        values(0)
        values(1)
        cap(1)
        add_ln(1)
        head0, first, pair1, pair2, pair3, single1, single2, last = range(len(GROUPS))
        half_q = QT // 2
        cap(2)
        weigh(0, 1)
        add_ln(2)
        round_q(0)
        quantize_pair(2)
        quantize_q(0)
        cap(3)
        values(2)
        values(3)
        add_ln(3)
        quantize_w(CHUNKS)
        values(CHUNKS)
        cap(4)
        weigh(1, 3)
        add_ln(4)
        round_q(1)
        add_sink(head0)
        quantize_pair(CHUNKS + 1)
        invert(head0)
        cap(5)
        values(CHUNKS + 1)
        values(CHUNKS + 2)
        add_ln(5)
        quantize_q(1)
        cap(6)
        weigh(3, 5)
        add_ln(6)
        add_sink(first)
        divide(head0)
        invert(first)
        quantize_pair(CHUNKS + 3)
        cap(7)
        values(CHUNKS + 3)
        values(CHUNKS + 4)
        cap(8)
        weigh(5, 7)
        add_ln(7)
        add_ln(8)
        add_sink(pair1)
        divide(first)
        invert(pair1)
        quantize_pair(CHUNKS + 5)
        cap(9)
        cap(10)
        weigh(7, 9)
        divide(pair1)
        values(CHUNKS + 5)
        values(CHUNKS + 6)
        add_ln(9)
        add_sink(pair2)
        add_ln(10)
        invert(pair2)
        quantize_and_values(7, 9)
        divide(pair2)
        cap(11)
        add_ln(11, 0, half_q)
        add_ln(11, half_q, QT)
        weigh(9, 10)
        weigh(10, 11)
        weigh(11, 12, 0, half_q)
        weigh(11, 12, half_q, QT)
        add_sink(pair3)
        quantize_and_values(9, 10)
        invert(pair3)
        quantize_and_values(10, 11)
        divide(pair3)
        quantize_w(len(UNITS) - 1, 0, half_q)
        quantize_w(len(UNITS) - 1, half_q, QT)
        values(len(UNITS) - 1)
        add_sink_on_scalar(single1)
        invert(single1)
        add_sink(single2)
        divide_on_scalar(single1)
        invert(single2)
        add_sink(last)
        divide(single2)
        invert(last)
        divide(last)
